import numpy as np
import ml_dtypes


def mxq(x, axis, fmt="e4m3"):
    dtype, down = {"e4m3": (ml_dtypes.float8_e4m3fn, 7), "e5m2": (ml_dtypes.float8_e5m2, 14)}[fmt]
    v = np.moveaxis(np.asarray(x, np.float32).astype(ml_dtypes.bfloat16).astype(np.float64), axis, -1)
    blocks = v.reshape(v.shape[:-1] + (-1, 32))
    amax = np.abs(blocks).max(-1, keepdims=True)
    byte = np.maximum(np.where(amax > 0, np.frexp(amax)[1] - 1 + 127, 0) - down, 1)
    scale = np.exp2(byte - 127.0)
    codes = (blocks / scale).astype(np.float32).astype(dtype).astype(np.float64)
    return np.moveaxis((codes * scale).reshape(v.shape), -1, axis)


WIDE = False


def mx_kscale(k):
    if not WIDE:
        return np.ones(k)
    levels = np.array([10, -10, 5, -5, 0])
    if k % 512:
        return np.exp2(np.random.permutation(np.resize(levels, k // 32))).repeat(32)
    a = np.empty((k // 512, 16))
    for p in range(k // 512):
        a[p, :8] = np.random.permutation(np.resize(levels, 8))
        for g in range(8):
            far = levels[np.abs(levels - a[p, g]) >= 10]
            a[p, g + 8] = far[np.random.randint(len(far))]
    return np.exp2(a.ravel()).repeat(32)


BF16 = ml_dtypes.bfloat16


def bf(x):
    return np.asarray(x, np.float32).astype(BF16)


def f64(x):
    return np.asarray(x).astype(np.float64)


E2M1 = np.array([0.0, 0.5, 1.0, 1.5, 2.0, 3.0, 4.0, 6.0, -0.0, -0.5, -1.0, -1.5, -2.0, -3.0, -4.0, -6.0])


def pack_weight(w, fmt):
    k, n = w.shape
    w = f64(bf(w)).reshape(k // 32, 32, n)
    amax = np.abs(w).max(1)
    if fmt == "e4m3":
        byte = np.frexp(amax)[1] - 1 + 127 - 7
    else:
        mant, ex = np.frexp(amax / 6.0)
        byte = np.where(mant > 0.5, ex, ex - 1) + 127
    byte = np.clip(np.where(amax > 0, byte, 1), 1, 254)
    scaled = (w * np.exp2(127.0 - byte)[:, None, :]).reshape(k, n).astype(np.float32)
    by_word = np.ascontiguousarray(scaled.reshape(k // 512, 128, 4, n).transpose(0, 1, 3, 2))
    if fmt == "e4m3":
        words = by_word.astype(ml_dtypes.float8_e4m3fn).view(np.uint8)
    else:
        c = by_word.astype(ml_dtypes.float4_e2m1fn).view(np.uint8) & 0xF
        words = c[..., 0::2] | (c[..., 1::2] << 4)
    return np.ascontiguousarray(words), np.ascontiguousarray(byte.astype(np.uint8).reshape(k // 512, 16, n))


def unpack_weight(words, scales, fmt):
    g, p, n, _ = words.shape
    if fmt == "e4m3":
        vals = np.ascontiguousarray(words).view(ml_dtypes.float8_e4m3fn).astype(np.float64)
    else:
        nib = np.empty((g, p, n, 4), np.uint8)
        nib[..., 0::2] = words & 0xF
        nib[..., 1::2] = words >> 4
        vals = E2M1[nib]
    vals = vals * np.repeat(np.exp2(scales.astype(np.float64) - 127.0), 8, axis=1)[..., None]
    return vals.transpose(0, 1, 3, 2).reshape(g * 512, n)

def planes(Y):
    n, m = Y.shape
    b = f64(bf(Y)).reshape(n // 32, 32, m)
    amax = np.abs(b).max(1)
    byte = np.clip(np.where(amax > 0, np.frexp(amax)[1] - 1 + 127 - 7, 1), 1, 254)
    codes = (b * np.exp2(127.0 - byte)[:, None, :]).reshape(n, m).astype(np.float32).astype(ml_dtypes.float8_e4m3fn).view(np.uint8)
    words = codes.reshape(n // 512, 128, 4, m).transpose(0, 1, 3, 2)
    return np.ascontiguousarray(words), np.ascontiguousarray(byte.astype(np.uint8).reshape(n // 512, 16, m))


B, D, F, N = 1024, 512, 1024, 1024


def softmax(v):
    e = np.exp(v - v.max(axis=-1, keepdims=True))
    return e / e.sum(axis=-1, keepdims=True)


def archetypes(logits, g, c):
    p = softmax(logits)
    pg = p * g[None, :]
    return mxq(pg, 1, "e4m3") @ c


def bounded_relaxation(lam):
    sq = np.sum(lam * lam, axis=-1)
    r = np.minimum(1.0, 1.0 / np.sqrt(sq + 1e-12))
    return lam * r[:, None]


def setup_inputs():
    kd, kn, kf = mx_kscale(D), mx_kscale(N), mx_kscale(F)
    x = bf(np.random.standard_normal((B, D)) * kd)
    we_words, we_scales = pack_weight(
        np.random.standard_normal((D, F)) / np.sqrt(D) / kd[:, None] * kf[None, :], "e4m3")
    logits = bf(np.random.standard_normal((F, N)) * 2.0)
    g = bf(np.random.standard_normal(N) * kn)
    c_words, c_scales = pack_weight(
        np.random.standard_normal((N, D)) * (4.0 * np.sqrt(N) / F) / kn[:, None], "e4m3")
    return {
        "x": x,
        "we_words": we_words,
        "we_scales": we_scales,
        "logits": logits,
        "g": g,
        "c_words": c_words,
        "c_scales": c_scales,
        "lam": bf(np.random.standard_normal((F, D)) / np.sqrt(D) * np.random.uniform(0.2, 2.0, (F, 1))),
        "s": bf((1.0 + 0.2 * np.random.standard_normal(F)) / kf),
    }


def core(x, we_words, we_scales, logits, g, c_words, c_scales, lam, s):
    z = np.maximum(mxq(f64(x), 1, "e4m3") @ unpack_weight(we_words, we_scales, "e4m3"), 0.0)
    a = archetypes(f64(logits), f64(g), unpack_weight(c_words, c_scales, "e4m3"))
    lamp = bounded_relaxation(f64(lam))
    dic = f64(s)[:, None] * (a + lamp)
    return mxq(z, 1, "e4m3") @ mxq(dic, 0, "e4m3")


def reference(x, we_words, we_scales, logits, g, c_words, c_scales, lam, s):
    R_out = core(x, we_words, we_scales, logits, g, c_words, c_scales, lam, s)
    words, scales = planes(R_out)
    return R_out, words, scales

@@ -1,0 +1,504 @@
+from contextlib import ExitStack
+
+import concourse.mybir as mybir
+from concourse.masks import make_identity
+
+B, D, F, N = 1024, 512, 1024, 1024
+FLOPS = 2 * B * D * F + 2 * F * N * D + 2 * B * F * D
+
+F32 = mybir.dt.float32
+BF16 = mybir.dt.bfloat16
+I32 = mybir.dt.int32
+U32 = mybir.dt.uint32
+U8 = mybir.dt.uint8
+FP8X4 = mybir.dt.float8_e4m3fn_x4
+ALU = mybir.AluOpType
+ACT = mybir.ActivationFunctionType
+
+P = 128
+PACK = 4
+K_PASS = P * PACK
+GROUPS = 2
+TILES = GROUPS * PACK
+HALF = D // 2
+EPS = 1e-12
+
+
+def tile_relaxedarchetypalreluautoencoder_x2_kernel(
+    tc, x, we_words, we_scales, logits, g, c_words, c_scales, lam, s, out_0, out_1, out_2
+):
+    nc = tc.nc
+    with ExitStack() as ctx:
+        keep = ctx.enter_context(tc.tile_pool(name="keep", bufs=1))
+        work = ctx.enter_context(tc.tile_pool(name="work", bufs=2))
+        psum = ctx.enter_context(tc.psum_pool(name="psum", bufs=2))
+        ctx.enter_context(tc.manual_schedule())
+
+        def kept(name, shape, dtype):
+            return keep.tile(shape, dtype, name=name, align_bytes=64)
+
+        def kept_list(name, count, shape, dtype):
+            return [kept("%s%d" % (name, i), shape, dtype) for i in range(count)]
+
+        ident = kept("ident", [P, P], F32)
+        minus_half = kept("minus_half", [P, 2], F32)
+        warm = kept("warm", [P, 1], F32)
+        logit_t = kept_list("logit", TILES, [P, N], BF16)
+        lam_t = kept_list("lam", TILES // 2, [P, 2, D], BF16)
+        x_t = kept_list("x", GROUPS, [P, PACK, D], BF16)
+        g_col = kept("g_col", [P, GROUPS, PACK], BF16)
+        s_col = kept("s_col", [P, GROUPS, PACK], BF16)
+        we_raw = kept("we_raw", [P, F], U32)
+        we_raw_sc = kept("we_raw_sc", [P, F], U8)
+        we_q = kept("we_q", [P, F], U32)
+        we_sc = kept("we_sc", [P, F], U8)
+        c_q = kept("c_q", [P, GROUPS * D], U32)
+        c_sc = kept("c_sc", [P, GROUPS * D], U8)
+        x_q = kept_list("x_q", GROUPS, [P, K_PASS], U32)
+        x_sc = kept_list("x_sc", GROUPS, [P, K_PASS], U8)
+        z_q = kept_list("z_q", TILES, [P, GROUPS * P], U32)
+        z_sc = kept_list("z_sc", TILES, [P, GROUPS * P], U8)
+        dic_rows = kept_list("dic_rows", GROUPS, [P, PACK, D], BF16)
+        dic_q = kept_list("dic_q", GROUPS, [P, D], U32)
+        dic_sc = kept_list("dic_sc", GROUPS, [P, D], U8)
+        out_t = kept_list("out", 2 * GROUPS, [P, PACK, HALF], F32)
+        out_q = kept_list("out_q", GROUPS, [P, D], U32)
+        out_sc = kept_list("out_sc", GROUPS, [P, D], U8)
+        neg_max = kept_list("neg_max", TILES, [P, 1], F32)
+        exp_sum = kept_list("exp_sum", TILES, [P, 1], F32)
+        inv_sum = kept_list("inv_sum", TILES, [P, 1], F32)
+        sq_sum = kept_list("sq_sum", TILES // 2, [P, 2], F32)
+        lam_gain = kept_list("lam_gain", TILES // 2, [P, 2], F32)
+        live = {}
+
+        def load_logits(j):
+            grp, t = divmod(j, PACK)
+            rows = logits[grp * K_PASS:(grp + 1) * K_PASS, :].rearrange("(p t) n -> p t n", t=PACK)
+            nc.sync.dma_start(out=logit_t[j][:], in_=rows[:, t, :])
+
+        def load_lam(pair):
+            grp, h = divmod(pair, 2)
+            rows = lam[grp * K_PASS:(grp + 1) * K_PASS, :].rearrange("(p t) d -> p t d", t=PACK)
+            nc.sync.dma_start(out=lam_t[pair][:], in_=rows[:, 2 * h:2 * h + 2, :])
+
+        def load_x(grp):
+            rows = x[grp * K_PASS:(grp + 1) * K_PASS, :].rearrange("(p t) d -> p t d", t=PACK)
+            nc.sync.dma_start(out=x_t[grp][:], in_=rows)
+
+        def load_we():
+            words = we_words[0].rearrange("p n t -> p (n t)").bitcast(I32)
+            nc.sync.dma_start(out=we_raw[:].bitcast(I32), in_=words)
+            for q in range(4):
+                nc.sync.dma_start(
+                    out=we_raw_sc[32 * q:32 * q + 4, :].bitcast(I32),
+                    in_=we_scales[0, 4 * q:4 * q + 4, :].bitcast(I32),
+                )
+
+        def load_c():
+            words = c_words.rearrange("g p d t -> p g (d t)").bitcast(I32)
+            nc.sync.dma_start(out=c_q[:].bitcast(I32).rearrange("p (g d) -> p g d", g=GROUPS), in_=words)
+            for q in range(4):
+                nc.sync.dma_start(
+                    out=c_sc[32 * q:32 * q + 4, :].bitcast(I32).rearrange("r (g d) -> r g d", g=GROUPS),
+                    in_=c_scales[:, 4 * q:4 * q + 4, :].bitcast(I32).rearrange("g r d -> r g d"),
+                )
+
+        def quantize(codes, scales, values):
+            nc.vector.quantize_mx(out=codes.bitcast(FP8X4), scales=scales, in_=values)
+
+        def mx_pass(acc, lhs_q, lhs_sc, rhs_q, rhs_sc, first, last):
+            nc.tensor.matmul_mx(
+                out=acc, lhsT=lhs_q.bitcast(FP8X4), lhsT_scale=lhs_sc,
+                rhs=rhs_q.bitcast(FP8X4), rhs_scale=rhs_sc, start=first, stop=last,
+            )
+
+        def interleave(dst, src):
+            nc.vector.tensor_copy(
+                out=dst.rearrange("p (c i) t -> p c t i", i=4),
+                in_=src.rearrange("p t (c i) -> p c t i", i=4),
+            )
+
+        def spread_g():
+            live["g"] = bank = psum.tile([P, 2, GROUPS, P], F32, name="g_row", bufs=1)
+            words = g_col[:].bitcast(F32)
+            for u in range(2):
+                for ng in range(GROUPS):
+                    nc.tensor.transpose(bank[:, u, ng, :], words[:, ng, u:u + 1].to_broadcast([P, P]), ident[:])
+
+        def sort_we_codes():
+            nc.vector.tensor_copy(
+                out=we_q[:].bitcast(I32).rearrange("p (g t c i) -> p g c t i", g=GROUPS, t=PACK, i=4),
+                in_=we_raw[:].bitcast(I32).rearrange("p (g c i t) -> p g c t i", g=GROUPS, t=PACK, i=4),
+            )
+
+        def sort_we_scales():
+            nc.vector.tensor_copy(
+                out=we_sc[:].rearrange("p (g t m) -> p g t m", g=GROUPS, t=PACK),
+                in_=we_raw_sc[:].rearrange("p (g m t) -> p g t m", g=GROUPS, t=PACK),
+            )
+
+        def turn_x(grp, pair):
+            words = x_t[grp][:].bitcast(F32)
+            live["x_bank", grp, pair] = bank = psum.tile([P, 2, 2, P], F32, name="z_acc")
+            for a in range(2):
+                for u in range(2):
+                    nc.tensor.transpose(bank[:, a, u, :], words[:, 2 * pair + a, u:D // 2:2], ident[:])
+
+        def fetch_x(grp, pair):
+            if pair == 0:
+                live["xT", grp] = work.tile([P, PACK, P, PACK], BF16, name="xT", align_bytes=64)
+            nc.scalar.copy(
+                out=live["xT", grp][:, 2 * pair:2 * pair + 2, :, :].bitcast(F32),
+                in_=live["x_bank", grp, pair][:].rearrange("p a u m -> p a m u"),
+            )
+
+        def quantize_x(grp):
+            quantize(x_q[grp][:], x_sc[grp][:], live["xT", grp][:].rearrange("p a m t -> p (a m t)"))
+
+        def encode(n, tag="z_acc"):
+            i, fg = divmod(n, GROUPS)
+            grp, slot = divmod(i, PACK)
+            cols = slice(slot * P, (slot + 1) * P)
+            live["z_bank", n] = bank = psum.tile([P, PACK, P], F32, name=tag)
+            for t in range(PACK):
+                wcols = slice((fg * PACK + t) * P, (fg * PACK + t + 1) * P)
+                mx_pass(bank[:, t, :], we_q[:, wcols], we_sc[:, wcols],
+                        x_q[grp][:, cols], x_sc[grp][:, cols], True, True)
+
+        def rectify(n, on_vector=False):
+            i, fg = divmod(n, GROUPS)
+            if fg == 0:
+                live["z", i] = work.tile([P, GROUPS, P, PACK], BF16, name="zT", align_bytes=64, bufs=4)
+            src = live["z_bank", n][:].rearrange("p t m -> p m t")
+            if on_vector:
+                nc.vector.tensor_scalar(out=live["z", i][:, fg, :, :], in0=src, scalar1=0.0, scalar2=None,
+                                        op0=ALU.max)
+            else:
+                nc.scalar.activation(out=live["z", i][:, fg, :, :], in_=src, func=ACT.Relu)
+
+        def quantize_z(i):
+            quantize(z_q[i][:], z_sc[i][:], live["z", i][:].rearrange("p g m t -> p (g m t)"))
+
+        def row_max(j):
+            live["neg", j] = neg = work.tile([P, N], BF16, name="neg", bufs=4)
+            nc.vector.tensor_scalar(
+                out=neg[:], in0=logit_t[j][:], scalar1=-1.0, scalar2=None,
+                op0=ALU.mult, op1=ALU.min, accum_out=neg_max[j][:],
+            )
+
+        def exponentials(j):
+            live["exp", j] = e = work.tile([P, N], F32, name="e")
+            nc.scalar.activation(
+                out=e[:].rearrange("p (u w h) -> p u w h", u=2, h=2),
+                in_=live["neg", j][:].rearrange("p (w u h) -> p u w h", u=2, h=2),
+                func=ACT.Exp, scale=-1.0, bias=neg_max[j][:], accum_out=exp_sum[j][:],
+            )
+
+        def invert_sum(j):
+            nc.vector.reciprocal(out=inv_sum[j][:], in_=exp_sum[j][:])
+
+        def weights(j):
+            live["pg", j] = pg = work.tile([P, N], BF16, name="pg")
+            nc.vector.scalar_tensor_tensor(
+                out=pg[:], in0=live["exp", j][:], scalar=inv_sum[j][:], in1=live["g"][:].rearrange("p u g n -> p (u g n)").bitcast(BF16),
+                op0=ALU.mult, op1=ALU.mult,
+            )
+
+        def turn_weights(j):
+            live["pg_bank", j] = bank = psum.tile([P, PACK, P], F32, name="turn")
+            words = live["pg", j][:].bitcast(F32)
+            for w in range(PACK):
+                nc.tensor.transpose(bank[:, w, :], words[:, w * P:(w + 1) * P], ident[:])
+
+        def fetch_weights(j):
+            live["pgT", j] = pgT = work.tile([P, GROUPS, P, PACK], BF16, name="pgT", align_bytes=64)
+            nc.scalar.copy(
+                out=pgT[:].bitcast(F32),
+                in_=live["pg_bank", j][:].rearrange("p (u g) f -> p g f u", u=2),
+            )
+
+        def quantize_weights(j):
+            live["pg_q", j] = codes = work.tile([P, GROUPS * P], U32, name="pg_q", align_bytes=64)
+            live["pg_sc", j] = scales = work.tile([P, GROUPS * P], U8, name="pg_sc", align_bytes=64)
+            quantize(codes[:], scales[:], live["pgT", j][:].rearrange("p g f t -> p (g f t)"))
+
+        def archetypes(j, parts=1):
+            live["a", j] = acc = psum.tile([P, D], F32, name="acc", bufs=3)
+            width = D // parts
+            for part in range(parts):
+                for ng in range(GROUPS):
+                    fcols = slice(ng * P, (ng + 1) * P)
+                    dcols = slice(ng * D + part * width, ng * D + (part + 1) * width)
+                    mx_pass(acc[:, part * width:(part + 1) * width], live["pg_q", j][:, fcols], live["pg_sc", j][:, fcols],
+                            c_q[:, dcols], c_sc[:, dcols], ng == 0, ng == GROUPS - 1)
+
+        def lam_rows(j):
+            return lam_t[j // 2][:, j % 2, :]
+
+        def gain(j):
+            return s_col[:, j // PACK, j % PACK:j % PACK + 1]
+
+        def lam_norm(j):
+            squares = work.tile([P, D], BF16, name="squares")
+            nc.scalar.activation(out=squares[:], in_=lam_rows(j), func=ACT.Square,
+                                 accum_out=sq_sum[j // 2][:, j % 2:j % 2 + 1])
+
+        def lam_factor(pair):
+            bounded = work.tile([P, 2], F32, name="bounded")
+            shrink = work.tile([P, 2], F32, name="shrink")
+            gains = s_col[:, pair // 2, 2 * (pair % 2):2 * (pair % 2) + 2]
+            nc.gpsimd.tensor_scalar(out=bounded[:], in0=sq_sum[pair][:], scalar1=EPS, scalar2=1.0,
+                                    op0=ALU.add, op1=ALU.max)
+            nc.gpsimd.tensor_tensor(out=shrink[:], in0=bounded[:], in1=minus_half[:], op=ALU.pow)
+            nc.gpsimd.tensor_tensor(out=lam_gain[pair][:], in0=shrink[:], in1=gains, op=ALU.mult)
+
+        def scale_lam(j):
+            live["lam", j] = scaled = work.tile([P, D], F32, name="lam_scaled", bufs=3)
+            nc.gpsimd.tensor_scalar(out=scaled[:], in0=lam_rows(j),
+                                    scalar1=lam_gain[j // 2][:, j % 2:j % 2 + 1], scalar2=0.0,
+                                    op0=ALU.mult, op1=ALU.add)
+
+        def dictionary(j, cols):
+            nc.vector.scalar_tensor_tensor(
+                out=dic_rows[j // PACK][:, j % PACK, cols], in0=live["a", j][:, cols], scalar=gain(j),
+                in1=live["lam", j][:, cols], op0=ALU.mult, op1=ALU.add,
+            )
+
+        def interleave_dic(grp, half):
+            live["dicT", grp, half] = dicT = work.tile([P, HALF, PACK], BF16, name="dicT", align_bytes=64, bufs=4)
+            interleave(dicT[:], dic_rows[grp][:, :, half * HALF:(half + 1) * HALF])
+
+        def quantize_dic(grp, half):
+            cols = slice(half * HALF, (half + 1) * HALF)
+            quantize(dic_q[grp][:, cols], dic_sc[grp][:, cols],
+                     live["dicT", grp, half][:].rearrange("p d t -> p (d t)"))
+
+        def decode(grp, half, pair, tag="acc"):
+            cols = slice(half * HALF, (half + 1) * HALF)
+            live["o_bank", grp, half, pair] = bank = psum.tile([P, 2, HALF], F32, name=tag, bufs=3 if tag == "acc" else 1)
+            for a in range(2):
+                i = grp * PACK + 2 * pair + a
+                for fg in range(GROUPS):
+                    bcols = slice(fg * P, (fg + 1) * P)
+                    mx_pass(bank[:, a, :], z_q[i][:, bcols], z_sc[i][:, bcols],
+                            dic_q[fg][:, cols], dic_sc[fg][:, cols], fg == 0, fg == GROUPS - 1)
+
+        def fetch_out(grp, half, pair, on_vector=False):
+            dst = out_t[2 * grp + half][:, 2 * pair:2 * pair + 2, :]
+            if on_vector:
+                nc.vector.tensor_copy(out=dst, in_=live["o_bank", grp, half, pair][:])
+            else:
+                nc.scalar.copy(out=dst, in_=live["o_bank", grp, half, pair][:])
+
+        def store_out(grp, half):
+            rows = out_0[grp * K_PASS:(grp + 1) * K_PASS, :].rearrange("(p t) d -> p t d", t=PACK)
+            nc.sync.dma_start(out=rows[:, :, half * HALF:(half + 1) * HALF], in_=out_t[2 * grp + half][:])
+
+        def interleave_out(grp, half):
+            live["outT", grp, half] = outT = work.tile([P, HALF, PACK], BF16, name="outT", align_bytes=64)
+            interleave(outT[:], out_t[2 * grp + half][:])
+
+        def quantize_out(grp, half):
+            cols = slice(half * HALF, (half + 1) * HALF)
+            quantize(out_q[grp][:, cols], out_sc[grp][:, cols],
+                     live["outT", grp, half][:].rearrange("p d t -> p (d t)"))
+
+        def store_codes(grp, cols):
+            words = out_1[grp].rearrange("p m t -> p (m t)").bitcast(I32)
+            nc.sync.dma_start(out=words[:, cols], in_=out_q[grp][:, cols].bitcast(I32))
+
+        def store_scales(grp):
+            for q in range(4):
+                nc.sync.dma_start(
+                    out=out_2[grp, 4 * q:4 * q + 4, :].bitcast(I32),
+                    in_=out_sc[grp][32 * q:32 * q + 4, :].bitcast(I32),
+                )
+
+        nc.vector.memset(warm[:], 0.0)
+        nc.vector.memset(we_raw_sc[:].bitcast(I32), 0)
+        nc.vector.memset(c_sc[:].bitcast(I32), 0)
+        make_identity(nc, ident[:])
+        nc.gpsimd.memset(minus_half[:], -0.5)
+        warm_out = kept("warm_out", [P, 1], F32)
+        nc.scalar.activation(out=warm_out[:], in_=warm[:], func=ACT.Exp)
+
+        load_logits(0)
+        nc.sync.dma_start(out=g_col[:], in_=g.rearrange("(g p t) -> p g t", g=GROUPS, t=PACK))
+        load_logits(1)
+        load_logits(2)
+        load_logits(3)
+        load_lam(0)
+        nc.sync.dma_start(out=s_col[:], in_=s.rearrange("(g p t) -> p g t", g=GROUPS, t=PACK))
+        load_x(0)
+        load_logits(4)
+        load_we()
+        load_lam(1)
+        load_logits(5)
+        load_c()
+        load_logits(6)
+        load_lam(2)
+        load_logits(7)
+        load_lam(3)
+        load_x(1)
+
+        whole = slice(0, D)
+        for j in range(3):
+            row_max(j)
+        spread_g()
+        exponentials(0)
+        invert_sum(0)
+        row_max(3)
+        exponentials(1)
+        lam_norm(0)
+        lam_norm(1)
+        lam_factor(0)
+        weights(0)
+        turn_x(0, 0)
+        turn_weights(0)
+        turn_x(0, 1)
+        invert_sum(1)
+        row_max(4)
+        fetch_x(0, 0)
+        fetch_weights(0)
+        exponentials(2)
+        fetch_x(0, 1)
+        weights(1)
+        scale_lam(0)
+        turn_weights(1)
+        quantize_weights(0)
+        sort_we_codes()
+        invert_sum(2)
+        row_max(5)
+        scale_lam(1)
+        lam_norm(2)
+        fetch_weights(1)
+        exponentials(3)
+        lam_norm(3)
+        lam_factor(1)
+        archetypes(0)
+        weights(2)
+        turn_weights(2)
+        quantize_weights(1)
+        archetypes(1)
+        quantize_x(0)
+        sort_we_scales()
+        for j in range(3, TILES):
+            dictionary(j - 3, whole)
+            scale_lam(j - 1)
+            if j == 7:
+                scale_lam(7)
+            invert_sum(j)
+            if j + 3 < TILES:
+                row_max(j + 3)
+            if j == 5:
+                quantize_z(0)
+            if j == 6:
+                quantize_x(1)
+            if j == 7:
+                interleave_dic(0, 0)
+            if j in (3, 4, 6):
+                lam_norm({3: 4, 4: 5, 6: 6}[j])
+            if j == 5:
+                fetch_x(1, 0)
+                turn_x(1, 1)
+            if j == 7:
+                rectify(2)
+            fetch_weights(j - 1)
+            if j + 1 < TILES:
+                exponentials(j + 1)
+            if j in (3, 4):
+                encode(j - 3)
+                rectify(j - 3)
+            if j == 4:
+                turn_x(1, 0)
+            if j == 5:
+                fetch_x(1, 1)
+            if j == 6:
+                lam_norm(7)
+                encode(2)
+                encode(3)
+            if j == 7:
+                encode(4)
+                rectify(3)
+                encode(5)
+                rectify(4)
+            weights(j)
+            if j in (4, 6):
+                lam_factor(j // 2)
+            turn_weights(j)
+            quantize_weights(j - 1)
+            archetypes(j - 1)
+        encode(6)
+        encode(7, "turn")
+        fetch_weights(7)
+        rectify(5)
+        dictionary(5, whole)
+        interleave_dic(0, 1)
+        quantize_z(1)
+        quantize_weights(7)
+        archetypes(7, 2)
+        encode(8, "turn")
+        encode(9)
+        rectify(6)
+        rectify(7)
+        encode(10)
+        encode(11, "turn")
+        dictionary(6, whole)
+        quantize_z(2)
+        dictionary(7, slice(0, HALF))
+        dictionary(7, slice(HALF, D))
+        rectify(8)
+        rectify(9)
+        encode(12, "turn")
+        encode(13)
+        quantize_dic(0, 0)
+        interleave_dic(1, 0)
+        quantize_z(3)
+        quantize_dic(1, 0)
+        rectify(10)
+        rectify(11)
+        decode(0, 0, 0, "g_row")
+        decode(0, 0, 1)
+        encode(14)
+        encode(15, "turn")
+        interleave_dic(1, 1)
+        quantize_dic(0, 1)
+        quantize_dic(1, 1)
+        decode(0, 1, 0)
+        decode(0, 1, 1)
+        rectify(12)
+        fetch_out(0, 0, 0)
+        fetch_out(0, 0, 1)
+        store_out(0, 0)
+        quantize_z(4)
+        quantize_z(5)
+        decode(1, 0, 0, "g_row")
+        rectify(13, True)
+        rectify(14, True)
+        fetch_out(0, 1, 0)
+        fetch_out(0, 1, 1)
+        store_out(0, 1)
+        rectify(15)
+        quantize_z(6)
+        interleave_out(0, 0)
+        quantize_z(7)
+        decode(1, 0, 1)
+        decode(1, 1, 0)
+        decode(1, 1, 1)
+        fetch_out(1, 0, 0)
+        quantize_out(0, 0)
+        interleave_out(0, 1)
+        fetch_out(1, 0, 1)
+        store_out(1, 0)
+        quantize_out(0, 1)
+        store_codes(0, whole)
+        store_scales(0)
+        interleave_out(1, 0)
+        fetch_out(1, 1, 0)
+        fetch_out(1, 1, 1)
+        store_out(1, 1)
+        interleave_out(1, 1)
+        quantize_out(1, 0)
+        quantize_out(1, 1)
+        store_codes(1, whole)
+        store_scales(1)

@@ -22,6 +22,7 @@ GROUPS = 2
 TILES = GROUPS * PACK
 HALF = D // 2
 EPS = 1e-12
+BANKS = {"g_row": 1, "turn": 2, "acc": 2, "z_acc": 3}
 
 
 def tile_relaxedarchetypalreluautoencoder_x2_kernel(
@@ -61,9 +62,8 @@ def tile_relaxedarchetypalreluautoencoder_x2_kernel(
         dic_rows = kept_list("dic_rows", GROUPS, [P, PACK, D], BF16)
         dic_q = kept_list("dic_q", GROUPS, [P, D], U32)
         dic_sc = kept_list("dic_sc", GROUPS, [P, D], U8)
-        out_t = kept_list("out", 2 * GROUPS, [P, PACK, HALF], F32)
         out_q = kept_list("out_q", GROUPS, [P, D], U32)
-        out_sc = kept_list("out_sc", GROUPS, [P, D], U8)
+        out_sc = kept("out_sc", [P, GROUPS, D], U8)
         neg_max = kept_list("neg_max", TILES, [P, 1], F32)
         exp_sum = kept_list("exp_sum", TILES, [P, 1], F32)
         inv_sum = kept_list("inv_sum", TILES, [P, 1], F32)
@@ -88,8 +88,10 @@ def tile_relaxedarchetypalreluautoencoder_x2_kernel(
         def load_we():
             words = we_words[0].rearrange("p n t -> p (n t)").bitcast(I32)
             nc.sync.dma_start(out=we_raw[:].bitcast(I32), in_=words)
+
+        def load_we_scales():
             for q in range(4):
-                nc.sync.dma_start(
+                nc.gpsimd.dma_start(
                     out=we_raw_sc[32 * q:32 * q + 4, :].bitcast(I32),
                     in_=we_scales[0, 4 * q:4 * q + 4, :].bitcast(I32),
                 )
@@ -97,8 +99,10 @@ def tile_relaxedarchetypalreluautoencoder_x2_kernel(
         def load_c():
             words = c_words.rearrange("g p d t -> p g (d t)").bitcast(I32)
             nc.sync.dma_start(out=c_q[:].bitcast(I32).rearrange("p (g d) -> p g d", g=GROUPS), in_=words)
+
+        def load_c_scales():
             for q in range(4):
-                nc.sync.dma_start(
+                nc.gpsimd.dma_start(
                     out=c_sc[32 * q:32 * q + 4, :].bitcast(I32).rearrange("r (g d) -> r g d", g=GROUPS),
                     in_=c_scales[:, 4 * q:4 * q + 4, :].bitcast(I32).rearrange("g r d -> r g d"),
                 )
@@ -139,7 +143,7 @@ def tile_relaxedarchetypalreluautoencoder_x2_kernel(
 
         def turn_x(grp, pair):
             words = x_t[grp][:].bitcast(F32)
-            live["x_bank", grp, pair] = bank = psum.tile([P, 2, 2, P], F32, name="z_acc")
+            live["x_bank", grp, pair] = bank = psum.tile([P, 2, 2, P], F32, name="z_acc", bufs=3)
             for a in range(2):
                 for u in range(2):
                     nc.tensor.transpose(bank[:, a, u, :], words[:, 2 * pair + a, u:D // 2:2], ident[:])
@@ -159,7 +163,7 @@ def tile_relaxedarchetypalreluautoencoder_x2_kernel(
             i, fg = divmod(n, GROUPS)
             grp, slot = divmod(i, PACK)
             cols = slice(slot * P, (slot + 1) * P)
-            live["z_bank", n] = bank = psum.tile([P, PACK, P], F32, name=tag)
+            live["z_bank", n] = bank = psum.tile([P, PACK, P], F32, name=tag, bufs=BANKS[tag])
             for t in range(PACK):
                 wcols = slice((fg * PACK + t) * P, (fg * PACK + t + 1) * P)
                 mx_pass(bank[:, t, :], we_q[:, wcols], we_sc[:, wcols],
@@ -187,7 +191,7 @@ def tile_relaxedarchetypalreluautoencoder_x2_kernel(
             )
 
         def exponentials(j):
-            live["exp", j] = e = work.tile([P, N], F32, name="e")
+            live["exp", j] = e = work.tile([P, N], F32, name="e", bufs=3)
             nc.scalar.activation(
                 out=e[:].rearrange("p (u w h) -> p u w h", u=2, h=2),
                 in_=live["neg", j][:].rearrange("p (w u h) -> p u w h", u=2, h=2),
@@ -223,7 +227,7 @@ def tile_relaxedarchetypalreluautoencoder_x2_kernel(
             quantize(codes[:], scales[:], live["pgT", j][:].rearrange("p g f t -> p (g f t)"))
 
         def archetypes(j, parts=1):
-            live["a", j] = acc = psum.tile([P, D], F32, name="acc", bufs=3)
+            live["a", j] = acc = psum.tile([P, D], F32, name="acc")
             width = D // parts
             for part in range(parts):
                 for ng in range(GROUPS):
@@ -252,9 +256,9 @@ def tile_relaxedarchetypalreluautoencoder_x2_kernel(
             nc.gpsimd.tensor_tensor(out=shrink[:], in0=bounded[:], in1=minus_half[:], op=ALU.pow)
             nc.gpsimd.tensor_tensor(out=lam_gain[pair][:], in0=shrink[:], in1=gains, op=ALU.mult)
 
-        def scale_lam(j):
-            live["lam", j] = scaled = work.tile([P, D], F32, name="lam_scaled", bufs=3)
-            nc.gpsimd.tensor_scalar(out=scaled[:], in0=lam_rows(j),
+        def scale_lam(j, engine):
+            live["lam", j] = scaled = work.tile([P, D], F32, name="lam_scaled")
+            engine.tensor_scalar(out=scaled[:], in0=lam_rows(j),
                                     scalar1=lam_gain[j // 2][:, j % 2:j % 2 + 1], scalar2=0.0,
                                     op0=ALU.mult, op1=ALU.add)
 
@@ -273,45 +277,44 @@ def tile_relaxedarchetypalreluautoencoder_x2_kernel(
             quantize(dic_q[grp][:, cols], dic_sc[grp][:, cols],
                      live["dicT", grp, half][:].rearrange("p d t -> p (d t)"))
 
-        def decode(grp, half, pair, tag="acc"):
-            cols = slice(half * HALF, (half + 1) * HALF)
-            live["o_bank", grp, half, pair] = bank = psum.tile([P, 2, HALF], F32, name=tag, bufs=3 if tag == "acc" else 1)
-            for a in range(2):
-                i = grp * PACK + 2 * pair + a
+        def decode(grp, cols, slots, tag):
+            width = cols.stop - cols.start
+            count = slots.stop - slots.start
+            live["o_bank", grp, cols.start, slots.start] = bank = psum.tile([P, count, width], F32, name=tag, bufs=BANKS[tag])
+            for a in range(count):
+                i = grp * PACK + slots.start + a
                 for fg in range(GROUPS):
                     bcols = slice(fg * P, (fg + 1) * P)
                     mx_pass(bank[:, a, :], z_q[i][:, bcols], z_sc[i][:, bcols],
                             dic_q[fg][:, cols], dic_sc[fg][:, cols], fg == 0, fg == GROUPS - 1)
 
-        def fetch_out(grp, half, pair, on_vector=False):
-            dst = out_t[2 * grp + half][:, 2 * pair:2 * pair + 2, :]
-            if on_vector:
-                nc.vector.tensor_copy(out=dst, in_=live["o_bank", grp, half, pair][:])
-            else:
-                nc.scalar.copy(out=dst, in_=live["o_bank", grp, half, pair][:])
+        def fetch_out(grp, cols, slots):
+            if slots.start == 0:
+                live["out", grp, cols.start] = work.tile([P, PACK, cols.stop - cols.start], F32, name="out", bufs=5)
+            nc.scalar.copy(out=live["out", grp, cols.start][:, slots, :], in_=live["o_bank", grp, cols.start, slots.start][:])
+            store_out(grp, cols, slots)
 
-        def store_out(grp, half):
+        def store_out(grp, cols, slots):
             rows = out_0[grp * K_PASS:(grp + 1) * K_PASS, :].rearrange("(p t) d -> p t d", t=PACK)
-            nc.sync.dma_start(out=rows[:, :, half * HALF:(half + 1) * HALF], in_=out_t[2 * grp + half][:])
+            nc.sync.dma_start(out=rows[:, slots, cols], in_=live["out", grp, cols.start][:, slots, :])
 
-        def interleave_out(grp, half):
-            live["outT", grp, half] = outT = work.tile([P, HALF, PACK], BF16, name="outT", align_bytes=64)
-            interleave(outT[:], out_t[2 * grp + half][:])
+        def interleave_out(grp, cols):
+            live["outT", grp, cols.start] = outT = work.tile([P, cols.stop - cols.start, PACK], BF16, name="outT", align_bytes=64, bufs=3)
+            interleave(outT[:], live["out", grp, cols.start][:])
 
-        def quantize_out(grp, half):
-            cols = slice(half * HALF, (half + 1) * HALF)
-            quantize(out_q[grp][:, cols], out_sc[grp][:, cols],
-                     live["outT", grp, half][:].rearrange("p d t -> p (d t)"))
+        def quantize_out(grp, cols):
+            quantize(out_q[grp][:, cols], out_sc[:, grp, cols],
+                     live["outT", grp, cols.start][:].rearrange("p d t -> p (d t)"))
 
         def store_codes(grp, cols):
             words = out_1[grp].rearrange("p m t -> p (m t)").bitcast(I32)
             nc.sync.dma_start(out=words[:, cols], in_=out_q[grp][:, cols].bitcast(I32))
 
-        def store_scales(grp):
+        def store_scales():
             for q in range(4):
-                nc.sync.dma_start(
-                    out=out_2[grp, 4 * q:4 * q + 4, :].bitcast(I32),
-                    in_=out_sc[grp][32 * q:32 * q + 4, :].bitcast(I32),
+                (nc.sync, nc.scalar)[q % 2].dma_start(
+                    out=out_2[:, 4 * q:4 * q + 4, :].bitcast(I32).rearrange("g r d -> r g d"),
+                    in_=out_sc[32 * q:32 * q + 4, :, :].bitcast(I32),
                 )
 
         nc.vector.memset(warm[:], 0.0)
@@ -329,176 +332,161 @@ def tile_relaxedarchetypalreluautoencoder_x2_kernel(
         load_logits(3)
         load_lam(0)
         nc.sync.dma_start(out=s_col[:], in_=s.rearrange("(g p t) -> p g t", g=GROUPS, t=PACK))
-        load_x(0)
-        load_logits(4)
-        load_we()
         load_lam(1)
+        load_logits(4)
+        load_x(0)
         load_logits(5)
         load_c()
+        load_we()
         load_logits(6)
         load_lam(2)
         load_logits(7)
         load_lam(3)
         load_x(1)
+        load_we_scales()
+        load_c_scales()
 
         whole = slice(0, D)
+        halves = [slice(0, HALF), slice(HALF, D)]
         for j in range(3):
             row_max(j)
         spread_g()
         exponentials(0)
-        invert_sum(0)
-        row_max(3)
-        exponentials(1)
-        lam_norm(0)
-        lam_norm(1)
-        lam_factor(0)
-        weights(0)
-        turn_x(0, 0)
-        turn_weights(0)
-        turn_x(0, 1)
-        invert_sum(1)
-        row_max(4)
-        fetch_x(0, 0)
-        fetch_weights(0)
-        exponentials(2)
-        fetch_x(0, 1)
-        weights(1)
-        scale_lam(0)
-        turn_weights(1)
-        quantize_weights(0)
-        sort_we_codes()
-        invert_sum(2)
-        row_max(5)
-        scale_lam(1)
-        lam_norm(2)
-        fetch_weights(1)
-        exponentials(3)
-        lam_norm(3)
-        lam_factor(1)
-        archetypes(0)
-        weights(2)
-        turn_weights(2)
-        quantize_weights(1)
-        archetypes(1)
-        quantize_x(0)
-        sort_we_scales()
-        for j in range(3, TILES):
-            dictionary(j - 3, whole)
-            scale_lam(j - 1)
-            if j == 7:
-                scale_lam(7)
+        LAM = {0: 0, 1: 1, 3: 2, 4: 3}
+        for j in range(TILES):
             invert_sum(j)
+            if j >= 3:
+                dictionary(j - 3, whole)
+                scale_lam(j - 1, nc.gpsimd)
+            if j - 1 in LAM:
+                lam_factor(LAM[j - 1])
+            if j in (1, 2):
+                scale_lam(j - 1, nc.gpsimd)
             if j + 3 < TILES:
                 row_max(j + 3)
-            if j == 5:
-                quantize_z(0)
-            if j == 6:
-                quantize_x(1)
-            if j == 7:
-                interleave_dic(0, 0)
-            if j in (3, 4, 6):
-                lam_norm({3: 4, 4: 5, 6: 6}[j])
-            if j == 5:
-                fetch_x(1, 0)
-                turn_x(1, 1)
-            if j == 7:
-                rectify(2)
-            fetch_weights(j - 1)
-            if j + 1 < TILES:
+            if j in (0, 5, 6):
                 exponentials(j + 1)
-            if j in (3, 4):
-                encode(j - 3)
-                rectify(j - 3)
+            if j in LAM:
+                lam_norm(2 * LAM[j])
+            if j == 2:
+                fetch_x(0, 0)
+            if j >= 1:
+                fetch_weights(j - 1)
+            if 1 <= j <= 4:
+                exponentials(j + 1)
+            if j in LAM:
+                lam_norm(2 * LAM[j] + 1)
+            if j == 2:
+                fetch_x(0, 1)
+            if j == 1:
+                turn_x(0, 0)
+                turn_x(0, 1)
             if j == 4:
-                turn_x(1, 0)
-            if j == 5:
-                fetch_x(1, 1)
-            if j == 6:
-                lam_norm(7)
+                encode(0)
+                encode(1)
                 encode(2)
-                encode(3)
+            if j == 5:
+                rectify(0)
+            if j == 6:
+                rectify(1)
+                rectify(2)
+                fetch_x(1, 0)
             if j == 7:
-                encode(4)
                 rectify(3)
-                encode(5)
-                rectify(4)
+                fetch_x(1, 1)
             weights(j)
-            if j in (4, 6):
-                lam_factor(j // 2)
             turn_weights(j)
-            quantize_weights(j - 1)
-            archetypes(j - 1)
+            if j == 6:
+                encode(3)
+            if j >= 1:
+                quantize_weights(j - 1)
+                archetypes(j - 1)
+            if j in (5, 6):
+                turn_x(1, j - 5)
+            if j == 2:
+                sort_we_codes()
+            if j == 3:
+                quantize_x(0)
+            if j == 1:
+                sort_we_scales()
+        lo, hi, q2, q3 = halves[0], halves[1], slice(HALF, HALF + P), slice(HALF + P, D)
+        s01, s23, s03 = slice(0, 2), slice(2, 4), slice(0, 4)
+        encode(4)
+        encode(5)
         encode(6)
         encode(7, "turn")
         fetch_weights(7)
-        rectify(5)
         dictionary(5, whole)
-        interleave_dic(0, 1)
-        quantize_z(1)
+        quantize_z(0)
+        scale_lam(7, nc.vector)
+        quantize_x(1)
         quantize_weights(7)
         archetypes(7, 2)
         encode(8, "turn")
+        rectify(4)
         encode(9)
-        rectify(6)
-        rectify(7)
+        rectify(5)
         encode(10)
-        encode(11, "turn")
         dictionary(6, whole)
-        quantize_z(2)
-        dictionary(7, slice(0, HALF))
-        dictionary(7, slice(HALF, D))
-        rectify(8)
-        rectify(9)
+        quantize_z(1)
+        interleave_dic(0, 0)
+        dictionary(7, lo)
+        dictionary(7, hi)
+        rectify(6)
+        encode(11)
+        rectify(7)
         encode(12, "turn")
-        encode(13)
-        quantize_dic(0, 0)
+        quantize_z(2)
         interleave_dic(1, 0)
-        quantize_z(3)
+        quantize_dic(0, 0)
         quantize_dic(1, 0)
-        rectify(10)
-        rectify(11)
-        decode(0, 0, 0, "g_row")
-        decode(0, 0, 1)
+        quantize_z(3)
+        rectify(8)
+        encode(13, "turn")
+        rectify(9)
         encode(14)
-        encode(15, "turn")
+        rectify(10)
+        encode(15)
+        decode(0, lo, s01, "g_row")
+        decode(0, lo, s23, "acc")
+        interleave_dic(0, 1)
         interleave_dic(1, 1)
         quantize_dic(0, 1)
         quantize_dic(1, 1)
-        decode(0, 1, 0)
-        decode(0, 1, 1)
+        rectify(11)
         rectify(12)
-        fetch_out(0, 0, 0)
-        fetch_out(0, 0, 1)
-        store_out(0, 0)
+        rectify(13)
+        decode(0, hi, s01, "acc")
+        decode(0, hi, s23, "turn")
+        fetch_out(0, lo, s01)
+        fetch_out(0, lo, s23)
         quantize_z(4)
         quantize_z(5)
-        decode(1, 0, 0, "g_row")
-        rectify(13, True)
-        rectify(14, True)
-        fetch_out(0, 1, 0)
-        fetch_out(0, 1, 1)
-        store_out(0, 1)
-        rectify(15)
+        rectify(14)
+        rectify(15, True)
         quantize_z(6)
-        interleave_out(0, 0)
+        decode(1, lo, s01, "g_row")
         quantize_z(7)
-        decode(1, 0, 1)
-        decode(1, 1, 0)
-        decode(1, 1, 1)
-        fetch_out(1, 0, 0)
-        quantize_out(0, 0)
-        interleave_out(0, 1)
-        fetch_out(1, 0, 1)
-        store_out(1, 0)
-        quantize_out(0, 1)
+        decode(1, lo, s23, "acc")
+        decode(1, q2, s03, "turn")
+        decode(1, q3, s03, "z_acc")
+        fetch_out(0, hi, s01)
+        fetch_out(0, hi, s23)
+        fetch_out(1, lo, s01)
+        fetch_out(1, lo, s23)
+        fetch_out(1, q2, s03)
+        interleave_out(0, lo)
+        interleave_out(0, hi)
+        quantize_out(0, lo)
+        quantize_out(0, hi)
         store_codes(0, whole)
-        store_scales(0)
-        interleave_out(1, 0)
-        fetch_out(1, 1, 0)
-        fetch_out(1, 1, 1)
-        store_out(1, 1)
-        interleave_out(1, 1)
-        quantize_out(1, 0)
-        quantize_out(1, 1)
-        store_codes(1, whole)
-        store_scales(1)
+        fetch_out(1, q3, s03)
+        interleave_out(1, lo)
+        interleave_out(1, q2)
+        quantize_out(1, lo)
+        store_codes(1, lo)
+        interleave_out(1, q3)
+        quantize_out(1, q2)
+        quantize_out(1, q3)
+        store_codes(1, hi)
+        store_scales()

@@ -1,4 +1,5 @@
 from contextlib import ExitStack
+from functools import partial
 
 import concourse.mybir as mybir
 from concourse.masks import make_identity
@@ -18,11 +19,28 @@ ACT = mybir.ActivationFunctionType
 P = 128
 PACK = 4
 K_PASS = P * PACK
-GROUPS = 2
-TILES = GROUPS * PACK
-HALF = D // 2
+PASSES = 2
+TILES = PASSES * PACK
+QUADRANTS = 4
 EPS = 1e-12
-BANKS = {"g_row": 1, "turn": 2, "acc": 2, "z_acc": 3}
+
+BANKS = {"g_bank": 1, "turn_bank": 2, "a_bank": 2, "z_bank": 3}
+
+MAX_LEAD = 3
+DIC_LAG = 3
+
+ALL_D = slice(0, D)
+LO, HI = slice(0, D // 2), slice(D // 2, D)
+HI_FIRST, HI_LAST = slice(D // 2, D // 2 + P), slice(D // 2 + P, D)
+FRONT, BACK, ALL_T = slice(0, 2), slice(2, PACK), slice(0, PACK)
+
+
+def width(cols):
+    return cols.stop - cols.start
+
+
+def block(index, size):
+    return slice(index * size, (index + 1) * size)
 
 
 def tile_relaxedarchetypalreluautoencoder_x2_kernel(
@@ -32,7 +50,7 @@ def tile_relaxedarchetypalreluautoencoder_x2_kernel(
     with ExitStack() as ctx:
         keep = ctx.enter_context(tc.tile_pool(name="keep", bufs=1))
         work = ctx.enter_context(tc.tile_pool(name="work", bufs=2))
-        psum = ctx.enter_context(tc.psum_pool(name="psum", bufs=2))
+        psum = ctx.enter_context(tc.psum_pool(name="psum", bufs=1))
         ctx.enter_context(tc.manual_schedule())
 
         def kept(name, shape, dtype):
@@ -41,71 +59,80 @@ def tile_relaxedarchetypalreluautoencoder_x2_kernel(
         def kept_list(name, count, shape, dtype):
             return [kept("%s%d" % (name, i), shape, dtype) for i in range(count)]
 
+        def bank_tile(shape, tag):
+            return psum.tile(shape, F32, name=tag, bufs=BANKS[tag])
+
         ident = kept("ident", [P, P], F32)
-        minus_half = kept("minus_half", [P, 2], F32)
-        warm = kept("warm", [P, 1], F32)
-        logit_t = kept_list("logit", TILES, [P, N], BF16)
-        lam_t = kept_list("lam", TILES // 2, [P, 2, D], BF16)
-        x_t = kept_list("x", GROUPS, [P, PACK, D], BF16)
-        g_col = kept("g_col", [P, GROUPS, PACK], BF16)
-        s_col = kept("s_col", [P, GROUPS, PACK], BF16)
-        we_raw = kept("we_raw", [P, F], U32)
-        we_raw_sc = kept("we_raw_sc", [P, F], U8)
+        minus_half = kept("minus_half", [P, MAX_LEAD], F32)
+        warm_in = kept("warm_in", [P, 1], F32)
+        warm_out = kept("warm_out", [P, 1], F32)
+        logit_sb = kept_list("logit", TILES, [P, N], BF16)
+        lam_sb = kept_list("lam", TILES // 2, [P, 2, D], BF16)
+        x_sb = kept_list("x", PASSES, [P, PACK, D], BF16)
+        g_sb = kept("g_sb", [P, PASSES, PACK], BF16)
+        s_sb = kept("s_sb", [P, PASSES, PACK], BF16)
+        s_f32 = kept("s_f32", [P, PASSES, PACK], F32)
+        we_raw_sc = work.tile([P, F], U8, name="we_raw_sc", tag="staging")
+        we_raw = work.tile([P, F], U32, name="we_raw", tag="staging")
         we_q = kept("we_q", [P, F], U32)
         we_sc = kept("we_sc", [P, F], U8)
-        c_q = kept("c_q", [P, GROUPS * D], U32)
-        c_sc = kept("c_sc", [P, GROUPS * D], U8)
-        x_q = kept_list("x_q", GROUPS, [P, K_PASS], U32)
-        x_sc = kept_list("x_sc", GROUPS, [P, K_PASS], U8)
-        z_q = kept_list("z_q", TILES, [P, GROUPS * P], U32)
-        z_sc = kept_list("z_sc", TILES, [P, GROUPS * P], U8)
-        dic_rows = kept_list("dic_rows", GROUPS, [P, PACK, D], BF16)
-        dic_q = kept_list("dic_q", GROUPS, [P, D], U32)
-        dic_sc = kept_list("dic_sc", GROUPS, [P, D], U8)
-        out_q = kept_list("out_q", GROUPS, [P, D], U32)
-        out_sc = kept("out_sc", [P, GROUPS, D], U8)
+        c_q = kept("c_q", [P, PASSES * D], U32)
+        c_sc = kept("c_sc", [P, PASSES * D], U8)
+        x_q = kept_list("x_q", PASSES, [P, K_PASS], U32)
+        x_sc = kept_list("x_sc", PASSES, [P, K_PASS], U8)
+        z_q = kept_list("z_q", TILES, [P, PASSES * P], U32)
+        z_sc = kept_list("z_sc", TILES, [P, PASSES * P], U8)
+        dic_rows = kept_list("dic_rows", PASSES, [P, PACK, D], BF16)
+        dic_q = kept_list("dic_q", PASSES, [P, D], U32)
+        dic_sc = kept_list("dic_sc", PASSES, [P, D], U8)
+        out_q = kept_list("out_q", PASSES, [P, D], U32)
+        out_sc = kept("out_sc", [P, PASSES, D], U8)
         neg_max = kept_list("neg_max", TILES, [P, 1], F32)
         exp_sum = kept_list("exp_sum", TILES, [P, 1], F32)
         inv_sum = kept_list("inv_sum", TILES, [P, 1], F32)
-        sq_sum = kept_list("sq_sum", TILES // 2, [P, 2], F32)
-        lam_gain = kept_list("lam_gain", TILES // 2, [P, 2], F32)
+        sq_sum = kept("sq_sum", [P, TILES], F32)
+        sq_bounded = kept("sq_bounded", [P, TILES], F32)
+        shrink = kept("shrink", [P, TILES], F32)
         live = {}
 
+
+        def pass_rows(matrix, grp):
+            return matrix[block(grp, K_PASS), :].rearrange("(p t) n -> p t n", t=PACK)
+
+        def load_vector(tile, vector):
+            nc.sync.dma_start(out=tile[:], in_=vector.rearrange("(g p t) -> p g t", g=PASSES, t=PACK))
+
         def load_logits(j):
-            grp, t = divmod(j, PACK)
-            rows = logits[grp * K_PASS:(grp + 1) * K_PASS, :].rearrange("(p t) n -> p t n", t=PACK)
-            nc.sync.dma_start(out=logit_t[j][:], in_=rows[:, t, :])
+            nc.sync.dma_start(out=logit_sb[j][:], in_=pass_rows(logits, j // PACK)[:, j % PACK, :])
 
         def load_lam(pair):
-            grp, h = divmod(pair, 2)
-            rows = lam[grp * K_PASS:(grp + 1) * K_PASS, :].rearrange("(p t) d -> p t d", t=PACK)
-            nc.sync.dma_start(out=lam_t[pair][:], in_=rows[:, 2 * h:2 * h + 2, :])
+            nc.sync.dma_start(out=lam_sb[pair][:], in_=pass_rows(lam, pair // 2)[:, block(pair % 2, 2), :])
 
         def load_x(grp):
-            rows = x[grp * K_PASS:(grp + 1) * K_PASS, :].rearrange("(p t) d -> p t d", t=PACK)
-            nc.sync.dma_start(out=x_t[grp][:], in_=rows)
+            nc.sync.dma_start(out=x_sb[grp][:], in_=pass_rows(x, grp))
 
-        def load_we():
+        def load_we_codes():
             words = we_words[0].rearrange("p n t -> p (n t)").bitcast(I32)
             nc.sync.dma_start(out=we_raw[:].bitcast(I32), in_=words)
 
         def load_we_scales():
-            for q in range(4):
-                nc.gpsimd.dma_start(
+            for q in range(QUADRANTS):
+                nc.sync.dma_start(
                     out=we_raw_sc[32 * q:32 * q + 4, :].bitcast(I32),
-                    in_=we_scales[0, 4 * q:4 * q + 4, :].bitcast(I32),
+                    in_=we_scales[0, block(q, 4), :].bitcast(I32),
                 )
 
-        def load_c():
+        def load_c_codes():
             words = c_words.rearrange("g p d t -> p g (d t)").bitcast(I32)
-            nc.sync.dma_start(out=c_q[:].bitcast(I32).rearrange("p (g d) -> p g d", g=GROUPS), in_=words)
+            nc.sync.dma_start(out=c_q[:].bitcast(I32).rearrange("p (g d) -> p g d", g=PASSES), in_=words)
 
         def load_c_scales():
-            for q in range(4):
-                nc.gpsimd.dma_start(
-                    out=c_sc[32 * q:32 * q + 4, :].bitcast(I32).rearrange("r (g d) -> r g d", g=GROUPS),
-                    in_=c_scales[:, 4 * q:4 * q + 4, :].bitcast(I32).rearrange("g r d -> r g d"),
+            for q in range(QUADRANTS):
+                nc.sync.dma_start(
+                    out=c_sc[32 * q:32 * q + 4, :].bitcast(I32).rearrange("r (g d) -> r g d", g=PASSES),
+                    in_=c_scales[:, block(q, 4), :].bitcast(I32).rearrange("g r d -> r g d"),
                 )
+
 
         def quantize(codes, scales, values):
             nc.vector.quantize_mx(out=codes.bitcast(FP8X4), scales=scales, in_=values)
@@ -122,28 +149,22 @@ def tile_relaxedarchetypalreluautoencoder_x2_kernel(
                 in_=src.rearrange("p t (c i) -> p c t i", i=4),
             )
 
-        def spread_g():
-            live["g"] = bank = psum.tile([P, 2, GROUPS, P], F32, name="g_row", bufs=1)
-            words = g_col[:].bitcast(F32)
-            for u in range(2):
-                for ng in range(GROUPS):
-                    nc.tensor.transpose(bank[:, u, ng, :], words[:, ng, u:u + 1].to_broadcast([P, P]), ident[:])
 
         def sort_we_codes():
             nc.vector.tensor_copy(
-                out=we_q[:].bitcast(I32).rearrange("p (g t c i) -> p g c t i", g=GROUPS, t=PACK, i=4),
-                in_=we_raw[:].bitcast(I32).rearrange("p (g c i t) -> p g c t i", g=GROUPS, t=PACK, i=4),
+                out=we_q[:].bitcast(I32).rearrange("p (g t c i) -> p g c t i", g=PASSES, t=PACK, i=4),
+                in_=we_raw[:].bitcast(I32).rearrange("p (g c i t) -> p g c t i", g=PASSES, t=PACK, i=4),
             )
 
         def sort_we_scales():
             nc.vector.tensor_copy(
-                out=we_sc[:].rearrange("p (g t m) -> p g t m", g=GROUPS, t=PACK),
-                in_=we_raw_sc[:].rearrange("p (g m t) -> p g t m", g=GROUPS, t=PACK),
+                out=we_sc[:].rearrange("p (g t m) -> p g t m", g=PASSES, t=PACK),
+                in_=we_raw_sc[:].rearrange("p (g m t) -> p g t m", g=PASSES, t=PACK),
             )
 
         def turn_x(grp, pair):
-            words = x_t[grp][:].bitcast(F32)
-            live["x_bank", grp, pair] = bank = psum.tile([P, 2, 2, P], F32, name="z_acc", bufs=3)
+            words = x_sb[grp][:].bitcast(F32)
+            live["x_bank", grp, pair] = bank = bank_tile([P, 2, 2, P], "z_bank")
             for a in range(2):
                 for u in range(2):
                     nc.tensor.transpose(bank[:, a, u, :], words[:, 2 * pair + a, u:D // 2:2], ident[:])
@@ -152,49 +173,59 @@ def tile_relaxedarchetypalreluautoencoder_x2_kernel(
             if pair == 0:
                 live["xT", grp] = work.tile([P, PACK, P, PACK], BF16, name="xT", align_bytes=64)
             nc.scalar.copy(
-                out=live["xT", grp][:, 2 * pair:2 * pair + 2, :, :].bitcast(F32),
+                out=live["xT", grp][:, block(pair, 2), :, :].bitcast(F32),
                 in_=live["x_bank", grp, pair][:].rearrange("p a u m -> p a m u"),
             )
 
         def quantize_x(grp):
             quantize(x_q[grp][:], x_sc[grp][:], live["xT", grp][:].rearrange("p a m t -> p (a m t)"))
 
-        def encode(n, tag="z_acc"):
-            i, fg = divmod(n, GROUPS)
-            grp, slot = divmod(i, PACK)
-            cols = slice(slot * P, (slot + 1) * P)
-            live["z_bank", n] = bank = psum.tile([P, PACK, P], F32, name=tag, bufs=BANKS[tag])
+        def encode(n, tag="z_bank"):
+            i, atom_pass = divmod(n, PASSES)
+            rows = block(i % PACK, P)
+            live["z_sums", n] = bank = bank_tile([P, PACK, P], tag)
             for t in range(PACK):
-                wcols = slice((fg * PACK + t) * P, (fg * PACK + t + 1) * P)
-                mx_pass(bank[:, t, :], we_q[:, wcols], we_sc[:, wcols],
-                        x_q[grp][:, cols], x_sc[grp][:, cols], True, True)
+                atoms = block(atom_pass * PACK + t, P)
+                mx_pass(bank[:, t, :], we_q[:, atoms], we_sc[:, atoms],
+                        x_q[i // PACK][:, rows], x_sc[i // PACK][:, rows], True, True)
 
-        def rectify(n, on_vector=False):
-            i, fg = divmod(n, GROUPS)
-            if fg == 0:
-                live["z", i] = work.tile([P, GROUPS, P, PACK], BF16, name="zT", align_bytes=64, bufs=4)
-            src = live["z_bank", n][:].rearrange("p t m -> p m t")
-            if on_vector:
-                nc.vector.tensor_scalar(out=live["z", i][:, fg, :, :], in0=src, scalar1=0.0, scalar2=None,
-                                        op0=ALU.max)
-            else:
-                nc.scalar.activation(out=live["z", i][:, fg, :, :], in_=src, func=ACT.Relu)
+        def rectified_part(n):
+            i, atom_pass = divmod(n, PASSES)
+            if atom_pass == 0:
+                live["zT", i] = work.tile([P, PASSES, P, PACK], BF16, name="zT", align_bytes=64, bufs=4)
+            return live["zT", i][:, atom_pass, :, :], live["z_sums", n][:].rearrange("p t m -> p m t")
+
+        def rectify(n):
+            dst, sums = rectified_part(n)
+            nc.scalar.activation(out=dst, in_=sums, func=ACT.Relu)
+
+        def rectify_on_vector(n):
+            dst, sums = rectified_part(n)
+            nc.vector.tensor_scalar(out=dst, in0=sums, scalar1=0.0, scalar2=None, op0=ALU.max)
 
         def quantize_z(i):
-            quantize(z_q[i][:], z_sc[i][:], live["z", i][:].rearrange("p g m t -> p (g m t)"))
+            quantize(z_q[i][:], z_sc[i][:], live["zT", i][:].rearrange("p g m t -> p (g m t)"))
+
+
+        def spread_g():
+            live["g"] = bank = bank_tile([P, 2, PASSES, P], "g_bank")
+            words = g_sb[:].bitcast(F32)
+            for u in range(2):
+                for grp in range(PASSES):
+                    nc.tensor.transpose(bank[:, u, grp, :], words[:, grp, u:u + 1].to_broadcast([P, P]), ident[:])
 
         def row_max(j):
-            live["neg", j] = neg = work.tile([P, N], BF16, name="neg", bufs=4)
+            live["neg", j] = neg = work.tile([P, N], BF16, name="neg", bufs=MAX_LEAD + 1)
             nc.vector.tensor_scalar(
-                out=neg[:], in0=logit_t[j][:], scalar1=-1.0, scalar2=None,
+                out=neg[:], in0=logit_sb[j][:], scalar1=-1.0, scalar2=None,
                 op0=ALU.mult, op1=ALU.min, accum_out=neg_max[j][:],
             )
 
         def exponentials(j):
-            live["exp", j] = e = work.tile([P, N], F32, name="e", bufs=3)
+            live["exps", j] = exps = work.tile([P, N], F32, name="exps", bufs=3)
             nc.scalar.activation(
-                out=e[:].rearrange("p (u w h) -> p u w h", u=2, h=2),
-                in_=live["neg", j][:].rearrange("p (w u h) -> p u w h", u=2, h=2),
+                out=exps[:].rearrange("p (u w e) -> p u w e", u=2, e=2),
+                in_=live["neg", j][:].rearrange("p (w u e) -> p u w e", u=2, e=2),
                 func=ACT.Exp, scale=-1.0, bias=neg_max[j][:], accum_out=exp_sum[j][:],
             )
 
@@ -204,102 +235,97 @@ def tile_relaxedarchetypalreluautoencoder_x2_kernel(
         def weights(j):
             live["pg", j] = pg = work.tile([P, N], BF16, name="pg")
             nc.vector.scalar_tensor_tensor(
-                out=pg[:], in0=live["exp", j][:], scalar=inv_sum[j][:], in1=live["g"][:].rearrange("p u g n -> p (u g n)").bitcast(BF16),
+                out=pg[:], in0=live["exps", j][:], scalar=inv_sum[j][:],
+                in1=live["g"][:].rearrange("p u g n -> p (u g n)").bitcast(BF16),
                 op0=ALU.mult, op1=ALU.mult,
             )
 
         def turn_weights(j):
-            live["pg_bank", j] = bank = psum.tile([P, PACK, P], F32, name="turn")
+            live["pg_bank", j] = bank = bank_tile([P, PACK, P], "turn_bank")
             words = live["pg", j][:].bitcast(F32)
-            for w in range(PACK):
-                nc.tensor.transpose(bank[:, w, :], words[:, w * P:(w + 1) * P], ident[:])
+            for run in range(PACK):
+                nc.tensor.transpose(bank[:, run, :], words[:, block(run, P)], ident[:])
 
         def fetch_weights(j):
-            live["pgT", j] = pgT = work.tile([P, GROUPS, P, PACK], BF16, name="pgT", align_bytes=64)
+            live["pgT", j] = pgT = work.tile([P, PASSES, P, PACK], BF16, name="pgT", align_bytes=64)
             nc.scalar.copy(
                 out=pgT[:].bitcast(F32),
                 in_=live["pg_bank", j][:].rearrange("p (u g) f -> p g f u", u=2),
             )
 
         def quantize_weights(j):
-            live["pg_q", j] = codes = work.tile([P, GROUPS * P], U32, name="pg_q", align_bytes=64)
-            live["pg_sc", j] = scales = work.tile([P, GROUPS * P], U8, name="pg_sc", align_bytes=64)
+            live["pg_q", j] = codes = work.tile([P, PASSES * P], U32, name="pg_q", align_bytes=64)
+            live["pg_sc", j] = scales = work.tile([P, PASSES * P], U8, name="pg_sc", align_bytes=64)
             quantize(codes[:], scales[:], live["pgT", j][:].rearrange("p g f t -> p (g f t)"))
 
-        def archetypes(j, parts=1):
-            live["a", j] = acc = psum.tile([P, D], F32, name="acc")
-            width = D // parts
-            for part in range(parts):
-                for ng in range(GROUPS):
-                    fcols = slice(ng * P, (ng + 1) * P)
-                    dcols = slice(ng * D + part * width, ng * D + (part + 1) * width)
-                    mx_pass(acc[:, part * width:(part + 1) * width], live["pg_q", j][:, fcols], live["pg_sc", j][:, fcols],
-                            c_q[:, dcols], c_sc[:, dcols], ng == 0, ng == GROUPS - 1)
+        def archetypes(j, parts=(ALL_D,)):
+            live["a", j] = acc = bank_tile([P, D], "a_bank")
+            for cols in parts:
+                for grp in range(PASSES):
+                    atoms = block(grp, P)
+                    c_cols = slice(grp * D + cols.start, grp * D + cols.stop)
+                    mx_pass(acc[:, cols], live["pg_q", j][:, atoms], live["pg_sc", j][:, atoms],
+                            c_q[:, c_cols], c_sc[:, c_cols], grp == 0, grp == PASSES - 1)
+
 
         def lam_rows(j):
-            return lam_t[j // 2][:, j % 2, :]
+            return lam_sb[j // 2][:, j % 2, :]
 
         def gain(j):
-            return s_col[:, j // PACK, j % PACK:j % PACK + 1]
+            return s_f32[:, j // PACK, j % PACK:j % PACK + 1]
 
         def lam_norm(j):
             squares = work.tile([P, D], BF16, name="squares")
-            nc.scalar.activation(out=squares[:], in_=lam_rows(j), func=ACT.Square,
-                                 accum_out=sq_sum[j // 2][:, j % 2:j % 2 + 1])
+            nc.scalar.activation(out=squares[:], in_=lam_rows(j), func=ACT.Square, accum_out=sq_sum[:, j:j + 1])
 
-        def lam_factor(pair):
-            bounded = work.tile([P, 2], F32, name="bounded")
-            shrink = work.tile([P, 2], F32, name="shrink")
-            gains = s_col[:, pair // 2, 2 * (pair % 2):2 * (pair % 2) + 2]
-            nc.gpsimd.tensor_scalar(out=bounded[:], in0=sq_sum[pair][:], scalar1=EPS, scalar2=1.0,
+        def lam_bound(first, count):
+            cols = slice(first, first + count)
+            nc.gpsimd.tensor_scalar(out=sq_bounded[:, cols], in0=sq_sum[:, cols], scalar1=EPS, scalar2=1.0,
                                     op0=ALU.add, op1=ALU.max)
-            nc.gpsimd.tensor_tensor(out=shrink[:], in0=bounded[:], in1=minus_half[:], op=ALU.pow)
-            nc.gpsimd.tensor_tensor(out=lam_gain[pair][:], in0=shrink[:], in1=gains, op=ALU.mult)
+            nc.gpsimd.tensor_tensor(out=shrink[:, cols], in0=sq_bounded[:, cols], in1=minus_half[:, :count],
+                                    op=ALU.pow)
 
         def scale_lam(j, engine):
-            live["lam", j] = scaled = work.tile([P, D], F32, name="lam_scaled")
-            engine.tensor_scalar(out=scaled[:], in0=lam_rows(j),
-                                    scalar1=lam_gain[j // 2][:, j % 2:j % 2 + 1], scalar2=0.0,
-                                    op0=ALU.mult, op1=ALU.add)
+            live["lam", j] = scaled = work.tile([P, D], F32, name="lam_scaled", tag="staging")
+            engine.tensor_scalar(out=scaled[:], in0=lam_rows(j), scalar1=shrink[:, j:j + 1], scalar2=gain(j),
+                                 op0=ALU.mult, op1=ALU.mult)
 
-        def dictionary(j, cols):
+        def dictionary(j, cols=ALL_D):
             nc.vector.scalar_tensor_tensor(
                 out=dic_rows[j // PACK][:, j % PACK, cols], in0=live["a", j][:, cols], scalar=gain(j),
                 in1=live["lam", j][:, cols], op0=ALU.mult, op1=ALU.add,
             )
 
-        def interleave_dic(grp, half):
-            live["dicT", grp, half] = dicT = work.tile([P, HALF, PACK], BF16, name="dicT", align_bytes=64, bufs=4)
-            interleave(dicT[:], dic_rows[grp][:, :, half * HALF:(half + 1) * HALF])
+        def interleave_dic(grp, cols):
+            live["dicT", grp, cols.start] = dicT = work.tile(
+                [P, width(cols), PACK], BF16, name="dicT", align_bytes=64, bufs=2 * PASSES)
+            interleave(dicT[:], dic_rows[grp][:, :, cols])
 
-        def quantize_dic(grp, half):
-            cols = slice(half * HALF, (half + 1) * HALF)
+        def quantize_dic(grp, cols):
             quantize(dic_q[grp][:, cols], dic_sc[grp][:, cols],
-                     live["dicT", grp, half][:].rearrange("p d t -> p (d t)"))
+                     live["dicT", grp, cols.start][:].rearrange("p d t -> p (d t)"))
+
 
         def decode(grp, cols, slots, tag):
-            width = cols.stop - cols.start
-            count = slots.stop - slots.start
-            live["o_bank", grp, cols.start, slots.start] = bank = psum.tile([P, count, width], F32, name=tag, bufs=BANKS[tag])
-            for a in range(count):
-                i = grp * PACK + slots.start + a
-                for fg in range(GROUPS):
-                    bcols = slice(fg * P, (fg + 1) * P)
-                    mx_pass(bank[:, a, :], z_q[i][:, bcols], z_sc[i][:, bcols],
-                            dic_q[fg][:, cols], dic_sc[fg][:, cols], fg == 0, fg == GROUPS - 1)
+            live["out_sums", grp, cols.start, slots.start] = bank = bank_tile([P, width(slots), width(cols)], tag)
+            for t in range(slots.start, slots.stop):
+                i = grp * PACK + t
+                for atom_pass in range(PASSES):
+                    rows = block(atom_pass, P)
+                    mx_pass(bank[:, t - slots.start, :], z_q[i][:, rows], z_sc[i][:, rows],
+                            dic_q[atom_pass][:, cols], dic_sc[atom_pass][:, cols],
+                            atom_pass == 0, atom_pass == PASSES - 1)
 
         def fetch_out(grp, cols, slots):
             if slots.start == 0:
-                live["out", grp, cols.start] = work.tile([P, PACK, cols.stop - cols.start], F32, name="out", bufs=5)
-            nc.scalar.copy(out=live["out", grp, cols.start][:, slots, :], in_=live["o_bank", grp, cols.start, slots.start][:])
-            store_out(grp, cols, slots)
-
-        def store_out(grp, cols, slots):
-            rows = out_0[grp * K_PASS:(grp + 1) * K_PASS, :].rearrange("(p t) d -> p t d", t=PACK)
-            nc.sync.dma_start(out=rows[:, slots, cols], in_=live["out", grp, cols.start][:, slots, :])
+                live["out", grp, cols.start] = work.tile([P, PACK, width(cols)], F32, name="out_sb", bufs=5)
+            part = live["out", grp, cols.start][:, slots, :]
+            nc.scalar.copy(out=part, in_=live["out_sums", grp, cols.start, slots.start][:])
+            nc.sync.dma_start(out=pass_rows(out_0, grp)[:, slots, cols], in_=part)
 
         def interleave_out(grp, cols):
-            live["outT", grp, cols.start] = outT = work.tile([P, cols.stop - cols.start, PACK], BF16, name="outT", align_bytes=64, bufs=3)
+            live["outT", grp, cols.start] = outT = work.tile(
+                [P, width(cols), PACK], BF16, name="outT", align_bytes=64, bufs=3)
             interleave(outT[:], live["out", grp, cols.start][:])
 
         def quantize_out(grp, cols):
@@ -311,182 +337,169 @@ def tile_relaxedarchetypalreluautoencoder_x2_kernel(
             nc.sync.dma_start(out=words[:, cols], in_=out_q[grp][:, cols].bitcast(I32))
 
         def store_scales():
-            for q in range(4):
-                (nc.sync, nc.scalar)[q % 2].dma_start(
-                    out=out_2[:, 4 * q:4 * q + 4, :].bitcast(I32).rearrange("g r d -> r g d"),
+            for q in range(QUADRANTS):
+                queue = nc.scalar if q % 2 else nc.sync
+                queue.dma_start(
+                    out=out_2[:, block(q, 4), :].bitcast(I32).rearrange("g r d -> r g d"),
                     in_=out_sc[32 * q:32 * q + 4, :, :].bitcast(I32),
                 )
 
-        nc.vector.memset(warm[:], 0.0)
+
+        nc.vector.memset(warm_in[:], 0.0)
         nc.vector.memset(we_raw_sc[:].bitcast(I32), 0)
         nc.vector.memset(c_sc[:].bitcast(I32), 0)
         make_identity(nc, ident[:])
         nc.gpsimd.memset(minus_half[:], -0.5)
-        warm_out = kept("warm_out", [P, 1], F32)
-        nc.scalar.activation(out=warm_out[:], in_=warm[:], func=ACT.Exp)
+        nc.scalar.activation(out=warm_out[:], in_=warm_in[:], func=ACT.Exp)
 
         load_logits(0)
-        nc.sync.dma_start(out=g_col[:], in_=g.rearrange("(g p t) -> p g t", g=GROUPS, t=PACK))
+        load_vector(g_sb, g)
         load_logits(1)
         load_logits(2)
         load_logits(3)
         load_lam(0)
-        nc.sync.dma_start(out=s_col[:], in_=s.rearrange("(g p t) -> p g t", g=GROUPS, t=PACK))
+        load_vector(s_sb, s)
         load_lam(1)
         load_logits(4)
         load_x(0)
+        load_we_scales()
         load_logits(5)
-        load_c()
-        load_we()
+        load_c_codes()
+        load_c_scales()
+        load_we_codes()
         load_logits(6)
         load_lam(2)
         load_logits(7)
         load_lam(3)
         load_x(1)
-        load_we_scales()
-        load_c_scales()
 
-        whole = slice(0, D)
-        halves = [slice(0, HALF), slice(HALF, D)]
-        for j in range(3):
-            row_max(j)
-        spread_g()
-        exponentials(0)
-        LAM = {0: 0, 1: 1, 3: 2, 4: 3}
-        for j in range(TILES):
+        def run(jobs):
+            for job in jobs:
+                job()
+
+        def step(j, scalar_first=(), scalar_last=(), gpsimd=(), tensor_first=(), tensor_middle=(),
+                 tensor_last=(), vector_last=()):
             invert_sum(j)
-            if j >= 3:
-                dictionary(j - 3, whole)
-                scale_lam(j - 1, nc.gpsimd)
-            if j - 1 in LAM:
-                lam_factor(LAM[j - 1])
-            if j in (1, 2):
-                scale_lam(j - 1, nc.gpsimd)
-            if j + 3 < TILES:
-                row_max(j + 3)
-            if j in (0, 5, 6):
+            if j >= DIC_LAG:
+                dictionary(j - DIC_LAG)
+            if j + MAX_LEAD < TILES:
+                row_max(j + MAX_LEAD)
+            exps_first = j == 0 or not scalar_first
+            if exps_first and j + 1 < TILES:
                 exponentials(j + 1)
-            if j in LAM:
-                lam_norm(2 * LAM[j])
-            if j == 2:
-                fetch_x(0, 0)
+            run(scalar_first)
+            run(gpsimd)
             if j >= 1:
                 fetch_weights(j - 1)
-            if 1 <= j <= 4:
+            if not exps_first:
                 exponentials(j + 1)
-            if j in LAM:
-                lam_norm(2 * LAM[j] + 1)
-            if j == 2:
-                fetch_x(0, 1)
-            if j == 1:
-                turn_x(0, 0)
-                turn_x(0, 1)
-            if j == 4:
-                encode(0)
-                encode(1)
-                encode(2)
-            if j == 5:
-                rectify(0)
-            if j == 6:
-                rectify(1)
-                rectify(2)
-                fetch_x(1, 0)
-            if j == 7:
-                rectify(3)
-                fetch_x(1, 1)
+            run(scalar_last)
+            run(tensor_first)
             weights(j)
             turn_weights(j)
-            if j == 6:
-                encode(3)
+            run(tensor_middle)
             if j >= 1:
                 quantize_weights(j - 1)
                 archetypes(j - 1)
-            if j in (5, 6):
-                turn_x(1, j - 5)
-            if j == 2:
-                sort_we_codes()
-            if j == 3:
-                quantize_x(0)
-            if j == 1:
-                sort_we_scales()
-        lo, hi, q2, q3 = halves[0], halves[1], slice(HALF, HALF + P), slice(HALF + P, D)
-        s01, s23, s03 = slice(0, 2), slice(2, 4), slice(0, 4)
-        encode(4)
-        encode(5)
-        encode(6)
-        encode(7, "turn")
-        fetch_weights(7)
-        dictionary(5, whole)
+            run(tensor_last)
+            run(vector_last)
+
+        norm = [partial(lam_norm, j) for j in range(TILES)]
+        scale = [partial(scale_lam, j, nc.gpsimd) for j in range(TILES)]
+        sums = [partial(encode, n) for n in range(PACK)]
+        relu = [partial(rectify, n) for n in range(PACK)]
+
+        for j in range(MAX_LEAD):
+            row_max(j)
+        spread_g()
+        nc.gpsimd.tensor_copy(out=s_f32[:], in_=s_sb[:])
+        exponentials(0)
+
+        step(0, scalar_first=norm[0:1], scalar_last=norm[1:2])
+        step(1, scalar_first=norm[2:3], scalar_last=norm[3:4], gpsimd=[partial(lam_bound, 0, 3)],
+             tensor_first=[partial(turn_x, 0, 0), partial(turn_x, 0, 1)], vector_last=[sort_we_scales])
+        step(2, scalar_first=[partial(fetch_x, 0, 0)], scalar_last=[partial(fetch_x, 0, 1)], gpsimd=scale[0:1],
+             vector_last=[sort_we_codes])
+        step(3, scalar_first=norm[4:5], scalar_last=norm[5:6], gpsimd=scale[1:3],
+             vector_last=[partial(quantize_x, 0)])
+        step(4, scalar_first=norm[6:7], scalar_last=norm[7:8], gpsimd=[partial(lam_bound, 3, 3), scale[3]],
+             tensor_first=sums[0:3])
+        step(5, scalar_last=relu[0:1], gpsimd=[partial(lam_bound, 6, 2), scale[4]],
+             tensor_last=[partial(turn_x, 1, 0)])
+        step(6, scalar_last=relu[1:3] + [partial(fetch_x, 1, 0)], gpsimd=scale[5:6],
+             tensor_middle=sums[3:4], tensor_last=[partial(turn_x, 1, 1)])
+        step(7, scalar_last=relu[3:4] + [partial(fetch_x, 1, 1)], gpsimd=scale[6:7])
+
+        last = TILES - 1
+        z_ring = ["z_bank"] * BANKS["z_bank"] + ["turn_bank"] * BANKS["turn_bank"]
+        first_late, parts = PACK, PASSES * TILES
+
+        def encode_late(n):
+            encode(n, z_ring[(n - first_late) % len(z_ring)])
+
+        for n in range(first_late, first_late + len(z_ring) - 1):
+            encode_late(n)
+        fetch_weights(last)
+        dictionary(last - 2)
         quantize_z(0)
-        scale_lam(7, nc.vector)
+        scale_lam(last, nc.vector)
         quantize_x(1)
-        quantize_weights(7)
-        archetypes(7, 2)
-        encode(8, "turn")
-        rectify(4)
-        encode(9)
-        rectify(5)
-        encode(10)
-        dictionary(6, whole)
-        quantize_z(1)
-        interleave_dic(0, 0)
-        dictionary(7, lo)
-        dictionary(7, hi)
-        rectify(6)
-        encode(11)
-        rectify(7)
-        encode(12, "turn")
-        quantize_z(2)
-        interleave_dic(1, 0)
-        quantize_dic(0, 0)
-        quantize_dic(1, 0)
-        quantize_z(3)
-        rectify(8)
-        encode(13, "turn")
-        rectify(9)
-        encode(14)
-        rectify(10)
-        encode(15)
-        decode(0, lo, s01, "g_row")
-        decode(0, lo, s23, "acc")
-        interleave_dic(0, 1)
-        interleave_dic(1, 1)
-        quantize_dic(0, 1)
-        quantize_dic(1, 1)
-        rectify(11)
-        rectify(12)
-        rectify(13)
-        decode(0, hi, s01, "acc")
-        decode(0, hi, s23, "turn")
-        fetch_out(0, lo, s01)
-        fetch_out(0, lo, s23)
+        quantize_weights(last)
+        archetypes(last, (LO, HI))
+        encode_late(first_late + len(z_ring) - 1)
+        for n in range(first_late, parts - 2):
+            rectify(n)
+            if n + len(z_ring) < parts:
+                encode_late(n + len(z_ring))
+            if n == 2 * PACK - 1:
+                dictionary(last - 1)
+                quantize_z(1)
+                interleave_dic(0, LO)
+                dictionary(last, LO)
+                dictionary(last, HI)
+                quantize_z(2)
+                interleave_dic(1, LO)
+                quantize_dic(0, LO)
+                quantize_dic(1, LO)
+                quantize_z(3)
+
+        decode(0, LO, FRONT, "g_bank")
+        decode(0, LO, BACK, "a_bank")
+        for grp in range(PASSES):
+            interleave_dic(grp, HI)
+        for grp in range(PASSES):
+            quantize_dic(grp, HI)
+        decode(0, HI, FRONT, "a_bank")
+        decode(0, HI, BACK, "turn_bank")
+        fetch_out(0, LO, FRONT)
+        fetch_out(0, LO, BACK)
         quantize_z(4)
         quantize_z(5)
-        rectify(14)
-        rectify(15, True)
+        rectify(parts - 2)
+        rectify_on_vector(parts - 1)
         quantize_z(6)
-        decode(1, lo, s01, "g_row")
         quantize_z(7)
-        decode(1, lo, s23, "acc")
-        decode(1, q2, s03, "turn")
-        decode(1, q3, s03, "z_acc")
-        fetch_out(0, hi, s01)
-        fetch_out(0, hi, s23)
-        fetch_out(1, lo, s01)
-        fetch_out(1, lo, s23)
-        fetch_out(1, q2, s03)
-        interleave_out(0, lo)
-        interleave_out(0, hi)
-        quantize_out(0, lo)
-        quantize_out(0, hi)
-        store_codes(0, whole)
-        fetch_out(1, q3, s03)
-        interleave_out(1, lo)
-        interleave_out(1, q2)
-        quantize_out(1, lo)
-        store_codes(1, lo)
-        interleave_out(1, q3)
-        quantize_out(1, q2)
-        quantize_out(1, q3)
-        store_codes(1, hi)
+        decode(1, LO, FRONT, "g_bank")
+        decode(1, LO, BACK, "a_bank")
+        decode(1, HI_FIRST, ALL_T, "turn_bank")
+        decode(1, HI_LAST, ALL_T, "z_bank")
+        fetch_out(0, HI, FRONT)
+        fetch_out(0, HI, BACK)
+        fetch_out(1, LO, FRONT)
+        fetch_out(1, LO, BACK)
+        fetch_out(1, HI_FIRST, ALL_T)
+        interleave_out(0, LO)
+        interleave_out(0, HI)
+        quantize_out(0, LO)
+        quantize_out(0, HI)
+        store_codes(0, ALL_D)
+        fetch_out(1, HI_LAST, ALL_T)
+        interleave_out(1, LO)
+        interleave_out(1, HI_FIRST)
+        quantize_out(1, LO)
+        store_codes(1, LO)
+        interleave_out(1, HI_LAST)
+        quantize_out(1, HI_FIRST)
+        quantize_out(1, HI_LAST)
+        store_codes(1, HI)
         store_scales()

@@ -32,7 +32,8 @@ DIC_LAG = 3
 ALL_D = slice(0, D)
 LO, HI = slice(0, D // 2), slice(D // 2, D)
 HI_FIRST, HI_LAST = slice(D // 2, D // 2 + P), slice(D // 2 + P, D)
-FRONT, BACK, ALL_T = slice(0, 2), slice(2, PACK), slice(0, PACK)
+FRONT = slice(0, 2)
+ONE = [slice(t, t + 1) for t in range(PACK)]
 
 
 def width(cols):
@@ -63,7 +64,7 @@ def tile_relaxedarchetypalreluautoencoder_x2_kernel(
             return psum.tile(shape, F32, name=tag, bufs=BANKS[tag])
 
         ident = kept("ident", [P, P], F32)
-        minus_half = kept("minus_half", [P, MAX_LEAD], F32)
+        minus_half = kept("minus_half", [P, 2], F32)
         warm_in = kept("warm_in", [P, 1], F32)
         warm_out = kept("warm_out", [P, 1], F32)
         logit_sb = kept_list("logit", TILES, [P, N], BF16)
@@ -85,6 +86,7 @@ def tile_relaxedarchetypalreluautoencoder_x2_kernel(
         dic_rows = kept_list("dic_rows", PASSES, [P, PACK, D], BF16)
         dic_q = kept_list("dic_q", PASSES, [P, D], U32)
         dic_sc = kept_list("dic_sc", PASSES, [P, D], U8)
+        out_sb = kept_list("out_sb", PASSES, [P, PACK, D], F32)
         out_q = kept_list("out_q", PASSES, [P, D], U32)
         out_sc = kept("out_sc", [P, PASSES, D], U8)
         neg_max = kept_list("neg_max", TILES, [P, 1], F32)
@@ -143,8 +145,8 @@ def tile_relaxedarchetypalreluautoencoder_x2_kernel(
                 rhs=rhs_q.bitcast(FP8X4), rhs_scale=rhs_sc, start=first, stop=last,
             )
 
-        def interleave(dst, src):
-            nc.vector.tensor_copy(
+        def interleave(dst, src, copy=nc.vector.tensor_copy):
+            copy(
                 out=dst.rearrange("p (c i) t -> p c t i", i=4),
                 in_=src.rearrange("p t (c i) -> p c t i", i=4),
             )
@@ -192,7 +194,7 @@ def tile_relaxedarchetypalreluautoencoder_x2_kernel(
         def rectified_part(n):
             i, atom_pass = divmod(n, PASSES)
             if atom_pass == 0:
-                live["zT", i] = work.tile([P, PASSES, P, PACK], BF16, name="zT", align_bytes=64, bufs=4)
+                live["zT", i] = work.tile([P, PASSES, P, PACK], BF16, name="zT", align_bytes=64, bufs=6)
             return live["zT", i][:, atom_pass, :, :], live["z_sums", n][:].rearrange("p t m -> p m t")
 
         def rectify(n):
@@ -274,16 +276,18 @@ def tile_relaxedarchetypalreluautoencoder_x2_kernel(
         def gain(j):
             return s_f32[:, j // PACK, j % PACK:j % PACK + 1]
 
+        def widen_gains():
+            nc.gpsimd.tensor_copy(out=s_f32[:], in_=s_sb[:])
+
         def lam_norm(j):
             squares = work.tile([P, D], BF16, name="squares")
             nc.scalar.activation(out=squares[:], in_=lam_rows(j), func=ACT.Square, accum_out=sq_sum[:, j:j + 1])
 
-        def lam_bound(first, count):
-            cols = slice(first, first + count)
+        def lam_bound(pair):
+            cols = block(pair, 2)
             nc.gpsimd.tensor_scalar(out=sq_bounded[:, cols], in0=sq_sum[:, cols], scalar1=EPS, scalar2=1.0,
                                     op0=ALU.add, op1=ALU.max)
-            nc.gpsimd.tensor_tensor(out=shrink[:, cols], in0=sq_bounded[:, cols], in1=minus_half[:, :count],
-                                    op=ALU.pow)
+            nc.gpsimd.tensor_tensor(out=shrink[:, cols], in0=sq_bounded[:, cols], in1=minus_half[:], op=ALU.pow)
 
         def scale_lam(j, engine):
             live["lam", j] = scaled = work.tile([P, D], F32, name="lam_scaled", tag="staging")
@@ -317,24 +321,22 @@ def tile_relaxedarchetypalreluautoencoder_x2_kernel(
                             atom_pass == 0, atom_pass == PASSES - 1)
 
         def fetch_out(grp, cols, slots):
-            if slots.start == 0:
-                live["out", grp, cols.start] = work.tile([P, PACK, width(cols)], F32, name="out_sb", bufs=5)
-            part = live["out", grp, cols.start][:, slots, :]
+            part = out_sb[grp][:, slots, cols]
             nc.scalar.copy(out=part, in_=live["out_sums", grp, cols.start, slots.start][:])
             nc.sync.dma_start(out=pass_rows(out_0, grp)[:, slots, cols], in_=part)
 
-        def interleave_out(grp, cols):
+        def interleave_out(grp, cols, copy=nc.vector.tensor_copy):
             live["outT", grp, cols.start] = outT = work.tile(
                 [P, width(cols), PACK], BF16, name="outT", align_bytes=64, bufs=3)
-            interleave(outT[:], live["out", grp, cols.start][:])
+            interleave(outT[:], out_sb[grp][:, :, cols], copy)
 
         def quantize_out(grp, cols):
             quantize(out_q[grp][:, cols], out_sc[:, grp, cols],
                      live["outT", grp, cols.start][:].rearrange("p d t -> p (d t)"))
 
-        def store_codes(grp, cols):
+        def store_codes(grp):
             words = out_1[grp].rearrange("p m t -> p (m t)").bitcast(I32)
-            nc.sync.dma_start(out=words[:, cols], in_=out_q[grp][:, cols].bitcast(I32))
+            nc.sync.dma_start(out=words, in_=out_q[grp][:].bitcast(I32))
 
         def store_scales():
             for q in range(QUADRANTS):
@@ -358,19 +360,19 @@ def tile_relaxedarchetypalreluautoencoder_x2_kernel(
         load_logits(2)
         load_logits(3)
         load_lam(0)
-        load_vector(s_sb, s)
-        load_lam(1)
-        load_logits(4)
-        load_x(0)
         load_we_scales()
+        load_logits(4)
+        load_lam(1)
+        load_x(0)
+        load_vector(s_sb, s)
         load_logits(5)
-        load_c_codes()
         load_c_scales()
+        load_c_codes()
         load_we_codes()
-        load_logits(6)
         load_lam(2)
-        load_logits(7)
+        load_logits(6)
         load_lam(3)
+        load_logits(7)
         load_x(1)
 
         def run(jobs):
@@ -406,29 +408,28 @@ def tile_relaxedarchetypalreluautoencoder_x2_kernel(
 
         norm = [partial(lam_norm, j) for j in range(TILES)]
         scale = [partial(scale_lam, j, nc.gpsimd) for j in range(TILES)]
-        sums = [partial(encode, n) for n in range(PACK)]
+        bound = [partial(lam_bound, pair) for pair in range(TILES // 2)]
+        sums = [partial(encode, n) for n in range(2 * BANKS["z_bank"])]
         relu = [partial(rectify, n) for n in range(PACK)]
 
         for j in range(MAX_LEAD):
             row_max(j)
         spread_g()
-        nc.gpsimd.tensor_copy(out=s_f32[:], in_=s_sb[:])
         exponentials(0)
 
         step(0, scalar_first=norm[0:1], scalar_last=norm[1:2])
-        step(1, scalar_first=norm[2:3], scalar_last=norm[3:4], gpsimd=[partial(lam_bound, 0, 3)],
+        step(1, scalar_first=norm[2:3], scalar_last=norm[3:4], gpsimd=[bound[0], widen_gains],
              tensor_first=[partial(turn_x, 0, 0), partial(turn_x, 0, 1)], vector_last=[sort_we_scales])
-        step(2, scalar_first=[partial(fetch_x, 0, 0)], scalar_last=[partial(fetch_x, 0, 1)], gpsimd=scale[0:1],
-             vector_last=[sort_we_codes])
+        step(2, scalar_first=[partial(fetch_x, 0, 0)], scalar_last=[partial(fetch_x, 0, 1)],
+             gpsimd=[scale[0], bound[1]], vector_last=[sort_we_codes])
         step(3, scalar_first=norm[4:5], scalar_last=norm[5:6], gpsimd=scale[1:3],
              vector_last=[partial(quantize_x, 0)])
-        step(4, scalar_first=norm[6:7], scalar_last=norm[7:8], gpsimd=[partial(lam_bound, 3, 3), scale[3]],
+        step(4, scalar_first=norm[6:7], scalar_last=norm[7:8], gpsimd=[bound[2], scale[3]],
              tensor_first=sums[0:3])
-        step(5, scalar_last=relu[0:1], gpsimd=[partial(lam_bound, 6, 2), scale[4]],
-             tensor_last=[partial(turn_x, 1, 0)])
-        step(6, scalar_last=relu[1:3] + [partial(fetch_x, 1, 0)], gpsimd=scale[5:6],
+        step(5, scalar_last=relu[0:1], gpsimd=scale[4:5], tensor_last=[partial(turn_x, 1, 0)])
+        step(6, scalar_last=relu[1:3] + [partial(fetch_x, 1, 0)], gpsimd=[bound[3], scale[5]],
              tensor_middle=sums[3:4], tensor_last=[partial(turn_x, 1, 1)])
-        step(7, scalar_last=relu[3:4] + [partial(fetch_x, 1, 1)], gpsimd=scale[6:7])
+        step(7, scalar_last=relu[3:4] + [partial(fetch_x, 1, 1)], gpsimd=scale[6:7], tensor_middle=sums[4:6])
 
         last = TILES - 1
         z_ring = ["z_bank"] * BANKS["z_bank"] + ["turn_bank"] * BANKS["turn_bank"]
@@ -437,7 +438,7 @@ def tile_relaxedarchetypalreluautoencoder_x2_kernel(
         def encode_late(n):
             encode(n, z_ring[(n - first_late) % len(z_ring)])
 
-        for n in range(first_late, first_late + len(z_ring) - 1):
+        for n in range(len(sums), first_late + len(z_ring) - 1):
             encode_late(n)
         fetch_weights(last)
         dictionary(last - 2)
@@ -453,53 +454,46 @@ def tile_relaxedarchetypalreluautoencoder_x2_kernel(
                 encode_late(n + len(z_ring))
             if n == 2 * PACK - 1:
                 dictionary(last - 1)
-                quantize_z(1)
                 interleave_dic(0, LO)
                 dictionary(last, LO)
                 dictionary(last, HI)
-                quantize_z(2)
+                quantize_z(1)
                 interleave_dic(1, LO)
                 quantize_dic(0, LO)
                 quantize_dic(1, LO)
-                quantize_z(3)
 
         decode(0, LO, FRONT, "g_bank")
-        decode(0, LO, BACK, "a_bank")
         for grp in range(PASSES):
             interleave_dic(grp, HI)
         for grp in range(PASSES):
             quantize_dic(grp, HI)
+        for i in range(2, PACK):
+            quantize_z(i)
         decode(0, HI, FRONT, "a_bank")
-        decode(0, HI, BACK, "turn_bank")
+        decode(0, ALL_D, ONE[2], "a_bank")
+        decode(0, ALL_D, ONE[3], "turn_bank")
         fetch_out(0, LO, FRONT)
-        fetch_out(0, LO, BACK)
-        quantize_z(4)
-        quantize_z(5)
         rectify(parts - 2)
         rectify_on_vector(parts - 1)
-        quantize_z(6)
-        quantize_z(7)
-        decode(1, LO, FRONT, "g_bank")
-        decode(1, LO, BACK, "a_bank")
-        decode(1, HI_FIRST, ALL_T, "turn_bank")
-        decode(1, HI_LAST, ALL_T, "z_bank")
+        for i in range(PACK, TILES):
+            quantize_z(i)
+        for t, tag in enumerate(("g_bank", "turn_bank", "z_bank", "z_bank")):
+            decode(1, ALL_D, ONE[t], tag)
         fetch_out(0, HI, FRONT)
-        fetch_out(0, HI, BACK)
-        fetch_out(1, LO, FRONT)
-        fetch_out(1, LO, BACK)
-        fetch_out(1, HI_FIRST, ALL_T)
+        fetch_out(0, ALL_D, ONE[2])
+        fetch_out(0, ALL_D, ONE[3])
+        for t in range(PACK):
+            fetch_out(1, ALL_D, ONE[t])
         interleave_out(0, LO)
         interleave_out(0, HI)
         quantize_out(0, LO)
         quantize_out(0, HI)
-        store_codes(0, ALL_D)
-        fetch_out(1, HI_LAST, ALL_T)
+        store_codes(0)
         interleave_out(1, LO)
+        interleave_out(1, HI_LAST, nc.scalar.copy)
         interleave_out(1, HI_FIRST)
         quantize_out(1, LO)
-        store_codes(1, LO)
-        interleave_out(1, HI_LAST)
-        quantize_out(1, HI_FIRST)
         quantize_out(1, HI_LAST)
-        store_codes(1, HI)
+        quantize_out(1, HI_FIRST)
+        store_codes(1)
         store_scales()

@@ -22,6 +22,8 @@ K_PASS = P * PACK
 PASSES = 2
 TILES = PASSES * PACK
 QUADRANTS = 4
+SCALE_ROWS = 4
+RUN = 4
 EPS = 1e-12
 
 BANKS = {"g_bank": 1, "turn_bank": 2, "a_bank": 2, "z_bank": 3}
@@ -40,8 +42,13 @@ def width(cols):
     return cols.stop - cols.start
 
 
-def block(index, size):
+def span(index, size):
     return slice(index * size, (index + 1) * size)
+
+
+def scale_partitions(q):
+    first = q * (P // QUADRANTS)
+    return slice(first, first + SCALE_ROWS)
 
 
 def tile_relaxedarchetypalreluautoencoder_x2_kernel(
@@ -65,8 +72,6 @@ def tile_relaxedarchetypalreluautoencoder_x2_kernel(
 
         ident = kept("ident", [P, P], F32)
         minus_half = kept("minus_half", [P, 2], F32)
-        warm_in = kept("warm_in", [P, 1], F32)
-        warm_out = kept("warm_out", [P, 1], F32)
         logit_sb = kept_list("logit", TILES, [P, N], BF16)
         lam_sb = kept_list("lam", TILES // 2, [P, 2, D], BF16)
         x_sb = kept_list("x", PASSES, [P, PACK, D], BF16)
@@ -99,16 +104,16 @@ def tile_relaxedarchetypalreluautoencoder_x2_kernel(
 
 
         def pass_rows(matrix, grp):
-            return matrix[block(grp, K_PASS), :].rearrange("(p t) n -> p t n", t=PACK)
+            return matrix[span(grp, K_PASS), :].rearrange("(p t) n -> p t n", t=PACK)
 
         def load_vector(tile, vector):
-            nc.sync.dma_start(out=tile[:], in_=vector.rearrange("(g p t) -> p g t", g=PASSES, t=PACK))
+            nc.sync.dma_start(out=tile[:], in_=vector.rearrange("(grp p t) -> p grp t", grp=PASSES, t=PACK))
 
         def load_logits(j):
             nc.sync.dma_start(out=logit_sb[j][:], in_=pass_rows(logits, j // PACK)[:, j % PACK, :])
 
         def load_lam(pair):
-            nc.sync.dma_start(out=lam_sb[pair][:], in_=pass_rows(lam, pair // 2)[:, block(pair % 2, 2), :])
+            nc.sync.dma_start(out=lam_sb[pair][:], in_=pass_rows(lam, pair // 2)[:, span(pair % 2, 2), :])
 
         def load_x(grp):
             nc.sync.dma_start(out=x_sb[grp][:], in_=pass_rows(x, grp))
@@ -120,19 +125,19 @@ def tile_relaxedarchetypalreluautoencoder_x2_kernel(
         def load_we_scales():
             for q in range(QUADRANTS):
                 nc.sync.dma_start(
-                    out=we_raw_sc[32 * q:32 * q + 4, :].bitcast(I32),
-                    in_=we_scales[0, block(q, 4), :].bitcast(I32),
+                    out=we_raw_sc[scale_partitions(q), :].bitcast(I32),
+                    in_=we_scales[0, span(q, SCALE_ROWS), :].bitcast(I32),
                 )
 
         def load_c_codes():
-            words = c_words.rearrange("g p d t -> p g (d t)").bitcast(I32)
-            nc.sync.dma_start(out=c_q[:].bitcast(I32).rearrange("p (g d) -> p g d", g=PASSES), in_=words)
+            words = c_words.rearrange("grp p d t -> p grp (d t)").bitcast(I32)
+            nc.sync.dma_start(out=c_q[:].bitcast(I32).rearrange("p (grp d) -> p grp d", grp=PASSES), in_=words)
 
         def load_c_scales():
             for q in range(QUADRANTS):
                 nc.sync.dma_start(
-                    out=c_sc[32 * q:32 * q + 4, :].bitcast(I32).rearrange("r (g d) -> r g d", g=PASSES),
-                    in_=c_scales[:, block(q, 4), :].bitcast(I32).rearrange("g r d -> r g d"),
+                    out=c_sc[scale_partitions(q), :].bitcast(I32).rearrange("r (grp d) -> r grp d", grp=PASSES),
+                    in_=c_scales[:, span(q, SCALE_ROWS), :].bitcast(I32).rearrange("grp r d -> r grp d"),
                 )
 
 
@@ -147,36 +152,36 @@ def tile_relaxedarchetypalreluautoencoder_x2_kernel(
 
         def interleave(dst, src, copy=nc.vector.tensor_copy):
             copy(
-                out=dst.rearrange("p (c i) t -> p c t i", i=4),
-                in_=src.rearrange("p t (c i) -> p c t i", i=4),
+                out=dst.rearrange("p (c i) t -> p c t i", i=RUN),
+                in_=src.rearrange("p t (c i) -> p c t i", i=RUN),
             )
 
 
         def sort_we_codes():
             nc.vector.tensor_copy(
-                out=we_q[:].bitcast(I32).rearrange("p (g t c i) -> p g c t i", g=PASSES, t=PACK, i=4),
-                in_=we_raw[:].bitcast(I32).rearrange("p (g c i t) -> p g c t i", g=PASSES, t=PACK, i=4),
+                out=we_q[:].bitcast(I32).rearrange("p (grp t c i) -> p grp c t i", grp=PASSES, t=PACK, i=RUN),
+                in_=we_raw[:].bitcast(I32).rearrange("p (grp c i t) -> p grp c t i", grp=PASSES, t=PACK, i=RUN),
             )
 
         def sort_we_scales():
             nc.vector.tensor_copy(
-                out=we_sc[:].rearrange("p (g t m) -> p g t m", g=PASSES, t=PACK),
-                in_=we_raw_sc[:].rearrange("p (g m t) -> p g t m", g=PASSES, t=PACK),
+                out=we_sc[:].rearrange("p (grp t m) -> p grp t m", grp=PASSES, t=PACK),
+                in_=we_raw_sc[:].rearrange("p (grp m t) -> p grp t m", grp=PASSES, t=PACK),
             )
 
-        def turn_x(grp, pair):
+        def turn_x(grp, half):
             words = x_sb[grp][:].bitcast(F32)
-            live["x_bank", grp, pair] = bank = bank_tile([P, 2, 2, P], "z_bank")
+            live["x_bank", grp, half] = bank = bank_tile([P, 2, 2, P], "z_bank")
             for a in range(2):
                 for u in range(2):
-                    nc.tensor.transpose(bank[:, a, u, :], words[:, 2 * pair + a, u:D // 2:2], ident[:])
+                    nc.tensor.transpose(bank[:, a, u, :], words[:, 2 * half + a, u:D // 2:2], ident[:])
 
-        def fetch_x(grp, pair):
-            if pair == 0:
+        def fetch_x(grp, half):
+            if half == 0:
                 live["xT", grp] = work.tile([P, PACK, P, PACK], BF16, name="xT", align_bytes=64)
             nc.scalar.copy(
-                out=live["xT", grp][:, block(pair, 2), :, :].bitcast(F32),
-                in_=live["x_bank", grp, pair][:].rearrange("p a u m -> p a m u"),
+                out=live["xT", grp][:, span(half, 2), :, :].bitcast(F32),
+                in_=live["x_bank", grp, half][:].rearrange("p a u m -> p a m u"),
             )
 
         def quantize_x(grp):
@@ -184,10 +189,10 @@ def tile_relaxedarchetypalreluautoencoder_x2_kernel(
 
         def encode(n, tag="z_bank"):
             i, atom_pass = divmod(n, PASSES)
-            rows = block(i % PACK, P)
+            rows = span(i % PACK, P)
             live["z_sums", n] = bank = bank_tile([P, PACK, P], tag)
             for t in range(PACK):
-                atoms = block(atom_pass * PACK + t, P)
+                atoms = span(atom_pass * PACK + t, P)
                 mx_pass(bank[:, t, :], we_q[:, atoms], we_sc[:, atoms],
                         x_q[i // PACK][:, rows], x_sc[i // PACK][:, rows], True, True)
 
@@ -206,7 +211,7 @@ def tile_relaxedarchetypalreluautoencoder_x2_kernel(
             nc.vector.tensor_scalar(out=dst, in0=sums, scalar1=0.0, scalar2=None, op0=ALU.max)
 
         def quantize_z(i):
-            quantize(z_q[i][:], z_sc[i][:], live["zT", i][:].rearrange("p g m t -> p (g m t)"))
+            quantize(z_q[i][:], z_sc[i][:], live["zT", i][:].rearrange("p grp m t -> p (grp m t)"))
 
 
         def spread_g():
@@ -238,33 +243,33 @@ def tile_relaxedarchetypalreluautoencoder_x2_kernel(
             live["pg", j] = pg = work.tile([P, N], BF16, name="pg")
             nc.vector.scalar_tensor_tensor(
                 out=pg[:], in0=live["exps", j][:], scalar=inv_sum[j][:],
-                in1=live["g"][:].rearrange("p u g n -> p (u g n)").bitcast(BF16),
+                in1=live["g"][:].rearrange("p u grp n -> p (u grp n)").bitcast(BF16),
                 op0=ALU.mult, op1=ALU.mult,
             )
 
         def turn_weights(j):
             live["pg_bank", j] = bank = bank_tile([P, PACK, P], "turn_bank")
             words = live["pg", j][:].bitcast(F32)
-            for run in range(PACK):
-                nc.tensor.transpose(bank[:, run, :], words[:, block(run, P)], ident[:])
+            for w in range(PACK):
+                nc.tensor.transpose(bank[:, w, :], words[:, span(w, P)], ident[:])
 
         def fetch_weights(j):
             live["pgT", j] = pgT = work.tile([P, PASSES, P, PACK], BF16, name="pgT", align_bytes=64)
             nc.scalar.copy(
                 out=pgT[:].bitcast(F32),
-                in_=live["pg_bank", j][:].rearrange("p (u g) f -> p g f u", u=2),
+                in_=live["pg_bank", j][:].rearrange("p (u grp) f -> p grp f u", u=2),
             )
 
         def quantize_weights(j):
             live["pg_q", j] = codes = work.tile([P, PASSES * P], U32, name="pg_q", align_bytes=64)
             live["pg_sc", j] = scales = work.tile([P, PASSES * P], U8, name="pg_sc", align_bytes=64)
-            quantize(codes[:], scales[:], live["pgT", j][:].rearrange("p g f t -> p (g f t)"))
+            quantize(codes[:], scales[:], live["pgT", j][:].rearrange("p grp f t -> p (grp f t)"))
 
-        def archetypes(j, parts=(ALL_D,)):
+        def archetypes(j, col_ranges=(ALL_D,)):
             live["a", j] = acc = bank_tile([P, D], "a_bank")
-            for cols in parts:
+            for cols in col_ranges:
                 for grp in range(PASSES):
-                    atoms = block(grp, P)
+                    atoms = span(grp, P)
                     c_cols = slice(grp * D + cols.start, grp * D + cols.stop)
                     mx_pass(acc[:, cols], live["pg_q", j][:, atoms], live["pg_sc", j][:, atoms],
                             c_q[:, c_cols], c_sc[:, c_cols], grp == 0, grp == PASSES - 1)
@@ -284,7 +289,7 @@ def tile_relaxedarchetypalreluautoencoder_x2_kernel(
             nc.scalar.activation(out=squares[:], in_=lam_rows(j), func=ACT.Square, accum_out=sq_sum[:, j:j + 1])
 
         def lam_bound(pair):
-            cols = block(pair, 2)
+            cols = span(pair, 2)
             nc.gpsimd.tensor_scalar(out=sq_bounded[:, cols], in0=sq_sum[:, cols], scalar1=EPS, scalar2=1.0,
                                     op0=ALU.add, op1=ALU.max)
             nc.gpsimd.tensor_tensor(out=shrink[:, cols], in0=sq_bounded[:, cols], in1=minus_half[:], op=ALU.pow)
@@ -315,15 +320,15 @@ def tile_relaxedarchetypalreluautoencoder_x2_kernel(
             for t in range(slots.start, slots.stop):
                 i = grp * PACK + t
                 for atom_pass in range(PASSES):
-                    rows = block(atom_pass, P)
+                    rows = span(atom_pass, P)
                     mx_pass(bank[:, t - slots.start, :], z_q[i][:, rows], z_sc[i][:, rows],
                             dic_q[atom_pass][:, cols], dic_sc[atom_pass][:, cols],
                             atom_pass == 0, atom_pass == PASSES - 1)
 
         def fetch_out(grp, cols, slots):
-            part = out_sb[grp][:, slots, cols]
-            nc.scalar.copy(out=part, in_=live["out_sums", grp, cols.start, slots.start][:])
-            nc.sync.dma_start(out=pass_rows(out_0, grp)[:, slots, cols], in_=part)
+            dst = out_sb[grp][:, slots, cols]
+            nc.scalar.copy(out=dst, in_=live["out_sums", grp, cols.start, slots.start][:])
+            nc.sync.dma_start(out=pass_rows(out_0, grp)[:, slots, cols], in_=dst)
 
         def interleave_out(grp, cols, copy=nc.vector.tensor_copy):
             live["outT", grp, cols.start] = outT = work.tile(
@@ -342,17 +347,15 @@ def tile_relaxedarchetypalreluautoencoder_x2_kernel(
             for q in range(QUADRANTS):
                 queue = nc.scalar if q % 2 else nc.sync
                 queue.dma_start(
-                    out=out_2[:, block(q, 4), :].bitcast(I32).rearrange("g r d -> r g d"),
-                    in_=out_sc[32 * q:32 * q + 4, :, :].bitcast(I32),
+                    out=out_2[:, span(q, SCALE_ROWS), :].bitcast(I32).rearrange("grp r d -> r grp d"),
+                    in_=out_sc[scale_partitions(q), :, :].bitcast(I32),
                 )
 
 
-        nc.vector.memset(warm_in[:], 0.0)
         nc.vector.memset(we_raw_sc[:].bitcast(I32), 0)
         nc.vector.memset(c_sc[:].bitcast(I32), 0)
         make_identity(nc, ident[:])
         nc.gpsimd.memset(minus_half[:], -0.5)
-        nc.scalar.activation(out=warm_out[:], in_=warm_in[:], func=ACT.Exp)
 
         load_logits(0)
         load_vector(g_sb, g)

@@ -1,5 +1,4 @@
 from contextlib import ExitStack
-from functools import partial
 
 import concourse.mybir as mybir
 from concourse.masks import make_identity
@@ -17,38 +16,7 @@ ALU = mybir.AluOpType
 ACT = mybir.ActivationFunctionType
 
 P = 128
-PACK = 4
-K_PASS = P * PACK
-PASSES = 2
-TILES = PASSES * PACK
-QUADRANTS = 4
-SCALE_ROWS = 4
-RUN = 4
-EPS = 1e-12
-
-BANKS = {"g_bank": 1, "turn_bank": 2, "a_bank": 2, "z_bank": 3}
-
-MAX_LEAD = 3
-DIC_LAG = 3
-
-ALL_D = slice(0, D)
-LO, HI = slice(0, D // 2), slice(D // 2, D)
-HI_FIRST, HI_LAST = slice(D // 2, D // 2 + P), slice(D // 2 + P, D)
-FRONT = slice(0, 2)
-ONE = [slice(t, t + 1) for t in range(PACK)]
-
-
-def width(cols):
-    return cols.stop - cols.start
-
-
-def span(index, size):
-    return slice(index * size, (index + 1) * size)
-
-
-def scale_partitions(q):
-    first = q * (P // QUADRANTS)
-    return slice(first, first + SCALE_ROWS)
+HALF = D // 2
 
 
 def tile_relaxedarchetypalreluautoencoder_x2_kernel(
@@ -56,447 +24,571 @@ def tile_relaxedarchetypalreluautoencoder_x2_kernel(
 ):
     nc = tc.nc
     with ExitStack() as ctx:
-        keep = ctx.enter_context(tc.tile_pool(name="keep", bufs=1))
-        work = ctx.enter_context(tc.tile_pool(name="work", bufs=2))
+        sb = ctx.enter_context(tc.tile_pool(name="sb", bufs=1))
         psum = ctx.enter_context(tc.psum_pool(name="psum", bufs=1))
         ctx.enter_context(tc.manual_schedule())
 
-        def kept(name, shape, dtype):
-            return keep.tile(shape, dtype, name=name, align_bytes=64)
+        def keep(name, shape, dtype, tag=None):
+            return sb.tile(shape, dtype, name=name, tag=tag or name, align_bytes=64)
 
-        def kept_list(name, count, shape, dtype):
-            return [kept("%s%d" % (name, i), shape, dtype) for i in range(count)]
+        def bank(name, k):
+            return psum.tile([P, 512], F32, name=name, tag="bank%d" % k)
 
-        def bank_tile(shape, tag):
-            return psum.tile(shape, F32, name=tag, bufs=BANKS[tag])
+        logits_v = logits.rearrange("(G p t) n -> G p t n", G=2, t=4)
+        x_v = x.rearrange("(G p t) k -> G p t k", G=2, t=4)
+        lam_v = lam.rearrange("(G p t) d -> G p t d", G=2, t=4)
+        out_v = out_0.rearrange("(G p t) d -> G p t d", G=2, t=4)
 
-        ident = kept("ident", [P, P], F32)
-        minus_half = kept("minus_half", [P, 2], F32)
-        logit_sb = kept_list("logit", TILES, [P, N], BF16)
-        lam_sb = kept_list("lam", TILES // 2, [P, 2, D], BF16)
-        x_sb = kept_list("x", PASSES, [P, PACK, D], BF16)
-        g_sb = kept("g_sb", [P, PASSES, PACK], BF16)
-        s_sb = kept("s_sb", [P, PASSES, PACK], BF16)
-        s_f32 = kept("s_f32", [P, PASSES, PACK], F32)
-        we_raw_sc = work.tile([P, F], U8, name="we_raw_sc", tag="staging")
-        we_raw = work.tile([P, F], U32, name="we_raw", tag="staging")
-        we_q = kept("we_q", [P, F], U32)
-        we_sc = kept("we_sc", [P, F], U8)
-        c_q = kept("c_q", [P, PASSES * D], U32)
-        c_sc = kept("c_sc", [P, PASSES * D], U8)
-        x_q = kept_list("x_q", PASSES, [P, K_PASS], U32)
-        x_sc = kept_list("x_sc", PASSES, [P, K_PASS], U8)
-        z_q = kept_list("z_q", TILES, [P, PASSES * P], U32)
-        z_sc = kept_list("z_sc", TILES, [P, PASSES * P], U8)
-        dic_rows = kept_list("dic_rows", PASSES, [P, PACK, D], BF16)
-        dic_q = kept_list("dic_q", PASSES, [P, D], U32)
-        dic_sc = kept_list("dic_sc", PASSES, [P, D], U8)
-        out_sb = kept_list("out_sb", PASSES, [P, PACK, D], F32)
-        out_q = kept_list("out_q", PASSES, [P, D], U32)
-        out_sc = kept("out_sc", [P, PASSES, D], U8)
-        neg_max = kept_list("neg_max", TILES, [P, 1], F32)
-        exp_sum = kept_list("exp_sum", TILES, [P, 1], F32)
-        inv_sum = kept_list("inv_sum", TILES, [P, 1], F32)
-        sq_sum = kept("sq_sum", [P, TILES], F32)
-        sq_bounded = kept("sq_bounded", [P, TILES], F32)
-        shrink = kept("shrink", [P, TILES], F32)
-        live = {}
+        zeros = keep("zeros", [P, P], BF16)
+        ones = keep("ones", [P, P], BF16)
+        g_row = keep("g_row", [P, N], BF16)
+        ident = keep("ident", [P, P], F32)
+        neg_half = keep("neg_half", [P, 4], F32)
+        we_scale_raw = keep("we_scale_raw", [P, F], U8)
+        c_scale = keep("c_scale", [P, 2, D], U8)
+        we_raw = keep("we_raw", [P, F], U32)
+        we_code = keep("we_code", [P, F], U32)
+        we_scale = keep("we_scale", [P, F], U8)
+        c_code = keep("c_code", [P, 2, D], U32)
+        s_raw = keep("s_raw", [P, 2, 4], BF16)
+        s_col = keep("s_col", [P, 8], F32)
+        lg = [keep("lg%d" % i, [P, N], BF16) for i in range(2)]
+        lg_pair = [keep("lgp%d" % j, [P, 2, N], BF16) for j in range(1, 4)]
+        lam_sb = [keep("lam%d" % G, [P, 4, D], BF16) for G in range(2)]
+        x_sb = [keep("x%d" % G, [P, 4, D], BF16) for G in range(2)]
+        neg_max = [keep("nmax%d" % i, [P, 1], F32) for i in range(8)]
+        total = [keep("total%d" % i, [P, 1], F32) for i in range(8)]
+        inv_total = [keep("inv%d" % i, [P, 1], F32) for i in range(8)]
+        e = {}
+        pg = {}
+        pg_t = [keep("pgt%d" % i, [P, 2, P, 4], BF16) for i in range(8)]
+        pg_code = [keep("pgc%d" % i, [P, 2 * P], U32) for i in range(8)]
+        pg_scale = [keep("pgs%d" % i, [P, 2 * P], U8) for i in range(8)]
+        sq = [keep("sq%d" % G, [P, 4], F32) for G in range(2)]
+        clamp = [keep("clamp%d" % G, [P, 4], F32) for G in range(2)]
+        shrink = [keep("shrink%d" % G, [P, 4], F32) for G in range(2)]
+        gain = [keep("gain%d" % G, [P, 4], F32) for G in range(2)]
+        lam_term = [keep("lamt%d" % i, [P, D], F32) for i in range(8)]
+        dic = [keep("dic%d" % G, [P, 4, D], BF16) for G in range(2)]
+        dic_il = [[keep("dici%d%d" % (G, h), [P, HALF, 4], BF16) for h in range(2)] for G in range(2)]
+        dic_code = [[keep("dicc%d%d" % (G, h), [P, HALF], U32) for h in range(2)] for G in range(2)]
+        dic_scale = [[keep("dics%d%d" % (G, h), [P, HALF], U8) for h in range(2)] for G in range(2)]
+        x_t = [keep("xt%d" % R, [P, 4, P, 4], BF16) for R in range(2)]
+        x_code = [keep("xc%d" % R, [P, 4 * P], U32) for R in range(2)]
+        x_scale = [keep("xs%d" % R, [P, 4 * P], U8) for R in range(2)]
+        z = [[keep("z%d%d" % (G, R), [P, 4, P, 4], BF16) for R in range(2)] for G in range(2)]
+        z_code = [[keep("zc%d%d" % (G, R), [P, 4 * P], U32) for R in range(2)] for G in range(2)]
+        z_scale = [[keep("zs%d%d" % (G, R), [P, 4 * P], U8) for R in range(2)] for G in range(2)]
+        res = [[keep("res%d%d" % (R, h), [P, 4, HALF], F32) for h in range(2)] for R in range(2)]
+        res_il = [[keep("resi%d%d" % (R, h), [P, HALF, 4], BF16) for h in range(2)] for R in range(2)]
+        res_code = [[keep("resc%d%d" % (R, h), [P, HALF], U32) for h in range(2)] for R in range(2)]
+        res_scale = keep("ress", [P, 2, D], U8)
+        g_bank = psum.tile([P, N], BF16, name="g_bank", tag="bank7")
+        held = {}
 
+        def logit_rows(i):
+            return lg[i][:] if i < 2 else lg_pair[i // 2 - 1][:, i % 2, :]
 
-        def pass_rows(matrix, grp):
-            return matrix[span(grp, K_PASS), :].rearrange("(p t) n -> p t n", t=PACK)
+        def load_logits(i):
+            if i < 2:
+                nc.sync.dma_start(out=lg[i][:], in_=logits_v[0, :, i, :])
+            else:
+                t = i % 4
+                nc.sync.dma_start(out=lg_pair[i // 2 - 1][:], in_=logits_v[i // 4, :, t : t + 2, :])
 
-        def load_vector(tile, vector):
-            nc.sync.dma_start(out=tile[:], in_=vector.rearrange("(grp p t) -> p grp t", grp=PASSES, t=PACK))
+        def load_rows(tiles, view, G):
+            nc.sync.dma_start(out=tiles[G][:], in_=view[G])
 
-        def load_logits(j):
-            nc.sync.dma_start(out=logit_sb[j][:], in_=pass_rows(logits, j // PACK)[:, j % PACK, :])
+        def load_g():
+            nc.sync.dma_start(out=g_row[0:1, :], in_=g.rearrange("(o n) -> o n", o=1))
 
-        def load_lam(pair):
-            nc.sync.dma_start(out=lam_sb[pair][:], in_=pass_rows(lam, pair // 2)[:, span(pair % 2, 2), :])
-
-        def load_x(grp):
-            nc.sync.dma_start(out=x_sb[grp][:], in_=pass_rows(x, grp))
-
-        def load_we_codes():
-            words = we_words[0].rearrange("p n t -> p (n t)").bitcast(I32)
-            nc.sync.dma_start(out=we_raw[:].bitcast(I32), in_=words)
-
-        def load_we_scales():
-            for q in range(QUADRANTS):
-                nc.sync.dma_start(
-                    out=we_raw_sc[scale_partitions(q), :].bitcast(I32),
-                    in_=we_scales[0, span(q, SCALE_ROWS), :].bitcast(I32),
-                )
-
-        def load_c_codes():
-            words = c_words.rearrange("grp p d t -> p grp (d t)").bitcast(I32)
-            nc.sync.dma_start(out=c_q[:].bitcast(I32).rearrange("p (grp d) -> p grp d", grp=PASSES), in_=words)
+        def load_s():
+            nc.sync.dma_start(out=s_raw[:], in_=s.rearrange("(G p t) -> p G t", G=2, t=4))
 
         def load_c_scales():
-            for q in range(QUADRANTS):
+            for q in range(4):
                 nc.sync.dma_start(
-                    out=c_sc[scale_partitions(q), :].bitcast(I32).rearrange("r (grp d) -> r grp d", grp=PASSES),
-                    in_=c_scales[:, span(q, SCALE_ROWS), :].bitcast(I32).rearrange("grp r d -> r grp d"),
+                    out=c_scale[32 * q : 32 * q + 4, :, :].bitcast(I32),
+                    in_=c_scales[:, 4 * q : 4 * q + 4, :].rearrange("g r d -> r g d").bitcast(I32),
                 )
 
+        def load_we_scales():
+            for q in range(4):
+                nc.sync.dma_start(
+                    out=we_scale_raw[32 * q : 32 * q + 4, :].bitcast(I32),
+                    in_=we_scales[0, 4 * q : 4 * q + 4, :].bitcast(I32),
+                )
+
+        def load_c():
+            nc.sync.dma_start(
+                out=c_code[:].bitcast(I32),
+                in_=c_words.rearrange("g p d t -> p g (d t)").bitcast(I32),
+            )
+
+        def load_we():
+            nc.sync.dma_start(
+                out=we_raw[:].bitcast(I32),
+                in_=we_words[0].rearrange("p f t -> p (f t)").bitcast(I32),
+            )
+
+        def setup_zeros():
+            nc.vector.memset(zeros[:], 0.0)
+
+        def setup_vector():
+            nc.vector.memset(g_row[:], 0.0)
+            nc.vector.memset(c_scale[:].rearrange("p g d -> p (g d)").bitcast(I32), 0)
+            nc.vector.memset(we_scale_raw[:].bitcast(I32), 0)
+
+        def setup_scalar():
+            nc.scalar.activation(out=ones[:], in_=zeros[:], func=ACT.Exp)
+
+        def setup_gpsimd():
+            make_identity(nc, ident[:])
+            nc.gpsimd.memset(neg_half[:], -0.5)
+
+        def copy(eng, out, in_):
+            if eng is nc.scalar:
+                nc.scalar.copy(out=out, in_=in_)
+            elif eng is nc.vector:
+                nc.vector.tensor_copy(out=out, in_=in_)
+            else:
+                nc.gpsimd.tensor_scalar(out=out, in0=in_, scalar1=1.0, scalar2=0.0, op0=ALU.mult, op1=ALU.add)
+
+        def spread_g():
+            g_pairs = g_row[:].rearrange("p (q u e) -> p u q e", u=2, e=2)
+            for u in range(2):
+                nc.tensor.matmul(
+                    out=g_bank[:, 512 * u : 512 * (u + 1)], lhsT=ones[:], rhs=g_pairs[:, u, :, :], start=True, stop=True
+                )
+
+        def widen_s():
+            nc.gpsimd.tensor_copy(out=s_col[:], in_=s_raw[:].rearrange("p G t -> p (G t)"))
+
+        def permute_we(G, eng):
+            cols = slice(512 * G, 512 * (G + 1))
+            eng.tensor_copy(
+                out=we_code[:, cols].bitcast(I32).rearrange("p (t m) -> p t m", t=4),
+                in_=we_raw[:, cols].bitcast(I32).rearrange("p (m t) -> p t m", t=4),
+            )
+            eng.tensor_copy(
+                out=we_scale[:, cols].rearrange("p (t m) -> p t m", t=4),
+                in_=we_scale_raw[:, cols].rearrange("p (m t) -> p t m", t=4),
+            )
+
+        def row_max(i):
+            rows = logit_rows(i)
+            nc.vector.tensor_scalar(
+                out=rows, in0=rows, scalar1=-1.0, scalar2=None, op0=ALU.mult, op1=ALU.min, accum_out=neg_max[i][:]
+            )
+
+        def exponentiate(i):
+            e[i] = keep("e%d" % i, [P, N], F32, "e%d" % (i % 4))
+            nc.scalar.activation(
+                out=e[i][:].rearrange("p (u q e) -> p u q e", u=2, e=2),
+                in_=logit_rows(i).rearrange("p (q u e) -> p u q e", u=2, e=2),
+                func=ACT.Exp,
+                bias=neg_max[i][:],
+                scale=-1.0,
+                accum_out=total[i][:],
+            )
+
+        def invert(i):
+            nc.vector.reciprocal(out=inv_total[i][:], in_=total[i][:])
+
+        def weigh(i):
+            pg[i] = keep("pg%d" % i, [P, N], BF16, "pg%d" % (i % 4))
+            nc.vector.scalar_tensor_tensor(
+                out=pg[i][:], in0=e[i][:], scalar=inv_total[i][:], in1=g_bank[:], op0=ALU.mult, op1=ALU.mult
+            )
+
+        def turn_pg(i, k):
+            words = pg[i][:].bitcast(F32)
+            b = bank("tp%d" % i, k)
+            held["tp", i] = b
+            for u in range(2):
+                for c in range(2):
+                    j = 2 * c + u
+                    nc.tensor.transpose(
+                        b[:, P * j : P * (j + 1)], words[:, 256 * u + P * c : 256 * u + P * (c + 1)], ident[:]
+                    )
+
+        def drain_pg(i, eng):
+            copy(
+                eng, out=pg_t[i][:].bitcast(F32), in_=held["tp", i][:].rearrange("p (c u f) -> p c f u", c=2, u=2)
+            )
 
         def quantize(codes, scales, values):
             nc.vector.quantize_mx(out=codes.bitcast(FP8X4), scales=scales, in_=values)
 
-        def mx_pass(acc, lhs_q, lhs_sc, rhs_q, rhs_sc, first, last):
-            nc.tensor.matmul_mx(
-                out=acc, lhsT=lhs_q.bitcast(FP8X4), lhsT_scale=lhs_sc,
-                rhs=rhs_q.bitcast(FP8X4), rhs_scale=rhs_sc, start=first, stop=last,
-            )
+        def quantize_pg(i):
+            quantize(pg_code[i][:], pg_scale[i][:], pg_t[i][:].rearrange("p c f t -> p (c f t)"))
 
-        def interleave(dst, src, copy=nc.vector.tensor_copy):
-            copy(
-                out=dst.rearrange("p (c i) t -> p c t i", i=RUN),
-                in_=src.rearrange("p t (c i) -> p c t i", i=RUN),
-            )
-
-
-        def sort_we_codes():
-            nc.vector.tensor_copy(
-                out=we_q[:].bitcast(I32).rearrange("p (grp t c i) -> p grp c t i", grp=PASSES, t=PACK, i=RUN),
-                in_=we_raw[:].bitcast(I32).rearrange("p (grp c i t) -> p grp c t i", grp=PASSES, t=PACK, i=RUN),
-            )
-
-        def sort_we_scales():
-            nc.vector.tensor_copy(
-                out=we_sc[:].rearrange("p (grp t m) -> p grp t m", grp=PASSES, t=PACK),
-                in_=we_raw_sc[:].rearrange("p (grp m t) -> p grp t m", grp=PASSES, t=PACK),
-            )
-
-        def turn_x(grp, half):
-            words = x_sb[grp][:].bitcast(F32)
-            live["x_bank", grp, half] = bank = bank_tile([P, 2, 2, P], "z_bank")
-            for a in range(2):
-                for u in range(2):
-                    nc.tensor.transpose(bank[:, a, u, :], words[:, 2 * half + a, u:D // 2:2], ident[:])
-
-        def fetch_x(grp, half):
-            if half == 0:
-                live["xT", grp] = work.tile([P, PACK, P, PACK], BF16, name="xT", align_bytes=64)
-            nc.scalar.copy(
-                out=live["xT", grp][:, span(half, 2), :, :].bitcast(F32),
-                in_=live["x_bank", grp, half][:].rearrange("p a u m -> p a m u"),
-            )
-
-        def quantize_x(grp):
-            quantize(x_q[grp][:], x_sc[grp][:], live["xT", grp][:].rearrange("p a m t -> p (a m t)"))
-
-        def encode(n, tag="z_bank"):
-            i, atom_pass = divmod(n, PASSES)
-            rows = span(i % PACK, P)
-            live["z_sums", n] = bank = bank_tile([P, PACK, P], tag)
-            for t in range(PACK):
-                atoms = span(atom_pass * PACK + t, P)
-                mx_pass(bank[:, t, :], we_q[:, atoms], we_sc[:, atoms],
-                        x_q[i // PACK][:, rows], x_sc[i // PACK][:, rows], True, True)
-
-        def rectified_part(n):
-            i, atom_pass = divmod(n, PASSES)
-            if atom_pass == 0:
-                live["zT", i] = work.tile([P, PASSES, P, PACK], BF16, name="zT", align_bytes=64, bufs=6)
-            return live["zT", i][:, atom_pass, :, :], live["z_sums", n][:].rearrange("p t m -> p m t")
-
-        def rectify(n):
-            dst, sums = rectified_part(n)
-            nc.scalar.activation(out=dst, in_=sums, func=ACT.Relu)
-
-        def rectify_on_vector(n):
-            dst, sums = rectified_part(n)
-            nc.vector.tensor_scalar(out=dst, in0=sums, scalar1=0.0, scalar2=None, op0=ALU.max)
-
-        def quantize_z(i):
-            quantize(z_q[i][:], z_sc[i][:], live["zT", i][:].rearrange("p grp m t -> p (grp m t)"))
-
-
-        def spread_g():
-            live["g"] = bank = bank_tile([P, 2, PASSES, P], "g_bank")
-            words = g_sb[:].bitcast(F32)
-            for u in range(2):
-                for grp in range(PASSES):
-                    nc.tensor.transpose(bank[:, u, grp, :], words[:, grp, u:u + 1].to_broadcast([P, P]), ident[:])
-
-        def row_max(j):
-            live["neg", j] = neg = work.tile([P, N], BF16, name="neg", bufs=MAX_LEAD + 1)
-            nc.vector.tensor_scalar(
-                out=neg[:], in0=logit_sb[j][:], scalar1=-1.0, scalar2=None,
-                op0=ALU.mult, op1=ALU.min, accum_out=neg_max[j][:],
-            )
-
-        def exponentials(j):
-            live["exps", j] = exps = work.tile([P, N], F32, name="exps", bufs=3)
-            nc.scalar.activation(
-                out=exps[:].rearrange("p (u w e) -> p u w e", u=2, e=2),
-                in_=live["neg", j][:].rearrange("p (w u e) -> p u w e", u=2, e=2),
-                func=ACT.Exp, scale=-1.0, bias=neg_max[j][:], accum_out=exp_sum[j][:],
-            )
-
-        def invert_sum(j):
-            nc.vector.reciprocal(out=inv_sum[j][:], in_=exp_sum[j][:])
-
-        def weights(j):
-            live["pg", j] = pg = work.tile([P, N], BF16, name="pg")
-            nc.vector.scalar_tensor_tensor(
-                out=pg[:], in0=live["exps", j][:], scalar=inv_sum[j][:],
-                in1=live["g"][:].rearrange("p u grp n -> p (u grp n)").bitcast(BF16),
-                op0=ALU.mult, op1=ALU.mult,
-            )
-
-        def turn_weights(j):
-            live["pg_bank", j] = bank = bank_tile([P, PACK, P], "turn_bank")
-            words = live["pg", j][:].bitcast(F32)
-            for w in range(PACK):
-                nc.tensor.transpose(bank[:, w, :], words[:, span(w, P)], ident[:])
-
-        def fetch_weights(j):
-            live["pgT", j] = pgT = work.tile([P, PASSES, P, PACK], BF16, name="pgT", align_bytes=64)
-            nc.scalar.copy(
-                out=pgT[:].bitcast(F32),
-                in_=live["pg_bank", j][:].rearrange("p (u grp) f -> p grp f u", u=2),
-            )
-
-        def quantize_weights(j):
-            live["pg_q", j] = codes = work.tile([P, PASSES * P], U32, name="pg_q", align_bytes=64)
-            live["pg_sc", j] = scales = work.tile([P, PASSES * P], U8, name="pg_sc", align_bytes=64)
-            quantize(codes[:], scales[:], live["pgT", j][:].rearrange("p grp f t -> p (grp f t)"))
-
-        def archetypes(j, col_ranges=(ALL_D,)):
-            live["a", j] = acc = bank_tile([P, D], "a_bank")
-            for cols in col_ranges:
-                for grp in range(PASSES):
-                    atoms = span(grp, P)
-                    c_cols = slice(grp * D + cols.start, grp * D + cols.stop)
-                    mx_pass(acc[:, cols], live["pg_q", j][:, atoms], live["pg_sc", j][:, atoms],
-                            c_q[:, c_cols], c_sc[:, c_cols], grp == 0, grp == PASSES - 1)
-
-
-        def lam_rows(j):
-            return lam_sb[j // 2][:, j % 2, :]
-
-        def gain(j):
-            return s_f32[:, j // PACK, j % PACK:j % PACK + 1]
-
-        def widen_gains():
-            nc.gpsimd.tensor_copy(out=s_f32[:], in_=s_sb[:])
-
-        def lam_norm(j):
-            squares = work.tile([P, D], BF16, name="squares")
-            nc.scalar.activation(out=squares[:], in_=lam_rows(j), func=ACT.Square, accum_out=sq_sum[:, j:j + 1])
-
-        def lam_bound(pair):
-            cols = span(pair, 2)
-            nc.gpsimd.tensor_scalar(out=sq_bounded[:, cols], in0=sq_sum[:, cols], scalar1=EPS, scalar2=1.0,
-                                    op0=ALU.add, op1=ALU.max)
-            nc.gpsimd.tensor_tensor(out=shrink[:, cols], in0=sq_bounded[:, cols], in1=minus_half[:], op=ALU.pow)
-
-        def scale_lam(j, engine):
-            live["lam", j] = scaled = work.tile([P, D], F32, name="lam_scaled", tag="staging")
-            engine.tensor_scalar(out=scaled[:], in0=lam_rows(j), scalar1=shrink[:, j:j + 1], scalar2=gain(j),
-                                 op0=ALU.mult, op1=ALU.mult)
-
-        def dictionary(j, cols=ALL_D):
-            nc.vector.scalar_tensor_tensor(
-                out=dic_rows[j // PACK][:, j % PACK, cols], in0=live["a", j][:, cols], scalar=gain(j),
-                in1=live["lam", j][:, cols], op0=ALU.mult, op1=ALU.add,
-            )
-
-        def interleave_dic(grp, cols):
-            live["dicT", grp, cols.start] = dicT = work.tile(
-                [P, width(cols), PACK], BF16, name="dicT", align_bytes=64, bufs=2 * PASSES)
-            interleave(dicT[:], dic_rows[grp][:, :, cols])
-
-        def quantize_dic(grp, cols):
-            quantize(dic_q[grp][:, cols], dic_sc[grp][:, cols],
-                     live["dicT", grp, cols.start][:].rearrange("p d t -> p (d t)"))
-
-
-        def decode(grp, cols, slots, tag):
-            live["out_sums", grp, cols.start, slots.start] = bank = bank_tile([P, width(slots), width(cols)], tag)
-            for t in range(slots.start, slots.stop):
-                i = grp * PACK + t
-                for atom_pass in range(PASSES):
-                    rows = span(atom_pass, P)
-                    mx_pass(bank[:, t - slots.start, :], z_q[i][:, rows], z_sc[i][:, rows],
-                            dic_q[atom_pass][:, cols], dic_sc[atom_pass][:, cols],
-                            atom_pass == 0, atom_pass == PASSES - 1)
-
-        def fetch_out(grp, cols, slots):
-            dst = out_sb[grp][:, slots, cols]
-            nc.scalar.copy(out=dst, in_=live["out_sums", grp, cols.start, slots.start][:])
-            nc.sync.dma_start(out=pass_rows(out_0, grp)[:, slots, cols], in_=dst)
-
-        def interleave_out(grp, cols, copy=nc.vector.tensor_copy):
-            live["outT", grp, cols.start] = outT = work.tile(
-                [P, width(cols), PACK], BF16, name="outT", align_bytes=64, bufs=3)
-            interleave(outT[:], out_sb[grp][:, :, cols], copy)
-
-        def quantize_out(grp, cols):
-            quantize(out_q[grp][:, cols], out_sc[:, grp, cols],
-                     live["outT", grp, cols.start][:].rearrange("p d t -> p (d t)"))
-
-        def store_codes(grp):
-            words = out_1[grp].rearrange("p m t -> p (m t)").bitcast(I32)
-            nc.sync.dma_start(out=words, in_=out_q[grp][:].bitcast(I32))
-
-        def store_scales():
-            for q in range(QUADRANTS):
-                queue = nc.scalar if q % 2 else nc.sync
-                queue.dma_start(
-                    out=out_2[:, span(q, SCALE_ROWS), :].bitcast(I32).rearrange("grp r d -> r grp d"),
-                    in_=out_sc[scale_partitions(q), :, :].bitcast(I32),
+        def archetypes(i, k):
+            b = bank("a%d" % i, k)
+            held["a", i] = b
+            for c in range(2):
+                cols = slice(P * c, P * (c + 1))
+                nc.tensor.matmul_mx(
+                    out=b[:],
+                    lhsT=pg_code[i][:, cols].bitcast(FP8X4),
+                    lhsT_scale=pg_scale[i][:, cols],
+                    rhs=c_code[:, c, :].bitcast(FP8X4),
+                    rhs_scale=c_scale[:, c, :],
+                    start=(c == 0),
+                    stop=(c == 1),
                 )
 
+        def square_sum(i):
+            nc.scalar.activation(
+                out=lam_term[i][:],
+                in_=lam_sb[i // 4][:, i % 4, :],
+                func=ACT.Square,
+                accum_out=sq[i // 4][:, i % 4 : i % 4 + 1],
+            )
 
-        nc.vector.memset(we_raw_sc[:].bitcast(I32), 0)
-        nc.vector.memset(c_sc[:].bitcast(I32), 0)
-        make_identity(nc, ident[:])
-        nc.gpsimd.memset(minus_half[:], -0.5)
+        def lam_gain(G):
+            nc.gpsimd.tensor_scalar(
+                out=clamp[G][:], in0=sq[G][:], scalar1=1e-12, scalar2=1.0, op0=ALU.add, op1=ALU.max
+            )
+            nc.gpsimd.tensor_tensor(out=shrink[G][:], in0=clamp[G][:], in1=neg_half[:], op=ALU.pow)
+            nc.gpsimd.tensor_tensor(out=gain[G][:], in0=shrink[G][:], in1=s_col[:, 4 * G : 4 * G + 4], op=ALU.mult)
+
+        def scale_lam(i, eng):
+            rows = lam_sb[i // 4][:, i % 4, :]
+            factor = gain[i // 4][:, i % 4 : i % 4 + 1]
+            if eng is nc.scalar:
+                nc.scalar.activation(out=lam_term[i][:], in_=rows, func=ACT.Copy, scale=factor)
+            else:
+                eng.tensor_scalar(
+                    out=lam_term[i][:], in0=rows, scalar1=factor, scalar2=0.0, op0=ALU.mult, op1=ALU.add
+                )
+
+        def dictionary(i):
+            nc.vector.scalar_tensor_tensor(
+                out=dic[i // 4][:, i % 4, :],
+                in0=held["a", i][:],
+                scalar=s_col[:, i : i + 1],
+                in1=lam_term[i][:],
+                op0=ALU.mult,
+                op1=ALU.add,
+            )
+
+        def interleave_dic(G, h, eng):
+            copy(
+                eng, out=dic_il[G][h][:], in_=dic[G][:, :, HALF * h : HALF * (h + 1)].rearrange("p t d -> p d t")
+            )
+
+        def quantize_dic(G, h):
+            quantize(dic_code[G][h][:], dic_scale[G][h][:], dic_il[G][h][:].rearrange("p d t -> p (d t)"))
+
+        def turn_x(R, j, k):
+            b = bank("tx%d%d" % (R, j), k)
+            held["tx", R, j] = b
+            for c in range(2):
+                words = x_sb[R][:, 2 * j + c, :].bitcast(F32)
+                for u in range(2):
+                    nc.tensor.transpose(b[:, P * (2 * c + u) : P * (2 * c + u + 1)], words[:, u : 256 : 2], ident[:])
+
+        def drain_x(R, j, eng):
+            copy(
+                eng, out=x_t[R][:, 2 * j : 2 * j + 2, :, :].bitcast(F32),
+                in_=held["tx", R, j][:].rearrange("p (c u m) -> p c m u", c=2, u=2),
+            )
+
+        def quantize_x(R, j):
+            cols = slice(2 * P * j, 2 * P * (j + 1))
+            quantize(
+                x_code[R][:, cols], x_scale[R][:, cols], x_t[R][:, 2 * j : 2 * j + 2].rearrange("p c m t -> p (c m t)")
+            )
+
+        def encode(G, R, c, k):
+            b = bank("zb%d%d%d" % (G, R, c), k)
+            held["z", G, R, c] = b
+            rows = slice(P * c, P * (c + 1))
+            for t in range(4):
+                cols = slice(512 * G + P * t, 512 * G + P * (t + 1))
+                nc.tensor.matmul_mx(
+                    out=b[:, P * t : P * (t + 1)],
+                    lhsT=we_code[:, cols].bitcast(FP8X4),
+                    lhsT_scale=we_scale[:, cols],
+                    rhs=x_code[R][:, rows].bitcast(FP8X4),
+                    rhs_scale=x_scale[R][:, rows],
+                    start=True,
+                    stop=True,
+                )
+
+        def relu(G, R, c, eng):
+            sums = held["z", G, R, c][:].rearrange("p (t m) -> p m t", t=4)
+            if eng is nc.scalar:
+                nc.scalar.activation(out=z[G][R][:, c, :, :], in_=sums, func=ACT.Relu)
+            else:
+                nc.vector.tensor_scalar(out=z[G][R][:, c, :, :], in0=sums, scalar1=0.0, scalar2=None, op0=ALU.max)
+
+        def quantize_z(G, R, j):
+            cols = slice(2 * P * j, 2 * P * (j + 1))
+            quantize(
+                z_code[G][R][:, cols],
+                z_scale[G][R][:, cols],
+                z[G][R][:, 2 * j : 2 * j + 2].rearrange("p c m t -> p (c m t)"),
+            )
+
+        def decode(R, h, j, k):
+            b = bank("o%d%d%d" % (R, h, j), k)
+            held["o", R, h, j] = b
+            for c in range(2):
+                rows = slice(P * (2 * j + c), P * (2 * j + c + 1))
+                for G in range(2):
+                    nc.tensor.matmul_mx(
+                        out=b[:, HALF * c : HALF * (c + 1)],
+                        lhsT=z_code[G][R][:, rows].bitcast(FP8X4),
+                        lhsT_scale=z_scale[G][R][:, rows],
+                        rhs=dic_code[G][h][:].bitcast(FP8X4),
+                        rhs_scale=dic_scale[G][h][:],
+                        start=(G == 0),
+                        stop=(G == 1),
+                    )
+
+        def drain_out(R, h, j, eng):
+            copy(
+                eng, out=res[R][h][:, 2 * j : 2 * j + 2, :], in_=held["o", R, h, j][:].rearrange("p (c d) -> p c d", c=2)
+            )
+
+        def store_out(R, h, j):
+            nc.sync.dma_start(
+                out=out_v[R, :, 2 * j : 2 * j + 2, HALF * h : HALF * (h + 1)], in_=res[R][h][:, 2 * j : 2 * j + 2, :]
+            )
+
+        def interleave_out(R, h, eng):
+            copy(eng, out=res_il[R][h][:], in_=res[R][h][:].rearrange("p t d -> p d t"))
+
+        def quantize_out(R, h):
+            quantize(
+                res_code[R][h][:],
+                res_scale[:, R, HALF * h : HALF * (h + 1)],
+                res_il[R][h][:].rearrange("p d t -> p (d t)"),
+            )
+
+        def store_codes(R, h):
+            nc.sync.dma_start(
+                out=out_1[R].rearrange("p d t -> p (d t)").bitcast(I32)[:, HALF * h : HALF * (h + 1)],
+                in_=res_code[R][h][:].bitcast(I32),
+            )
+
+        def store_scales(R, eng):
+            for q in range(4):
+                eng.dma_start(
+                    out=out_2[R, 4 * q : 4 * q + 4, :].bitcast(I32),
+                    in_=res_scale[32 * q : 32 * q + 4, R, :].bitcast(I32),
+                )
 
         load_logits(0)
-        load_vector(g_sb, g)
+        setup_zeros()
         load_logits(1)
+        setup_vector()
+        setup_scalar()
         load_logits(2)
-        load_logits(3)
-        load_lam(0)
-        load_we_scales()
+        setup_gpsimd()
+        load_g()
         load_logits(4)
-        load_lam(1)
-        load_x(0)
-        load_vector(s_sb, s)
-        load_logits(5)
-        load_c_scales()
-        load_c_codes()
-        load_we_codes()
-        load_lam(2)
-        load_logits(6)
-        load_lam(3)
-        load_logits(7)
-        load_x(1)
-
-        def run(jobs):
-            for job in jobs:
-                job()
-
-        def step(j, scalar_first=(), scalar_last=(), gpsimd=(), tensor_first=(), tensor_middle=(),
-                 tensor_last=(), vector_last=()):
-            invert_sum(j)
-            if j >= DIC_LAG:
-                dictionary(j - DIC_LAG)
-            if j + MAX_LEAD < TILES:
-                row_max(j + MAX_LEAD)
-            exps_first = j == 0 or not scalar_first
-            if exps_first and j + 1 < TILES:
-                exponentials(j + 1)
-            run(scalar_first)
-            run(gpsimd)
-            if j >= 1:
-                fetch_weights(j - 1)
-            if not exps_first:
-                exponentials(j + 1)
-            run(scalar_last)
-            run(tensor_first)
-            weights(j)
-            turn_weights(j)
-            run(tensor_middle)
-            if j >= 1:
-                quantize_weights(j - 1)
-                archetypes(j - 1)
-            run(tensor_last)
-            run(vector_last)
-
-        norm = [partial(lam_norm, j) for j in range(TILES)]
-        scale = [partial(scale_lam, j, nc.gpsimd) for j in range(TILES)]
-        bound = [partial(lam_bound, pair) for pair in range(TILES // 2)]
-        sums = [partial(encode, n) for n in range(2 * BANKS["z_bank"])]
-        relu = [partial(rectify, n) for n in range(PACK)]
-
-        for j in range(MAX_LEAD):
-            row_max(j)
+        load_rows(lam_sb, lam_v, 0)
+        load_we_scales()
+        row_max(0)
+        row_max(1)
+        exponentiate(0)
+        load_rows(x_sb, x_v, 0)
+        row_max(2)
+        load_s()
         spread_g()
-        exponentials(0)
-
-        step(0, scalar_first=norm[0:1], scalar_last=norm[1:2])
-        step(1, scalar_first=norm[2:3], scalar_last=norm[3:4], gpsimd=[bound[0], widen_gains],
-             tensor_first=[partial(turn_x, 0, 0), partial(turn_x, 0, 1)], vector_last=[sort_we_scales])
-        step(2, scalar_first=[partial(fetch_x, 0, 0)], scalar_last=[partial(fetch_x, 0, 1)],
-             gpsimd=[scale[0], bound[1]], vector_last=[sort_we_codes])
-        step(3, scalar_first=norm[4:5], scalar_last=norm[5:6], gpsimd=scale[1:3],
-             vector_last=[partial(quantize_x, 0)])
-        step(4, scalar_first=norm[6:7], scalar_last=norm[7:8], gpsimd=[bound[2], scale[3]],
-             tensor_first=sums[0:3])
-        step(5, scalar_last=relu[0:1], gpsimd=scale[4:5], tensor_last=[partial(turn_x, 1, 0)])
-        step(6, scalar_last=relu[1:3] + [partial(fetch_x, 1, 0)], gpsimd=[bound[3], scale[5]],
-             tensor_middle=sums[3:4], tensor_last=[partial(turn_x, 1, 1)])
-        step(7, scalar_last=relu[3:4] + [partial(fetch_x, 1, 1)], gpsimd=scale[6:7], tensor_middle=sums[4:6])
-
-        last = TILES - 1
-        z_ring = ["z_bank"] * BANKS["z_bank"] + ["turn_bank"] * BANKS["turn_bank"]
-        first_late, parts = PACK, PASSES * TILES
-
-        def encode_late(n):
-            encode(n, z_ring[(n - first_late) % len(z_ring)])
-
-        for n in range(len(sums), first_late + len(z_ring) - 1):
-            encode_late(n)
-        fetch_weights(last)
-        dictionary(last - 2)
-        quantize_z(0)
-        scale_lam(last, nc.vector)
-        quantize_x(1)
-        quantize_weights(last)
-        archetypes(last, (LO, HI))
-        encode_late(first_late + len(z_ring) - 1)
-        for n in range(first_late, parts - 2):
-            rectify(n)
-            if n + len(z_ring) < parts:
-                encode_late(n + len(z_ring))
-            if n == 2 * PACK - 1:
-                dictionary(last - 1)
-                interleave_dic(0, LO)
-                dictionary(last, LO)
-                dictionary(last, HI)
-                quantize_z(1)
-                interleave_dic(1, LO)
-                quantize_dic(0, LO)
-                quantize_dic(1, LO)
-
-        decode(0, LO, FRONT, "g_bank")
-        for grp in range(PASSES):
-            interleave_dic(grp, HI)
-        for grp in range(PASSES):
-            quantize_dic(grp, HI)
-        for i in range(2, PACK):
-            quantize_z(i)
-        decode(0, HI, FRONT, "a_bank")
-        decode(0, ALL_D, ONE[2], "a_bank")
-        decode(0, ALL_D, ONE[3], "turn_bank")
-        fetch_out(0, LO, FRONT)
-        rectify(parts - 2)
-        rectify_on_vector(parts - 1)
-        for i in range(PACK, TILES):
-            quantize_z(i)
-        for t, tag in enumerate(("g_bank", "turn_bank", "z_bank", "z_bank")):
-            decode(1, ALL_D, ONE[t], tag)
-        fetch_out(0, HI, FRONT)
-        fetch_out(0, ALL_D, ONE[2])
-        fetch_out(0, ALL_D, ONE[3])
-        for t in range(PACK):
-            fetch_out(1, ALL_D, ONE[t])
-        interleave_out(0, LO)
-        interleave_out(0, HI)
-        quantize_out(0, LO)
-        quantize_out(0, HI)
-        store_codes(0)
-        interleave_out(1, LO)
-        interleave_out(1, HI_LAST, nc.scalar.copy)
-        interleave_out(1, HI_FIRST)
-        quantize_out(1, LO)
-        quantize_out(1, HI_LAST)
-        quantize_out(1, HI_FIRST)
-        store_codes(1)
-        store_scales()
+        exponentiate(1)
+        invert(0)
+        row_max(3)
+        load_rows(lam_sb, lam_v, 1)
+        exponentiate(2)
+        row_max(4)
+        weigh(0)
+        load_rows(x_sb, x_v, 1)
+        load_we()
+        load_c_scales()
+        square_sum(2)
+        exponentiate(3)
+        invert(1)
+        row_max(5)
+        turn_x(0, 0, 0)
+        load_logits(6)
+        widen_s()
+        invert(2)
+        weigh(1)
+        square_sum(3)
+        load_c()
+        square_sum(1)
+        invert(3)
+        drain_x(0, 0, nc.vector)
+        turn_pg(1, 1)
+        square_sum(0)
+        weigh(3)
+        turn_x(1, 0, 2)
+        exponentiate(4)
+        lam_gain(0)
+        turn_x(1, 1, 3)
+        weigh(2)
+        square_sum(7)
+        turn_pg(3, 4)
+        exponentiate(5)
+        permute_we(0, nc.vector)
+        turn_pg(0, 5)
+        turn_x(0, 1, 6)
+        scale_lam(2, nc.gpsimd)
+        invert(4)
+        row_max(6)
+        drain_pg(3, nc.scalar)
+        turn_pg(2, 0)
+        permute_we(1, nc.vector)
+        exponentiate(6)
+        quantize_x(0, 0)
+        invert(5)
+        scale_lam(3, nc.gpsimd)
+        weigh(4)
+        square_sum(6)
+        scale_lam(0, nc.gpsimd)
+        drain_x(1, 1, nc.scalar)
+        row_max(7)
+        turn_pg(4, 4)
+        drain_pg(1, nc.scalar)
+        scale_lam(1, nc.gpsimd)
+        encode(1, 0, 1, 3)
+        drain_x(0, 1, nc.vector)
+        drain_pg(0, nc.scalar)
+        quantize_pg(1)
+        drain_pg(4, nc.scalar)
+        weigh(5)
+        archetypes(1, 1)
+        drain_pg(2, nc.scalar)
+        drain_x(1, 0, nc.scalar)
+        quantize_x(1, 1)
+        encode(1, 0, 0, 6)
+        quantize_pg(3)
+        square_sum(5)
+        quantize_x(0, 1)
+        invert(6)
+        relu(1, 0, 0, nc.vector)
+        square_sum(4)
+        encode(0, 0, 3, 5)
+        encode(0, 0, 1, 4)
+        quantize_pg(0)
+        relu(1, 0, 1, nc.scalar)
+        encode(1, 0, 3, 0)
+        quantize_pg(2)
+        archetypes(3, 2)
+        quantize_pg(4)
+        relu(0, 0, 3, nc.scalar)
+        quantize_x(1, 0)
+        archetypes(2, 6)
+        weigh(6)
+        lam_gain(1)
+        exponentiate(7)
+        encode(0, 0, 2, 3)
+        dictionary(3)
+        relu(0, 0, 1, nc.scalar)
+        turn_pg(6, 5)
+        invert(7)
+        relu(1, 0, 3, nc.scalar)
+        quantize_z(1, 0, 0)
+        turn_pg(5, 2)
+        weigh(7)
+        scale_lam(6, nc.gpsimd)
+        encode(0, 0, 0, 4)
+        drain_pg(6, nc.scalar)
+        archetypes(0, 0)
+        scale_lam(5, nc.gpsimd)
+        drain_pg(5, nc.scalar)
+        dictionary(1)
+        turn_pg(7, 5)
+        relu(0, 0, 2, nc.scalar)
+        scale_lam(4, nc.gpsimd)
+        encode(1, 0, 2, 2)
+        dictionary(2)
+        relu(0, 0, 0, nc.scalar)
+        archetypes(4, 1)
+        drain_pg(7, nc.vector)
+        scale_lam(7, nc.gpsimd)
+        relu(1, 0, 2, nc.scalar)
+        encode(0, 1, 2, 3)
+        dictionary(0)
+        encode(0, 1, 0, 6)
+        encode(0, 1, 3, 4)
+        quantize_pg(7)
+        interleave_dic(0, 0, nc.scalar)
+        encode(1, 1, 3, 5)
+        dictionary(4)
+        archetypes(7, 2)
+        quantize_pg(6)
+        quantize_pg(5)
+        interleave_dic(0, 1, nc.scalar)
+        dictionary(7)
+        archetypes(5, 0)
+        quantize_z(0, 0, 0)
+        archetypes(6, 1)
+        quantize_z(0, 0, 1)
+        relu(0, 1, 3, nc.scalar)
+        dictionary(5)
+        encode(1, 1, 1, 2)
+        relu(1, 1, 3, nc.scalar)
+        encode(0, 1, 1, 4)
+        dictionary(6)
+        encode(1, 1, 2, 0)
+        relu(0, 1, 0, nc.scalar)
+        quantize_dic(0, 0)
+        encode(1, 1, 0, 5)
+        interleave_dic(1, 0, nc.vector)
+        relu(1, 1, 2, nc.scalar)
+        quantize_dic(0, 1)
+        interleave_dic(1, 1, nc.scalar)
+        quantize_dic(1, 0)
+        quantize_z(1, 0, 1)
+        decode(0, 0, 0, 1)
+        relu(1, 1, 1, nc.vector)
+        relu(1, 1, 0, nc.scalar)
+        decode(0, 0, 1, 6)
+        quantize_dic(1, 1)
+        relu(0, 1, 1, nc.vector)
+        drain_out(0, 0, 0, nc.scalar)
+        decode(0, 1, 0, 0)
+        quantize_z(1, 1, 0)
+        drain_out(0, 0, 1, nc.scalar)
+        store_out(0, 0, 0)
+        decode(0, 1, 1, 2)
+        relu(0, 1, 2, nc.vector)
+        drain_out(0, 1, 0, nc.scalar)
+        store_out(0, 0, 1)
+        quantize_z(0, 1, 0)
+        drain_out(0, 1, 1, nc.scalar)
+        quantize_z(0, 1, 1)
+        store_out(0, 1, 0)
+        decode(1, 0, 0, 5)
+        interleave_out(0, 0, nc.vector)
+        store_out(0, 1, 1)
+        interleave_out(0, 1, nc.scalar)
+        decode(1, 1, 0, 4)
+        quantize_z(1, 1, 1)
+        quantize_out(0, 0)
+        decode(1, 1, 1, 1)
+        drain_out(1, 1, 0, nc.vector)
+        store_codes(0, 0)
+        decode(1, 0, 1, 6)
+        quantize_out(0, 1)
+        store_out(1, 1, 0)
+        drain_out(1, 1, 1, nc.scalar)
+        store_codes(0, 1)
+        drain_out(1, 0, 1, nc.vector)
+        store_out(1, 1, 1)
+        interleave_out(1, 1, nc.scalar)
+        store_scales(0, nc.sync)
+        drain_out(1, 0, 0, nc.vector)
+        store_out(1, 0, 1)
+        interleave_out(1, 0, nc.vector)
+        store_out(1, 0, 0)
+        quantize_out(1, 1)
+        quantize_out(1, 0)
+        store_codes(1, 1)
+        store_codes(1, 0)
+        store_scales(1, nc.sync)

@@ -43,6 +43,7 @@ def tile_relaxedarchetypalreluautoencoder_x2_kernel(
         ones = keep("ones", [P, P], BF16)
         g_row = keep("g_row", [P, N], BF16)
         ident = keep("ident", [P, P], F32)
+        ident_bf = keep("ident_bf", [P, P], BF16)
         neg_half = keep("neg_half", [P, 4], F32)
         we_scale_raw = keep("we_scale_raw", [P, F], U8)
         c_scale = keep("c_scale", [P, 2, D], U8)
@@ -52,8 +53,8 @@ def tile_relaxedarchetypalreluautoencoder_x2_kernel(
         c_code = keep("c_code", [P, 2, D], U32)
         s_raw = keep("s_raw", [P, 2, 4], BF16)
         s_col = keep("s_col", [P, 8], F32)
-        lg = [keep("lg%d" % i, [P, N], BF16) for i in range(2)]
-        lg_pair = [keep("lgp%d" % j, [P, 2, N], BF16) for j in range(1, 4)]
+        lg = [keep("lg%d" % i, [P, N], BF16) for i in range(4)]
+        lg_pair = [keep("lgp%d" % j, [P, 2, N], BF16) for j in range(2)]
         lam_sb = [keep("lam%d" % G, [P, 4, D], BF16) for G in range(2)]
         x_sb = [keep("x%d" % G, [P, 4, D], BF16) for G in range(2)]
         neg_max = [keep("nmax%d" % i, [P, 1], F32) for i in range(8)]
@@ -79,25 +80,28 @@ def tile_relaxedarchetypalreluautoencoder_x2_kernel(
         z = [[keep("z%d%d" % (G, R), [P, 4, P, 4], BF16) for R in range(2)] for G in range(2)]
         z_code = [[keep("zc%d%d" % (G, R), [P, 4 * P], U32) for R in range(2)] for G in range(2)]
         z_scale = [[keep("zs%d%d" % (G, R), [P, 4 * P], U8) for R in range(2)] for G in range(2)]
-        res = [[keep("res%d%d" % (R, h), [P, 4, HALF], F32) for h in range(2)] for R in range(2)]
-        res_il = [[keep("resi%d%d" % (R, h), [P, HALF, 4], BF16) for h in range(2)] for R in range(2)]
-        res_code = [[keep("resc%d%d" % (R, h), [P, HALF], U32) for h in range(2)] for R in range(2)]
+        res = [keep("res%d" % R, [P, 4, D], F32) for R in range(2)]
+        res_il = [keep("resi%d" % R, [P, D, 4], BF16) for R in range(2)]
+        res_code = [keep("resc%d" % R, [P, D], U32) for R in range(2)]
         res_scale = keep("ress", [P, 2, D], U8)
         g_bank = psum.tile([P, N], BF16, name="g_bank", tag="bank7")
         held = {}
 
         def logit_rows(i):
-            return lg[i][:] if i < 2 else lg_pair[i // 2 - 1][:, i % 2, :]
+            return lg[i][:] if i < 4 else lg_pair[i // 2 - 2][:, i % 2, :]
 
         def load_logits(i):
-            if i < 2:
+            if i < 4:
                 nc.sync.dma_start(out=lg[i][:], in_=logits_v[0, :, i, :])
             else:
                 t = i % 4
-                nc.sync.dma_start(out=lg_pair[i // 2 - 1][:], in_=logits_v[i // 4, :, t : t + 2, :])
+                nc.sync.dma_start(out=lg_pair[i // 2 - 2][:], in_=logits_v[i // 4, :, t : t + 2, :])
 
         def load_rows(tiles, view, G):
             nc.sync.dma_start(out=tiles[G][:], in_=view[G])
+
+        def load_lam(G, j):
+            nc.sync.dma_start(out=lam_sb[G][:, 2 * j : 2 * j + 2, :], in_=lam_v[G, :, 2 * j : 2 * j + 2, :])
 
         def load_g():
             nc.sync.dma_start(out=g_row[0:1, :], in_=g.rearrange("(o n) -> o n", o=1))
@@ -144,6 +148,7 @@ def tile_relaxedarchetypalreluautoencoder_x2_kernel(
 
         def setup_gpsimd():
             make_identity(nc, ident[:])
+            make_identity(nc, ident_bf[:])
             nc.gpsimd.memset(neg_half[:], -0.5)
 
         def copy(eng, out, in_):
@@ -167,8 +172,8 @@ def tile_relaxedarchetypalreluautoencoder_x2_kernel(
         def permute_we(G, eng):
             cols = slice(512 * G, 512 * (G + 1))
             eng.tensor_copy(
-                out=we_code[:, cols].bitcast(I32).rearrange("p (t m) -> p t m", t=4),
-                in_=we_raw[:, cols].bitcast(I32).rearrange("p (m t) -> p t m", t=4),
+                out=(we_code[:, cols] if eng is nc.gpsimd else we_code[:, cols].bitcast(I32)).rearrange("p (t m) -> p t m", t=4),
+                in_=(we_raw[:, cols] if eng is nc.gpsimd else we_raw[:, cols].bitcast(I32)).rearrange("p (m t) -> p t m", t=4),
             )
             eng.tensor_copy(
                 out=we_scale[:, cols].rearrange("p (t m) -> p t m", t=4),
@@ -182,7 +187,7 @@ def tile_relaxedarchetypalreluautoencoder_x2_kernel(
             )
 
         def exponentiate(i):
-            e[i] = keep("e%d" % i, [P, N], F32, "e%d" % (i % 4))
+            e[i] = keep("e%d" % i, [P, N], F32, "e%d" % i)
             nc.scalar.activation(
                 out=e[i][:].rearrange("p (u q e) -> p u q e", u=2, e=2),
                 in_=logit_rows(i).rearrange("p (q u e) -> p u q e", u=2, e=2),
@@ -192,11 +197,11 @@ def tile_relaxedarchetypalreluautoencoder_x2_kernel(
                 accum_out=total[i][:],
             )
 
-        def invert(i):
+        def invert(i, eng):
             nc.vector.reciprocal(out=inv_total[i][:], in_=total[i][:])
 
         def weigh(i):
-            pg[i] = keep("pg%d" % i, [P, N], BF16, "pg%d" % (i % 4))
+            pg[i] = keep("pg%d" % i, [P, N], BF16, "pg%d" % i)
             nc.vector.scalar_tensor_tensor(
                 out=pg[i][:], in0=e[i][:], scalar=inv_total[i][:], in1=g_bank[:], op0=ALU.mult, op1=ALU.mult
             )
@@ -278,6 +283,22 @@ def tile_relaxedarchetypalreluautoencoder_x2_kernel(
                 eng, out=dic_il[G][h][:], in_=dic[G][:, :, HALF * h : HALF * (h + 1)].rearrange("p t d -> p d t")
             )
 
+        def weave_dic(G, h, k):
+            b = psum.tile([P, 4 * HALF], BF16, name="wv%d%d" % (G, h), tag="bank%d" % k)
+            held["wv", G, h] = b
+            for j in range(2):
+                d0 = HALF * h + P * j
+                nc.tensor.matmul(
+                    out=b[:, 512 * j : 512 * (j + 1)],
+                    lhsT=ident_bf[:],
+                    rhs=dic[G][:, :, d0 : d0 + P].rearrange("p t d -> p d t"),
+                    start=True,
+                    stop=True,
+                )
+
+        def drain_dic(G, h, eng):
+            copy(eng, out=dic_il[G][h][:].rearrange("p d t -> p (d t)"), in_=held["wv", G, h][:])
+
         def quantize_dic(G, h):
             quantize(dic_code[G][h][:], dic_scale[G][h][:], dic_il[G][h][:].rearrange("p d t -> p (d t)"))
 
@@ -332,263 +353,272 @@ def tile_relaxedarchetypalreluautoencoder_x2_kernel(
                 z[G][R][:, 2 * j : 2 * j + 2].rearrange("p c m t -> p (c m t)"),
             )
 
-        def decode(R, h, j, k):
-            b = bank("o%d%d%d" % (R, h, j), k)
-            held["o", R, h, j] = b
-            for c in range(2):
-                rows = slice(P * (2 * j + c), P * (2 * j + c + 1))
+        def decode(R, q, k):
+            b = bank("o%d%d" % (R, q), k)
+            held["o", R, q] = b
+            h, cols = q // 2, slice(P * (q % 2), P * (q % 2 + 1))
+            for t in range(4):
+                rows = slice(P * t, P * (t + 1))
                 for G in range(2):
                     nc.tensor.matmul_mx(
-                        out=b[:, HALF * c : HALF * (c + 1)],
+                        out=b[:, rows],
                         lhsT=z_code[G][R][:, rows].bitcast(FP8X4),
                         lhsT_scale=z_scale[G][R][:, rows],
-                        rhs=dic_code[G][h][:].bitcast(FP8X4),
-                        rhs_scale=dic_scale[G][h][:],
+                        rhs=dic_code[G][h][:, cols].bitcast(FP8X4),
+                        rhs_scale=dic_scale[G][h][:, cols],
                         start=(G == 0),
                         stop=(G == 1),
                     )
 
-        def drain_out(R, h, j, eng):
-            copy(
-                eng, out=res[R][h][:, 2 * j : 2 * j + 2, :], in_=held["o", R, h, j][:].rearrange("p (c d) -> p c d", c=2)
+        def drain_out(R, q, eng):
+            copy(eng, out=res[R][:, :, P * q : P * (q + 1)], in_=held["o", R, q][:].rearrange("p (t d) -> p t d", t=4))
+
+        def round_out(R, q, eng, from_bank=False):
+            cols = slice(P * q, P * (q + 1))
+            if from_bank:
+                sums = held["o", R, q][:].rearrange("p (t d) -> p d t", t=4)
+            else:
+                sums = res[R][:, :, cols].rearrange("p t d -> p d t")
+            copy(eng, out=res_il[R][:, cols, :], in_=sums)
+
+        def store_out(R, q, n):
+            cols = slice(P * q, P * (q + n))
+            nc.sync.dma_start(out=out_v[R, :, :, cols], in_=res[R][:, :, cols])
+
+        def quantize_out(R, q, n):
+            cols = slice(P * q, P * (q + n))
+            quantize(res_code[R][:, cols], res_scale[:, R, cols], res_il[R][:, cols, :].rearrange("p d t -> p (d t)"))
+
+        def store_codes(R, q, n, eng):
+            cols = slice(P * q, P * (q + n))
+            eng.dma_start(
+                out=out_1[R].rearrange("p d t -> p (d t)").bitcast(I32)[:, cols], in_=res_code[R][:, cols].bitcast(I32)
             )
 
-        def store_out(R, h, j):
-            nc.sync.dma_start(
-                out=out_v[R, :, 2 * j : 2 * j + 2, HALF * h : HALF * (h + 1)], in_=res[R][h][:, 2 * j : 2 * j + 2, :]
-            )
-
-        def interleave_out(R, h, eng):
-            copy(eng, out=res_il[R][h][:], in_=res[R][h][:].rearrange("p t d -> p d t"))
-
-        def quantize_out(R, h):
-            quantize(
-                res_code[R][h][:],
-                res_scale[:, R, HALF * h : HALF * (h + 1)],
-                res_il[R][h][:].rearrange("p d t -> p (d t)"),
-            )
-
-        def store_codes(R, h):
-            nc.sync.dma_start(
-                out=out_1[R].rearrange("p d t -> p (d t)").bitcast(I32)[:, HALF * h : HALF * (h + 1)],
-                in_=res_code[R][h][:].bitcast(I32),
-            )
-
-        def store_scales(R, eng):
+        def store_scales(eng):
             for q in range(4):
                 eng.dma_start(
-                    out=out_2[R, 4 * q : 4 * q + 4, :].bitcast(I32),
-                    in_=res_scale[32 * q : 32 * q + 4, R, :].bitcast(I32),
+                    out=out_2[:, 4 * q : 4 * q + 4, :].rearrange("g r d -> r g d").bitcast(I32),
+                    in_=res_scale[32 * q : 32 * q + 4, :, :].bitcast(I32),
                 )
 
         load_logits(0)
         setup_zeros()
-        load_logits(1)
+        load_s()
         setup_vector()
         setup_scalar()
-        load_logits(2)
+        load_logits(1)
         setup_gpsimd()
         load_g()
-        load_logits(4)
-        load_rows(lam_sb, lam_v, 0)
+        load_logits(2)
+        load_we()
         load_we_scales()
         row_max(0)
+        widen_s()
+        load_logits(3)
+        load_lam(0, 0)
+        spread_g()
         row_max(1)
         exponentiate(0)
         load_rows(x_sb, x_v, 0)
         row_max(2)
-        load_s()
-        spread_g()
         exponentiate(1)
-        invert(0)
-        row_max(3)
-        load_rows(lam_sb, lam_v, 1)
-        exponentiate(2)
-        row_max(4)
+        invert(0, nc.vector)
+        load_lam(0, 1)
         weigh(0)
+        load_logits(4)
         load_rows(x_sb, x_v, 1)
-        load_we()
         load_c_scales()
-        square_sum(2)
-        exponentiate(3)
-        invert(1)
-        row_max(5)
-        turn_x(0, 0, 0)
-        load_logits(6)
-        widen_s()
-        invert(2)
+        permute_we(1, nc.gpsimd)
+        exponentiate(2)
+        invert(1, nc.vector)
+        row_max(3)
+        turn_pg(0, 0)
         weigh(1)
-        square_sum(3)
-        load_c()
-        square_sum(1)
-        invert(3)
-        drain_x(0, 0, nc.vector)
-        turn_pg(1, 1)
         square_sum(0)
-        weigh(3)
-        turn_x(1, 0, 2)
-        exponentiate(4)
-        lam_gain(0)
-        turn_x(1, 1, 3)
+        exponentiate(3)
+        load_lam(1, 1)
+        invert(2, nc.vector)
+        drain_pg(0, nc.vector)
+        turn_pg(1, 1)
+        load_logits(6)
+        turn_x(0, 1, 2)
+        square_sum(1)
+        invert(3, nc.vector)
         weigh(2)
-        square_sum(7)
-        turn_pg(3, 4)
-        exponentiate(5)
-        permute_we(0, nc.vector)
-        turn_pg(0, 5)
-        turn_x(0, 1, 6)
-        scale_lam(2, nc.gpsimd)
-        invert(4)
-        row_max(6)
-        drain_pg(3, nc.scalar)
-        turn_pg(2, 0)
-        permute_we(1, nc.vector)
-        exponentiate(6)
-        quantize_x(0, 0)
-        invert(5)
-        scale_lam(3, nc.gpsimd)
-        weigh(4)
-        square_sum(6)
-        scale_lam(0, nc.gpsimd)
-        drain_x(1, 1, nc.scalar)
-        row_max(7)
-        turn_pg(4, 4)
+        turn_x(0, 0, 3)
+        square_sum(2)
+        load_lam(1, 0)
+        permute_we(0, nc.gpsimd)
+        square_sum(3)
+        row_max(4)
+        turn_pg(2, 4)
+        load_c()
         drain_pg(1, nc.scalar)
-        scale_lam(1, nc.gpsimd)
-        encode(1, 0, 1, 3)
-        drain_x(0, 1, nc.vector)
-        drain_pg(0, nc.scalar)
-        quantize_pg(1)
-        drain_pg(4, nc.scalar)
-        weigh(5)
-        archetypes(1, 1)
+        turn_x(1, 0, 5)
+        row_max(5)
+        exponentiate(4)
+        weigh(3)
+        turn_x(1, 1, 6)
         drain_pg(2, nc.scalar)
-        drain_x(1, 0, nc.scalar)
-        quantize_x(1, 1)
-        encode(1, 0, 0, 6)
-        quantize_pg(3)
+        invert(4, nc.vector)
+        drain_x(0, 0, nc.vector)
+        turn_pg(3, 0)
+        drain_x(0, 1, nc.scalar)
+        weigh(4)
         square_sum(5)
+        lam_gain(0)
+        exponentiate(5)
+        row_max(6)
+        turn_pg(4, 1)
+        drain_x(1, 0, nc.vector)
+        drain_pg(3, nc.scalar)
+        invert(5, nc.vector)
         quantize_x(0, 1)
-        invert(6)
-        relu(1, 0, 0, nc.vector)
-        square_sum(4)
-        encode(0, 0, 3, 5)
-        encode(0, 0, 1, 4)
-        quantize_pg(0)
-        relu(1, 0, 1, nc.scalar)
-        encode(1, 0, 3, 0)
-        quantize_pg(2)
-        archetypes(3, 2)
-        quantize_pg(4)
-        relu(0, 0, 3, nc.scalar)
+        square_sum(7)
         quantize_x(1, 0)
-        archetypes(2, 6)
-        weigh(6)
-        lam_gain(1)
-        exponentiate(7)
-        encode(0, 0, 2, 3)
-        dictionary(3)
-        relu(0, 0, 1, nc.scalar)
-        turn_pg(6, 5)
-        invert(7)
-        relu(1, 0, 3, nc.scalar)
-        quantize_z(1, 0, 0)
-        turn_pg(5, 2)
-        weigh(7)
-        scale_lam(6, nc.gpsimd)
-        encode(0, 0, 0, 4)
-        drain_pg(6, nc.scalar)
-        archetypes(0, 0)
-        scale_lam(5, nc.gpsimd)
-        drain_pg(5, nc.scalar)
-        dictionary(1)
-        turn_pg(7, 5)
-        relu(0, 0, 2, nc.scalar)
-        scale_lam(4, nc.gpsimd)
-        encode(1, 0, 2, 2)
-        dictionary(2)
-        relu(0, 0, 0, nc.scalar)
-        archetypes(4, 1)
-        drain_pg(7, nc.vector)
-        scale_lam(7, nc.gpsimd)
-        relu(1, 0, 2, nc.scalar)
-        encode(0, 1, 2, 3)
-        dictionary(0)
-        encode(0, 1, 0, 6)
-        encode(0, 1, 3, 4)
-        quantize_pg(7)
-        interleave_dic(0, 0, nc.scalar)
-        encode(1, 1, 3, 5)
-        dictionary(4)
-        archetypes(7, 2)
-        quantize_pg(6)
-        quantize_pg(5)
-        interleave_dic(0, 1, nc.scalar)
-        dictionary(7)
-        archetypes(5, 0)
-        quantize_z(0, 0, 0)
-        archetypes(6, 1)
-        quantize_z(0, 0, 1)
-        relu(0, 1, 3, nc.scalar)
-        dictionary(5)
-        encode(1, 1, 1, 2)
-        relu(1, 1, 3, nc.scalar)
-        encode(0, 1, 1, 4)
-        dictionary(6)
-        encode(1, 1, 2, 0)
-        relu(0, 1, 0, nc.scalar)
-        quantize_dic(0, 0)
+        encode(1, 0, 2, 4)
+        quantize_x(0, 0)
+        drain_pg(4, nc.scalar)
+        quantize_pg(1)
+        quantize_pg(0)
+        encode(0, 0, 0, 3)
+        exponentiate(6)
+        quantize_pg(4)
+        encode(0, 0, 1, 2)
+        row_max(7)
+        scale_lam(1, nc.gpsimd)
+        square_sum(4)
         encode(1, 1, 0, 5)
-        interleave_dic(1, 0, nc.vector)
-        relu(1, 1, 2, nc.scalar)
-        quantize_dic(0, 1)
-        interleave_dic(1, 1, nc.scalar)
-        quantize_dic(1, 0)
-        quantize_z(1, 0, 1)
-        decode(0, 0, 0, 1)
-        relu(1, 1, 1, nc.vector)
+        invert(6, nc.vector)
+        quantize_pg(3)
+        archetypes(1, 0)
+        quantize_pg(2)
+        relu(1, 0, 2, nc.scalar)
+        scale_lam(0, nc.gpsimd)
+        relu(0, 0, 0, nc.vector)
+        archetypes(4, 1)
+        drain_x(1, 1, nc.scalar)
+        dictionary(1)
+        encode(0, 1, 1, 4)
+        scale_lam(2, nc.gpsimd)
+        square_sum(6)
+        encode(0, 0, 2, 3)
+        weigh(5)
+        archetypes(0, 6)
+        relu(0, 0, 1, nc.scalar)
+        lam_gain(1)
+        archetypes(3, 0)
+        relu(0, 0, 2, nc.scalar)
+        weigh(6)
+        archetypes(2, 2)
         relu(1, 1, 0, nc.scalar)
-        decode(0, 0, 1, 6)
-        quantize_dic(1, 1)
-        relu(0, 1, 1, nc.vector)
-        drain_out(0, 0, 0, nc.scalar)
-        decode(0, 1, 0, 0)
-        quantize_z(1, 1, 0)
-        drain_out(0, 0, 1, nc.scalar)
-        store_out(0, 0, 0)
-        decode(0, 1, 1, 2)
-        relu(0, 1, 2, nc.vector)
-        drain_out(0, 1, 0, nc.scalar)
-        store_out(0, 0, 1)
+        turn_pg(5, 3)
+        exponentiate(7)
+        scale_lam(3, nc.gpsimd)
+        dictionary(0)
+        turn_pg(6, 5)
+        dictionary(2)
+        encode(1, 1, 1, 6)
+        scale_lam(6, nc.gpsimd)
+        drain_pg(5, nc.scalar)
+        invert(7, nc.vector)
+        dictionary(3)
+        encode(1, 0, 1, 2)
+        scale_lam(4, nc.gpsimd)
+        relu(1, 1, 1, nc.scalar)
+        encode(1, 0, 3, 3)
+        weigh(7)
+        encode(1, 0, 0, 0)
+        drain_pg(6, nc.scalar)
+        scale_lam(5, nc.gpsimd)
+        weave_dic(0, 1, 6)
+        relu(1, 0, 1, nc.scalar)
+        quantize_pg(5)
+        turn_pg(7, 5)
+        quantize_pg(6)
+        relu(1, 0, 3, nc.scalar)
+        archetypes(5, 2)
+        dictionary(4)
+        scale_lam(7, nc.gpsimd)
+        drain_pg(7, nc.scalar)
+        encode(0, 0, 3, 3)
+        quantize_x(1, 1)
+        drain_dic(0, 1, nc.scalar)
+        archetypes(6, 1)
+        quantize_pg(7)
+        dictionary(5)
+        relu(0, 0, 3, nc.scalar)
+        encode(0, 1, 0, 5)
+        archetypes(7, 6)
+        dictionary(6)
+        relu(0, 1, 0, nc.scalar)
+        weave_dic(0, 0, 2)
+        dictionary(7)
+        relu(1, 0, 0, nc.scalar)
+        encode(1, 1, 3, 3)
+        quantize_z(0, 0, 1)
+        relu(0, 1, 1, nc.scalar)
+        weave_dic(1, 0, 1)
+        quantize_z(1, 0, 1)
+        drain_dic(0, 0, nc.scalar)
+        quantize_z(0, 0, 0)
+        weave_dic(1, 1, 5)
         quantize_z(0, 1, 0)
-        drain_out(0, 1, 1, nc.scalar)
-        quantize_z(0, 1, 1)
-        store_out(0, 1, 0)
-        decode(1, 0, 0, 5)
-        interleave_out(0, 0, nc.vector)
-        store_out(0, 1, 1)
-        interleave_out(0, 1, nc.scalar)
-        decode(1, 1, 0, 4)
+        drain_dic(1, 0, nc.scalar)
+        quantize_dic(0, 0)
+        quantize_z(1, 0, 0)
+        encode(1, 1, 2, 6)
+        relu(1, 1, 3, nc.scalar)
+        quantize_dic(1, 0)
+        encode(0, 1, 3, 0)
+        drain_dic(1, 1, nc.vector)
+        encode(0, 1, 2, 4)
+        relu(1, 1, 2, nc.scalar)
+        decode(0, 0, 2)
+        quantize_dic(0, 1)
+        relu(0, 1, 3, nc.scalar)
+        quantize_dic(1, 1)
+        decode(0, 1, 1)
+        quantize_z(1, 1, 0)
+        drain_out(0, 0, nc.scalar)
+        relu(0, 1, 2, nc.vector)
+        decode(0, 3, 3)
+        drain_out(0, 1, nc.scalar)
         quantize_z(1, 1, 1)
-        quantize_out(0, 0)
-        decode(1, 1, 1, 1)
-        drain_out(1, 1, 0, nc.vector)
-        store_codes(0, 0)
-        decode(1, 0, 1, 6)
-        quantize_out(0, 1)
-        store_out(1, 1, 0)
-        drain_out(1, 1, 1, nc.scalar)
-        store_codes(0, 1)
-        drain_out(1, 0, 1, nc.vector)
-        store_out(1, 1, 1)
-        interleave_out(1, 1, nc.scalar)
-        store_scales(0, nc.sync)
-        drain_out(1, 0, 0, nc.vector)
-        store_out(1, 0, 1)
-        interleave_out(1, 0, nc.vector)
-        store_out(1, 0, 0)
-        quantize_out(1, 1)
-        quantize_out(1, 0)
-        store_codes(1, 1)
-        store_codes(1, 0)
-        store_scales(1, nc.sync)
+        decode(0, 2, 5)
+        quantize_z(0, 1, 1)
+        drain_out(0, 3, nc.scalar)
+        store_out(0, 0, 2)
+        round_out(0, 1, nc.vector)
+        decode(1, 2, 6)
+        round_out(0, 0, nc.vector)
+        drain_out(0, 2, nc.scalar)
+        round_out(0, 3, nc.vector)
+        decode(1, 3, 0)
+        store_out(0, 2, 2)
+        round_out(0, 2, nc.vector)
+        drain_out(1, 2, nc.scalar)
+        decode(1, 1, 2)
+        quantize_out(0, 0, 2)
+        round_out(1, 2, nc.scalar, True)
+        round_out(1, 3, nc.vector, True)
+        store_codes(0, 0, 2, nc.sync)
+        decode(1, 0, 4)
+        store_out(1, 2, 1)
+        quantize_out(1, 2, 1)
+        drain_out(1, 3, nc.scalar)
+        quantize_out(1, 3, 1)
+        drain_out(1, 1, nc.vector)
+        store_codes(1, 2, 1, nc.scalar)
+        store_out(1, 3, 1)
+        store_codes(1, 3, 1, nc.scalar)
+        drain_out(1, 0, nc.vector)
+        round_out(1, 1, nc.vector)
+        store_out(1, 0, 2)
+        round_out(1, 0, nc.vector)
+        quantize_out(0, 2, 2)
+        quantize_out(1, 0, 2)
+        store_codes(0, 2, 2, nc.sync)
+        store_codes(1, 0, 2, nc.sync)
+        store_scales(nc.sync)

@@ -43,7 +43,6 @@ def tile_relaxedarchetypalreluautoencoder_x2_kernel(
         ones = keep("ones", [P, P], BF16)
         g_row = keep("g_row", [P, N], BF16)
         ident = keep("ident", [P, P], F32)
-        ident_bf = keep("ident_bf", [P, P], BF16)
         neg_half = keep("neg_half", [P, 4], F32)
         we_scale_raw = keep("we_scale_raw", [P, F], U8)
         c_scale = keep("c_scale", [P, 2, D], U8)
@@ -148,7 +147,6 @@ def tile_relaxedarchetypalreluautoencoder_x2_kernel(
 
         def setup_gpsimd():
             make_identity(nc, ident[:])
-            make_identity(nc, ident_bf[:])
             nc.gpsimd.memset(neg_half[:], -0.5)
 
         def copy(eng, out, in_):
@@ -283,22 +281,6 @@ def tile_relaxedarchetypalreluautoencoder_x2_kernel(
                 eng, out=dic_il[G][h][:], in_=dic[G][:, :, HALF * h : HALF * (h + 1)].rearrange("p t d -> p d t")
             )
 
-        def weave_dic(G, h, k):
-            b = psum.tile([P, 4 * HALF], BF16, name="wv%d%d" % (G, h), tag="bank%d" % k)
-            held["wv", G, h] = b
-            for j in range(2):
-                d0 = HALF * h + P * j
-                nc.tensor.matmul(
-                    out=b[:, 512 * j : 512 * (j + 1)],
-                    lhsT=ident_bf[:],
-                    rhs=dic[G][:, :, d0 : d0 + P].rearrange("p t d -> p d t"),
-                    start=True,
-                    stop=True,
-                )
-
-        def drain_dic(G, h, eng):
-            copy(eng, out=dic_il[G][h][:].rearrange("p d t -> p (d t)"), in_=held["wv", G, h][:])
-
         def quantize_dic(G, h):
             quantize(dic_code[G][h][:], dic_scale[G][h][:], dic_il[G][h][:].rearrange("p d t -> p (d t)"))
 
@@ -402,223 +384,219 @@ def tile_relaxedarchetypalreluautoencoder_x2_kernel(
                     in_=res_scale[32 * q : 32 * q + 4, :, :].bitcast(I32),
                 )
 
-        load_logits(0)
+        load_lam(0, 1)
         setup_zeros()
-        load_s()
+        load_logits(0)
         setup_vector()
         setup_scalar()
-        load_logits(1)
+        load_s()
         setup_gpsimd()
         load_g()
         load_logits(2)
-        load_we()
+        load_logits(3)
+        load_logits(1)
+        load_lam(0, 0)
+        load_logits(4)
+        square_sum(2)
         load_we_scales()
         row_max(0)
         widen_s()
-        load_logits(3)
-        load_lam(0, 0)
+        square_sum(3)
         spread_g()
-        row_max(1)
+        row_max(2)
         exponentiate(0)
         load_rows(x_sb, x_v, 0)
-        row_max(2)
-        exponentiate(1)
-        invert(0, nc.vector)
-        load_lam(0, 1)
-        weigh(0)
-        load_logits(4)
-        load_rows(x_sb, x_v, 1)
-        load_c_scales()
-        permute_we(1, nc.gpsimd)
-        exponentiate(2)
-        invert(1, nc.vector)
         row_max(3)
-        turn_pg(0, 0)
-        weigh(1)
-        square_sum(0)
-        exponentiate(3)
-        load_lam(1, 1)
-        invert(2, nc.vector)
-        drain_pg(0, nc.vector)
-        turn_pg(1, 1)
-        load_logits(6)
-        turn_x(0, 1, 2)
-        square_sum(1)
-        invert(3, nc.vector)
-        weigh(2)
-        turn_x(0, 0, 3)
-        square_sum(2)
         load_lam(1, 0)
-        permute_we(0, nc.gpsimd)
-        square_sum(3)
-        row_max(4)
-        turn_pg(2, 4)
+        exponentiate(2)
+        invert(0, nc.vector)
+        row_max(1)
+        load_logits(6)
+        weigh(0)
+        square_sum(1)
         load_c()
-        drain_pg(1, nc.scalar)
-        turn_x(1, 0, 5)
-        row_max(5)
-        exponentiate(4)
-        weigh(3)
-        turn_x(1, 1, 6)
-        drain_pg(2, nc.scalar)
-        invert(4, nc.vector)
-        drain_x(0, 0, nc.vector)
-        turn_pg(3, 0)
-        drain_x(0, 1, nc.scalar)
-        weigh(4)
-        square_sum(5)
+        load_lam(1, 1)
+        load_rows(x_sb, x_v, 1)
+        square_sum(0)
+        load_we()
+        load_c_scales()
+        invert(2, nc.vector)
+        row_max(4)
+        turn_pg(0, 0)
+        exponentiate(3)
         lam_gain(0)
+        weigh(2)
+        turn_x(0, 1, 1)
+        exponentiate(1)
+        invert(3, nc.vector)
+        row_max(5)
+        turn_pg(2, 2)
+        scale_lam(1, nc.gpsimd)
+        weigh(3)
         exponentiate(5)
+        scale_lam(2, nc.gpsimd)
+        invert(1, nc.vector)
         row_max(6)
-        turn_pg(4, 1)
-        drain_x(1, 0, nc.vector)
-        drain_pg(3, nc.scalar)
+        turn_pg(3, 3)
+        drain_pg(2, nc.scalar)
+        scale_lam(0, nc.gpsimd)
+        turn_x(0, 0, 4)
+        row_max(7)
+        drain_x(0, 1, nc.scalar)
+        weigh(1)
+        square_sum(5)
+        turn_x(1, 1, 5)
+        drain_pg(0, nc.scalar)
         invert(5, nc.vector)
+        quantize_pg(2)
+        square_sum(4)
+        turn_x(1, 0, 6)
+        quantize_pg(0)
         quantize_x(0, 1)
+        drain_pg(3, nc.scalar)
+        archetypes(0, 2)
+        permute_we(0, nc.vector)
+        square_sum(6)
+        quantize_pg(3)
         square_sum(7)
+        permute_we(1, nc.vector)
+        archetypes(2, 1)
+        exponentiate(4)
+        weigh(5)
+        lam_gain(1)
+        turn_pg(1, 0)
+        exponentiate(6)
+        invert(4, nc.vector)
+        dictionary(0)
+        turn_pg(5, 3)
+        scale_lam(3, nc.gpsimd)
+        weigh(4)
+        encode(0, 0, 2, 2)
+        exponentiate(7)
+        scale_lam(6, nc.gpsimd)
+        invert(6, nc.vector)
+        dictionary(2)
+        drain_pg(1, nc.scalar)
+        scale_lam(7, nc.gpsimd)
+        invert(7, nc.vector)
+        weigh(6)
+        encode(1, 0, 3, 1)
+        relu(0, 0, 2, nc.scalar)
+        scale_lam(5, nc.gpsimd)
+        archetypes(3, 0)
+        drain_x(1, 1, nc.scalar)
+        weigh(7)
+        scale_lam(4, nc.gpsimd)
+        drain_x(1, 0, nc.scalar)
+        encode(0, 0, 3, 2)
+        drain_pg(5, nc.scalar)
+        turn_pg(4, 5)
+        quantize_pg(1)
+        drain_x(0, 0, nc.scalar)
+        turn_pg(6, 6)
         quantize_x(1, 0)
-        encode(1, 0, 2, 4)
+        turn_pg(7, 3)
+        quantize_pg(5)
+        relu(0, 0, 3, nc.scalar)
+        archetypes(1, 4)
+        quantize_x(1, 1)
         quantize_x(0, 0)
         drain_pg(4, nc.scalar)
-        quantize_pg(1)
-        quantize_pg(0)
-        encode(0, 0, 0, 3)
-        exponentiate(6)
-        quantize_pg(4)
-        encode(0, 0, 1, 2)
-        row_max(7)
-        scale_lam(1, nc.gpsimd)
-        square_sum(4)
-        encode(1, 1, 0, 5)
-        invert(6, nc.vector)
-        quantize_pg(3)
-        archetypes(1, 0)
-        quantize_pg(2)
-        relu(1, 0, 2, nc.scalar)
-        scale_lam(0, nc.gpsimd)
-        relu(0, 0, 0, nc.vector)
-        archetypes(4, 1)
-        drain_x(1, 1, nc.scalar)
-        dictionary(1)
-        encode(0, 1, 1, 4)
-        scale_lam(2, nc.gpsimd)
-        square_sum(6)
-        encode(0, 0, 2, 3)
-        weigh(5)
-        archetypes(0, 6)
-        relu(0, 0, 1, nc.scalar)
-        lam_gain(1)
-        archetypes(3, 0)
-        relu(0, 0, 2, nc.scalar)
-        weigh(6)
-        archetypes(2, 2)
-        relu(1, 1, 0, nc.scalar)
-        turn_pg(5, 3)
-        exponentiate(7)
-        scale_lam(3, nc.gpsimd)
-        dictionary(0)
-        turn_pg(6, 5)
-        dictionary(2)
-        encode(1, 1, 1, 6)
-        scale_lam(6, nc.gpsimd)
-        drain_pg(5, nc.scalar)
-        invert(7, nc.vector)
         dictionary(3)
-        encode(1, 0, 1, 2)
-        scale_lam(4, nc.gpsimd)
-        relu(1, 1, 1, nc.scalar)
-        encode(1, 0, 3, 3)
-        weigh(7)
-        encode(1, 0, 0, 0)
-        drain_pg(6, nc.scalar)
-        scale_lam(5, nc.gpsimd)
-        weave_dic(0, 1, 6)
-        relu(1, 0, 1, nc.scalar)
-        quantize_pg(5)
-        turn_pg(7, 5)
-        quantize_pg(6)
-        relu(1, 0, 3, nc.scalar)
-        archetypes(5, 2)
-        dictionary(4)
-        scale_lam(7, nc.gpsimd)
+        encode(1, 0, 2, 2)
         drain_pg(7, nc.scalar)
-        encode(0, 0, 3, 3)
-        quantize_x(1, 1)
-        drain_dic(0, 1, nc.scalar)
-        archetypes(6, 1)
+        encode(1, 0, 0, 5)
+        dictionary(1)
+        archetypes(5, 0)
+        drain_pg(6, nc.scalar)
         quantize_pg(7)
-        dictionary(5)
-        relu(0, 0, 3, nc.scalar)
-        encode(0, 1, 0, 5)
-        archetypes(7, 6)
-        dictionary(6)
-        relu(0, 1, 0, nc.scalar)
-        weave_dic(0, 0, 2)
-        dictionary(7)
+        encode(0, 1, 0, 3)
+        relu(1, 0, 3, nc.scalar)
+        interleave_dic(0, 0, nc.vector)
+        encode(1, 0, 1, 4)
+        encode(0, 1, 1, 6)
         relu(1, 0, 0, nc.scalar)
-        encode(1, 1, 3, 3)
-        quantize_z(0, 0, 1)
-        relu(0, 1, 1, nc.scalar)
-        weave_dic(1, 0, 1)
-        quantize_z(1, 0, 1)
-        drain_dic(0, 0, nc.scalar)
-        quantize_z(0, 0, 0)
-        weave_dic(1, 1, 5)
-        quantize_z(0, 1, 0)
-        drain_dic(1, 0, nc.scalar)
+        quantize_pg(6)
+        archetypes(7, 1)
         quantize_dic(0, 0)
+        relu(0, 1, 0, nc.scalar)
+        encode(1, 1, 0, 5)
+        quantize_pg(4)
+        dictionary(5)
+        interleave_dic(0, 1, nc.gpsimd)
+        relu(0, 1, 1, nc.scalar)
+        archetypes(6, 3)
+        dictionary(7)
+        relu(1, 0, 2, nc.scalar)
+        archetypes(4, 0)
+        dictionary(6)
+        relu(1, 0, 1, nc.scalar)
+        encode(1, 1, 1, 6)
+        encode(0, 1, 2, 1)
+        dictionary(4)
+        relu(1, 1, 0, nc.scalar)
+        encode(0, 0, 1, 2)
+        encode(1, 1, 2, 3)
+        quantize_z(0, 0, 1)
+        relu(0, 1, 2, nc.scalar)
+        encode(0, 1, 3, 4)
+        interleave_dic(1, 0, nc.vector)
+        encode(0, 0, 0, 0)
+        relu(0, 0, 1, nc.scalar)
+        encode(1, 1, 3, 5)
+        quantize_z(1, 0, 1)
+        relu(0, 0, 0, nc.scalar)
         quantize_z(1, 0, 0)
-        encode(1, 1, 2, 6)
-        relu(1, 1, 3, nc.scalar)
         quantize_dic(1, 0)
-        encode(0, 1, 3, 0)
-        drain_dic(1, 1, nc.vector)
-        encode(0, 1, 2, 4)
         relu(1, 1, 2, nc.scalar)
-        decode(0, 0, 2)
+        quantize_z(0, 0, 0)
+        interleave_dic(1, 1, nc.vector)
+        relu(1, 1, 3, nc.scalar)
+        decode(0, 0, 1)
+        relu(1, 1, 1, nc.scalar)
         quantize_dic(0, 1)
-        relu(0, 1, 3, nc.scalar)
+        decode(0, 1, 2)
         quantize_dic(1, 1)
-        decode(0, 1, 1)
-        quantize_z(1, 1, 0)
-        drain_out(0, 0, nc.scalar)
-        relu(0, 1, 2, nc.vector)
-        decode(0, 3, 3)
-        drain_out(0, 1, nc.scalar)
+        relu(0, 1, 3, nc.scalar)
         quantize_z(1, 1, 1)
-        decode(0, 2, 5)
-        quantize_z(0, 1, 1)
-        drain_out(0, 3, nc.scalar)
+        decode(0, 2, 0)
+        drain_out(0, 0, nc.vector)
+        drain_out(0, 1, nc.scalar)
+        decode(0, 3, 3)
+        quantize_z(1, 1, 0)
         store_out(0, 0, 2)
-        round_out(0, 1, nc.vector)
-        decode(1, 2, 6)
-        round_out(0, 0, nc.vector)
         drain_out(0, 2, nc.scalar)
-        round_out(0, 3, nc.vector)
-        decode(1, 3, 0)
+        quantize_z(0, 1, 1)
+        quantize_z(0, 1, 0)
+        drain_out(0, 3, nc.scalar)
+        round_out(0, 1, nc.vector)
+        decode(1, 2, 5)
+        round_out(0, 0, nc.vector)
         store_out(0, 2, 2)
         round_out(0, 2, nc.vector)
-        drain_out(1, 2, nc.scalar)
-        decode(1, 1, 2)
+        decode(1, 1, 6)
         quantize_out(0, 0, 2)
-        round_out(1, 2, nc.scalar, True)
-        round_out(1, 3, nc.vector, True)
-        store_codes(0, 0, 2, nc.sync)
+        drain_out(1, 2, nc.scalar)
+        round_out(0, 3, nc.vector)
         decode(1, 0, 4)
+        store_codes(0, 0, 2, nc.sync)
+        round_out(1, 2, nc.scalar, True)
         store_out(1, 2, 1)
-        quantize_out(1, 2, 1)
-        drain_out(1, 3, nc.scalar)
-        quantize_out(1, 3, 1)
-        drain_out(1, 1, nc.vector)
-        store_codes(1, 2, 1, nc.scalar)
-        store_out(1, 3, 1)
-        store_codes(1, 3, 1, nc.scalar)
-        drain_out(1, 0, nc.vector)
-        round_out(1, 1, nc.vector)
-        store_out(1, 0, 2)
-        round_out(1, 0, nc.vector)
         quantize_out(0, 2, 2)
-        quantize_out(1, 0, 2)
+        decode(1, 3, 1)
+        quantize_out(1, 2, 1)
+        drain_out(1, 0, nc.scalar)
         store_codes(0, 2, 2, nc.sync)
+        drain_out(1, 1, nc.vector)
+        store_codes(1, 2, 1, nc.sync)
+        drain_out(1, 3, nc.scalar)
+        store_out(1, 0, 2)
+        round_out(1, 1, nc.vector)
+        store_out(1, 3, 1)
+        round_out(1, 0, nc.vector)
+        round_out(1, 3, nc.vector)
+        quantize_out(1, 0, 2)
+        quantize_out(1, 3, 1)
         store_codes(1, 0, 2, nc.sync)
-        store_scales(nc.sync)
+        store_codes(1, 3, 1, nc.scalar)
+        store_scales(nc.scalar)

@@ -71,8 +71,8 @@ def tile_relaxedarchetypalreluautoencoder_x2_kernel(
         lam_term = [keep("lamt%d" % i, [P, D], F32) for i in range(8)]
         dic = [keep("dic%d" % G, [P, 4, D], BF16) for G in range(2)]
         dic_il = [[keep("dici%d%d" % (G, h), [P, HALF, 4], BF16) for h in range(2)] for G in range(2)]
-        dic_code = [[keep("dicc%d%d" % (G, h), [P, HALF], U32) for h in range(2)] for G in range(2)]
-        dic_scale = [[keep("dics%d%d" % (G, h), [P, HALF], U8) for h in range(2)] for G in range(2)]
+        dic_code = [keep("dicc%d" % G, [P, D], U32) for G in range(2)]
+        dic_scale = [keep("dics%d" % G, [P, D], U8) for G in range(2)]
         x_t = [keep("xt%d" % R, [P, 4, P, 4], BF16) for R in range(2)]
         x_code = [keep("xc%d" % R, [P, 4 * P], U32) for R in range(2)]
         x_scale = [keep("xs%d" % R, [P, 4 * P], U8) for R in range(2)]
@@ -282,7 +282,8 @@ def tile_relaxedarchetypalreluautoencoder_x2_kernel(
             )
 
         def quantize_dic(G, h):
-            quantize(dic_code[G][h][:], dic_scale[G][h][:], dic_il[G][h][:].rearrange("p d t -> p (d t)"))
+            cols = slice(HALF * h, HALF * (h + 1))
+            quantize(dic_code[G][:, cols], dic_scale[G][:, cols], dic_il[G][h][:].rearrange("p d t -> p (d t)"))
 
         def turn_x(R, j, k):
             b = bank("tx%d%d" % (R, j), k)
@@ -335,37 +336,30 @@ def tile_relaxedarchetypalreluautoencoder_x2_kernel(
                 z[G][R][:, 2 * j : 2 * j + 2].rearrange("p c m t -> p (c m t)"),
             )
 
-        def decode(R, q, k):
-            b = bank("o%d%d" % (R, q), k)
-            held["o", R, q] = b
-            h, cols = q // 2, slice(P * (q % 2), P * (q % 2 + 1))
-            for t in range(4):
-                rows = slice(P * t, P * (t + 1))
-                for G in range(2):
-                    nc.tensor.matmul_mx(
-                        out=b[:, rows],
-                        lhsT=z_code[G][R][:, rows].bitcast(FP8X4),
-                        lhsT_scale=z_scale[G][R][:, rows],
-                        rhs=dic_code[G][h][:, cols].bitcast(FP8X4),
-                        rhs_scale=dic_scale[G][h][:, cols],
-                        start=(G == 0),
-                        stop=(G == 1),
-                    )
+        def decode_rows(R, t, k):
+            b = bank("o%d%d" % (R, t), k)
+            held["o", R, t] = b
+            rows = slice(P * t, P * (t + 1))
+            for G in range(2):
+                nc.tensor.matmul_mx(
+                    out=b[:],
+                    lhsT=z_code[G][R][:, rows].bitcast(FP8X4),
+                    lhsT_scale=z_scale[G][R][:, rows],
+                    rhs=dic_code[G][:].bitcast(FP8X4),
+                    rhs_scale=dic_scale[G][:],
+                    start=(G == 0),
+                    stop=(G == 1),
+                )
 
-        def drain_out(R, q, eng):
-            copy(eng, out=res[R][:, :, P * q : P * (q + 1)], in_=held["o", R, q][:].rearrange("p (t d) -> p t d", t=4))
+        def drain_rows(R, t, eng):
+            copy(eng, out=res[R][:, t, :], in_=held["o", R, t][:])
 
-        def round_out(R, q, eng, from_bank=False):
+        def store_rows(R, t):
+            nc.sync.dma_start(out=out_v[R, :, t, :], in_=res[R][:, t, :])
+
+        def round_out(R, q, eng):
             cols = slice(P * q, P * (q + 1))
-            if from_bank:
-                sums = held["o", R, q][:].rearrange("p (t d) -> p d t", t=4)
-            else:
-                sums = res[R][:, :, cols].rearrange("p t d -> p d t")
-            copy(eng, out=res_il[R][:, cols, :], in_=sums)
-
-        def store_out(R, q, n):
-            cols = slice(P * q, P * (q + n))
-            nc.sync.dma_start(out=out_v[R, :, :, cols], in_=res[R][:, :, cols])
+            copy(eng, out=res_il[R][:, cols, :], in_=res[R][:, :, cols].rearrange("p t d -> p d t"))
 
         def quantize_out(R, q, n):
             cols = slice(P * q, P * (q + n))
@@ -379,12 +373,12 @@ def tile_relaxedarchetypalreluautoencoder_x2_kernel(
 
         def store_scales(eng):
             for q in range(4):
-                eng.dma_start(
+                (eng if q % 2 else nc.scalar).dma_start(
                     out=out_2[:, 4 * q : 4 * q + 4, :].rearrange("g r d -> r g d").bitcast(I32),
                     in_=res_scale[32 * q : 32 * q + 4, :, :].bitcast(I32),
                 )
 
-        load_lam(0, 1)
+        load_lam(0, 0)
         setup_zeros()
         load_logits(0)
         setup_vector()
@@ -392,211 +386,212 @@ def tile_relaxedarchetypalreluautoencoder_x2_kernel(
         load_s()
         setup_gpsimd()
         load_g()
-        load_logits(2)
         load_logits(3)
         load_logits(1)
-        load_lam(0, 0)
+        load_logits(2)
+        load_lam(0, 1)
         load_logits(4)
-        square_sum(2)
-        load_we_scales()
-        row_max(0)
-        widen_s()
-        square_sum(3)
-        spread_g()
-        row_max(2)
-        exponentiate(0)
-        load_rows(x_sb, x_v, 0)
-        row_max(3)
-        load_lam(1, 0)
-        exponentiate(2)
-        invert(0, nc.vector)
-        row_max(1)
-        load_logits(6)
-        weigh(0)
         square_sum(1)
-        load_c()
-        load_lam(1, 1)
-        load_rows(x_sb, x_v, 1)
+        load_lam(1, 0)
         square_sum(0)
-        load_we()
-        load_c_scales()
-        invert(2, nc.vector)
-        row_max(4)
-        turn_pg(0, 0)
+        row_max(0)
+        load_logits(6)
+        widen_s()
+        spread_g()
+        load_lam(1, 1)
+        load_we_scales()
+        row_max(3)
+        exponentiate(0)
+        row_max(1)
         exponentiate(3)
-        lam_gain(0)
-        weigh(2)
-        turn_x(0, 1, 1)
-        exponentiate(1)
+        invert(0, nc.vector)
+        row_max(2)
+        weigh(0)
+        square_sum(2)
+        square_sum(3)
+        load_rows(x_sb, x_v, 0)
         invert(3, nc.vector)
         row_max(5)
-        turn_pg(2, 2)
-        scale_lam(1, nc.gpsimd)
+        turn_pg(0, 0)
+        exponentiate(1)
+        lam_gain(0)
+        load_we()
         weigh(3)
-        exponentiate(5)
-        scale_lam(2, nc.gpsimd)
+        exponentiate(2)
+        load_c_scales()
         invert(1, nc.vector)
+        row_max(4)
+        turn_pg(3, 1)
+        scale_lam(2, nc.gpsimd)
         row_max(6)
-        turn_pg(3, 3)
-        drain_pg(2, nc.scalar)
+        exponentiate(5)
+        load_rows(x_sb, x_v, 1)
+        load_c()
         scale_lam(0, nc.gpsimd)
-        turn_x(0, 0, 4)
-        row_max(7)
-        drain_x(0, 1, nc.scalar)
+        invert(2, nc.vector)
         weigh(1)
-        square_sum(5)
-        turn_x(1, 1, 5)
-        drain_pg(0, nc.scalar)
-        invert(5, nc.vector)
-        quantize_pg(2)
-        square_sum(4)
-        turn_x(1, 0, 6)
-        quantize_pg(0)
-        quantize_x(0, 1)
         drain_pg(3, nc.scalar)
-        archetypes(0, 2)
-        permute_we(0, nc.vector)
-        square_sum(6)
-        quantize_pg(3)
-        square_sum(7)
-        permute_we(1, nc.vector)
-        archetypes(2, 1)
-        exponentiate(4)
-        weigh(5)
-        lam_gain(1)
-        turn_pg(1, 0)
-        exponentiate(6)
-        invert(4, nc.vector)
-        dictionary(0)
-        turn_pg(5, 3)
+        scale_lam(1, nc.gpsimd)
+        turn_x(0, 0, 2)
+        weigh(2)
+        square_sum(4)
         scale_lam(3, nc.gpsimd)
-        weigh(4)
-        encode(0, 0, 2, 2)
-        exponentiate(7)
-        scale_lam(6, nc.gpsimd)
+        turn_pg(1, 3)
+        square_sum(5)
+        invert(5, nc.vector)
+        permute_we(0, nc.vector)
+        turn_pg(2, 4)
+        exponentiate(6)
+        turn_x(0, 1, 5)
+        quantize_pg(3)
+        permute_we(1, nc.vector)
+        square_sum(7)
+        turn_x(1, 1, 6)
         invert(6, nc.vector)
-        dictionary(2)
-        drain_pg(1, nc.scalar)
-        scale_lam(7, nc.gpsimd)
-        invert(7, nc.vector)
+        weigh(5)
+        square_sum(6)
+        exponentiate(4)
+        lam_gain(1)
         weigh(6)
-        encode(1, 0, 3, 1)
-        relu(0, 0, 2, nc.scalar)
-        scale_lam(5, nc.gpsimd)
-        archetypes(3, 0)
-        drain_x(1, 1, nc.scalar)
-        weigh(7)
-        scale_lam(4, nc.gpsimd)
-        drain_x(1, 0, nc.scalar)
-        encode(0, 0, 3, 2)
-        drain_pg(5, nc.scalar)
-        turn_pg(4, 5)
-        quantize_pg(1)
+        turn_pg(5, 1)
         drain_x(0, 0, nc.scalar)
-        turn_pg(6, 6)
-        quantize_x(1, 0)
-        turn_pg(7, 3)
-        quantize_pg(5)
-        relu(0, 0, 3, nc.scalar)
-        archetypes(1, 4)
-        quantize_x(1, 1)
+        invert(4, nc.vector)
+        row_max(7)
+        drain_pg(1, nc.scalar)
+        turn_x(1, 0, 2)
+        scale_lam(7, nc.gpsimd)
+        drain_pg(0, nc.scalar)
+        weigh(4)
+        archetypes(3, 3)
+        scale_lam(4, nc.gpsimd)
+        exponentiate(7)
         quantize_x(0, 0)
-        drain_pg(4, nc.scalar)
+        quantize_pg(1)
+        drain_x(0, 1, nc.scalar)
+        encode(1, 0, 1, 0)
+        quantize_pg(0)
+        invert(7, nc.vector)
+        scale_lam(5, nc.gpsimd)
         dictionary(3)
-        encode(1, 0, 2, 2)
-        drain_pg(7, nc.scalar)
-        encode(1, 0, 0, 5)
-        dictionary(1)
-        archetypes(5, 0)
-        drain_pg(6, nc.scalar)
-        quantize_pg(7)
-        encode(0, 1, 0, 3)
-        relu(1, 0, 3, nc.scalar)
-        interleave_dic(0, 0, nc.vector)
-        encode(1, 0, 1, 4)
-        encode(0, 1, 1, 6)
-        relu(1, 0, 0, nc.scalar)
-        quantize_pg(6)
-        archetypes(7, 1)
-        quantize_dic(0, 0)
-        relu(0, 1, 0, nc.scalar)
-        encode(1, 1, 0, 5)
-        quantize_pg(4)
-        dictionary(5)
-        interleave_dic(0, 1, nc.gpsimd)
-        relu(0, 1, 1, nc.scalar)
-        archetypes(6, 3)
-        dictionary(7)
-        relu(1, 0, 2, nc.scalar)
-        archetypes(4, 0)
-        dictionary(6)
+        drain_pg(2, nc.scalar)
+        archetypes(1, 5)
+        weigh(7)
         relu(1, 0, 1, nc.scalar)
-        encode(1, 1, 1, 6)
-        encode(0, 1, 2, 1)
-        dictionary(4)
-        relu(1, 1, 0, nc.scalar)
-        encode(0, 0, 1, 2)
-        encode(1, 1, 2, 3)
-        quantize_z(0, 0, 1)
-        relu(0, 1, 2, nc.scalar)
-        encode(0, 1, 3, 4)
-        interleave_dic(1, 0, nc.vector)
-        encode(0, 0, 0, 0)
-        relu(0, 0, 1, nc.scalar)
-        encode(1, 1, 3, 5)
-        quantize_z(1, 0, 1)
+        scale_lam(6, nc.gpsimd)
+        archetypes(0, 3)
+        drain_x(1, 0, nc.scalar)
+        encode(0, 0, 0, 4)
+        turn_pg(6, 0)
+        dictionary(1)
+        drain_pg(5, nc.scalar)
+        turn_pg(4, 2)
+        dictionary(0)
+        turn_pg(7, 5)
+        drain_x(1, 1, nc.scalar)
+        encode(1, 0, 0, 1)
+        quantize_pg(2)
+        drain_pg(4, nc.scalar)
+        encode(0, 0, 1, 3)
+        quantize_x(1, 1)
+        archetypes(2, 6)
+        quantize_pg(5)
         relu(0, 0, 0, nc.scalar)
-        quantize_z(1, 0, 0)
-        quantize_dic(1, 0)
-        relu(1, 1, 2, nc.scalar)
+        quantize_pg(4)
+        archetypes(5, 2)
+        drain_pg(6, nc.scalar)
+        quantize_x(0, 1)
+        quantize_x(1, 0)
+        encode(0, 1, 3, 4)
+        drain_pg(7, nc.scalar)
+        quantize_pg(6)
+        archetypes(4, 0)
+        dictionary(2)
+        relu(0, 0, 1, nc.scalar)
+        encode(1, 0, 3, 5)
+        quantize_pg(7)
+        archetypes(6, 6)
+        relu(1, 0, 0, nc.scalar)
         quantize_z(0, 0, 0)
-        interleave_dic(1, 1, nc.vector)
-        relu(1, 1, 3, nc.scalar)
-        decode(0, 0, 1)
-        relu(1, 1, 1, nc.scalar)
-        quantize_dic(0, 1)
-        decode(0, 1, 2)
-        quantize_dic(1, 1)
+        interleave_dic(0, 0, nc.gpsimd)
+        dictionary(5)
+        encode(1, 0, 2, 3)
         relu(0, 1, 3, nc.scalar)
-        quantize_z(1, 1, 1)
-        decode(0, 2, 0)
-        drain_out(0, 0, nc.vector)
-        drain_out(0, 1, nc.scalar)
-        decode(0, 3, 3)
+        encode(0, 0, 2, 1)
+        dictionary(6)
+        archetypes(7, 2)
+        relu(1, 0, 3, nc.scalar)
+        dictionary(4)
+        encode(1, 1, 0, 4)
+        relu(1, 0, 2, nc.scalar)
+        encode(0, 1, 1, 6)
+        dictionary(7)
+        relu(0, 0, 2, nc.scalar)
+        encode(1, 1, 2, 5)
+        encode(0, 1, 0, 0)
+        quantize_dic(0, 0)
+        interleave_dic(0, 1, nc.scalar)
+        encode(0, 0, 3, 3)
+        quantize_z(1, 0, 0)
+        encode(1, 1, 3, 2)
+        interleave_dic(1, 0, nc.vector)
+        encode(0, 1, 2, 1)
+        interleave_dic(1, 1, nc.vector)
+        relu(1, 1, 0, nc.scalar)
+        relu(0, 0, 3, nc.scalar)
+        quantize_dic(0, 1)
+        encode(1, 1, 1, 4)
+        quantize_dic(1, 1)
+        relu(1, 1, 2, nc.scalar)
+        quantize_dic(1, 0)
+        quantize_z(1, 0, 1)
+        relu(1, 1, 1, nc.scalar)
+        decode_rows(0, 1, 3)
+        quantize_z(0, 0, 1)
+        relu(0, 1, 1, nc.vector)
+        relu(0, 1, 2, nc.scalar)
+        decode_rows(0, 0, 5)
+        relu(0, 1, 0, nc.vector)
+        drain_rows(0, 1, nc.scalar)
+        decode_rows(0, 2, 4)
         quantize_z(1, 1, 0)
-        store_out(0, 0, 2)
-        drain_out(0, 2, nc.scalar)
-        quantize_z(0, 1, 1)
+        drain_rows(0, 0, nc.scalar)
+        decode_rows(0, 3, 6)
+        store_rows(0, 1)
         quantize_z(0, 1, 0)
-        drain_out(0, 3, nc.scalar)
-        round_out(0, 1, nc.vector)
-        decode(1, 2, 5)
-        round_out(0, 0, nc.vector)
-        store_out(0, 2, 2)
+        relu(1, 1, 3, nc.scalar)
+        drain_rows(0, 2, nc.vector)
+        store_rows(0, 0)
+        decode_rows(1, 1, 1)
+        drain_rows(0, 3, nc.scalar)
+        quantize_z(0, 1, 1)
+        store_rows(0, 2)
+        decode_rows(1, 0, 0)
+        quantize_z(1, 1, 1)
+        drain_rows(1, 1, nc.scalar)
+        store_rows(0, 3)
         round_out(0, 2, nc.vector)
-        decode(1, 1, 6)
-        quantize_out(0, 0, 2)
-        drain_out(1, 2, nc.scalar)
+        decode_rows(1, 2, 3)
+        round_out(0, 0, nc.vector)
+        drain_rows(1, 0, nc.scalar)
+        store_rows(1, 1)
         round_out(0, 3, nc.vector)
-        decode(1, 0, 4)
-        store_codes(0, 0, 2, nc.sync)
-        round_out(1, 2, nc.scalar, True)
-        store_out(1, 2, 1)
+        decode_rows(1, 3, 5)
+        drain_rows(1, 2, nc.scalar)
+        round_out(0, 1, nc.vector)
+        store_rows(1, 0)
         quantize_out(0, 2, 2)
-        decode(1, 3, 1)
-        quantize_out(1, 2, 1)
-        drain_out(1, 0, nc.scalar)
+        drain_rows(1, 3, nc.scalar)
+        quantize_out(0, 0, 2)
         store_codes(0, 2, 2, nc.sync)
-        drain_out(1, 1, nc.vector)
-        store_codes(1, 2, 1, nc.sync)
-        drain_out(1, 3, nc.scalar)
-        store_out(1, 0, 2)
-        round_out(1, 1, nc.vector)
-        store_out(1, 3, 1)
+        round_out(1, 2, nc.vector)
+        store_codes(0, 0, 2, nc.sync)
+        round_out(1, 3, nc.scalar)
+        store_rows(1, 3)
+        store_rows(1, 2)
         round_out(1, 0, nc.vector)
-        round_out(1, 3, nc.vector)
+        round_out(1, 1, nc.vector)
+        quantize_out(1, 2, 2)
         quantize_out(1, 0, 2)
-        quantize_out(1, 3, 1)
+        store_codes(1, 2, 2, nc.scalar)
         store_codes(1, 0, 2, nc.sync)
-        store_codes(1, 3, 1, nc.scalar)
-        store_scales(nc.scalar)
+        store_scales(nc.sync)

@@ -276,10 +276,18 @@ def tile_relaxedarchetypalreluautoencoder_x2_kernel(
                 op1=ALU.add,
             )
 
+        def interleave(eng, dst, src):
+            if eng is nc.gpsimd:
+                copy(eng, out=dst, in_=src.rearrange("p t d -> p d t"))
+            else:
+                copy(
+                    eng,
+                    out=dst.rearrange("p (c i) t -> p c t i", i=4),
+                    in_=src.rearrange("p t (c i) -> p c t i", i=4),
+                )
+
         def interleave_dic(G, h, eng):
-            copy(
-                eng, out=dic_il[G][h][:], in_=dic[G][:, :, HALF * h : HALF * (h + 1)].rearrange("p t d -> p d t")
-            )
+            interleave(eng, dic_il[G][h][:], dic[G][:, :, HALF * h : HALF * (h + 1)])
 
         def quantize_dic(G, h):
             cols = slice(HALF * h, HALF * (h + 1))
@@ -359,7 +367,7 @@ def tile_relaxedarchetypalreluautoencoder_x2_kernel(
 
         def round_out(R, q, eng):
             cols = slice(P * q, P * (q + 1))
-            copy(eng, out=res_il[R][:, cols, :], in_=res[R][:, :, cols].rearrange("p t d -> p d t"))
+            interleave(eng, res_il[R][:, cols, :], res[R][:, :, cols])
 
         def quantize_out(R, q, n):
             cols = slice(P * q, P * (q + n))
@@ -383,7 +391,6 @@ def tile_relaxedarchetypalreluautoencoder_x2_kernel(
         load_logits(0)
         setup_vector()
         setup_scalar()
-        load_s()
         setup_gpsimd()
         load_g()
         load_logits(3)
@@ -391,205 +398,206 @@ def tile_relaxedarchetypalreluautoencoder_x2_kernel(
         load_logits(2)
         load_lam(0, 1)
         load_logits(4)
+        load_s()
         square_sum(1)
-        load_lam(1, 0)
+        load_rows(x_sb, x_v, 0)
         square_sum(0)
         row_max(0)
         load_logits(6)
-        widen_s()
         spread_g()
         load_lam(1, 1)
-        load_we_scales()
         row_max(3)
         exponentiate(0)
+        load_lam(1, 0)
         row_max(1)
+        load_we_scales()
         exponentiate(3)
         invert(0, nc.vector)
         row_max(2)
         weigh(0)
         square_sum(2)
         square_sum(3)
-        load_rows(x_sb, x_v, 0)
         invert(3, nc.vector)
-        row_max(5)
-        turn_pg(0, 0)
-        exponentiate(1)
-        lam_gain(0)
-        load_we()
-        weigh(3)
-        exponentiate(2)
-        load_c_scales()
-        invert(1, nc.vector)
+        widen_s()
         row_max(4)
-        turn_pg(3, 1)
-        scale_lam(2, nc.gpsimd)
-        row_max(6)
-        exponentiate(5)
-        load_rows(x_sb, x_v, 1)
-        load_c()
-        scale_lam(0, nc.gpsimd)
+        exponentiate(2)
+        lam_gain(0)
+        weigh(3)
+        load_we()
+        turn_x(0, 0, 0)
+        exponentiate(1)
         invert(2, nc.vector)
-        weigh(1)
-        drain_pg(3, nc.scalar)
-        scale_lam(1, nc.gpsimd)
-        turn_x(0, 0, 2)
+        row_max(5)
+        turn_pg(0, 1)
+        scale_lam(0, nc.gpsimd)
+        load_rows(x_sb, x_v, 1)
         weigh(2)
-        square_sum(4)
+        turn_x(0, 1, 2)
+        exponentiate(5)
+        load_c_scales()
         scale_lam(3, nc.gpsimd)
-        turn_pg(1, 3)
-        square_sum(5)
-        invert(5, nc.vector)
-        permute_we(0, nc.vector)
-        turn_pg(2, 4)
-        exponentiate(6)
-        turn_x(0, 1, 5)
-        quantize_pg(3)
-        permute_we(1, nc.vector)
-        square_sum(7)
-        turn_x(1, 1, 6)
-        invert(6, nc.vector)
-        weigh(5)
-        square_sum(6)
-        exponentiate(4)
-        lam_gain(1)
-        weigh(6)
-        turn_pg(5, 1)
-        drain_x(0, 0, nc.scalar)
-        invert(4, nc.vector)
+        turn_pg(3, 3)
+        invert(1, nc.vector)
         row_max(7)
-        drain_pg(1, nc.scalar)
-        turn_x(1, 0, 2)
-        scale_lam(7, nc.gpsimd)
+        exponentiate(4)
+        scale_lam(2, nc.gpsimd)
+        turn_pg(2, 4)
+        load_c()
+        invert(5, nc.vector)
+        weigh(1)
+        scale_lam(1, nc.gpsimd)
         drain_pg(0, nc.scalar)
-        weigh(4)
-        archetypes(3, 3)
-        scale_lam(4, nc.gpsimd)
-        exponentiate(7)
-        quantize_x(0, 0)
-        quantize_pg(1)
+        invert(4, nc.vector)
         drain_x(0, 1, nc.scalar)
-        encode(1, 0, 1, 0)
-        quantize_pg(0)
-        invert(7, nc.vector)
-        scale_lam(5, nc.gpsimd)
-        dictionary(3)
+        weigh(5)
+        turn_pg(1, 5)
         drain_pg(2, nc.scalar)
-        archetypes(1, 5)
-        weigh(7)
-        relu(1, 0, 1, nc.scalar)
-        scale_lam(6, nc.gpsimd)
-        archetypes(0, 3)
-        drain_x(1, 0, nc.scalar)
-        encode(0, 0, 0, 4)
-        turn_pg(6, 0)
-        dictionary(1)
-        drain_pg(5, nc.scalar)
-        turn_pg(4, 2)
-        dictionary(0)
-        turn_pg(7, 5)
-        drain_x(1, 1, nc.scalar)
-        encode(1, 0, 0, 1)
+        turn_x(1, 0, 6)
+        quantize_x(0, 1)
+        drain_pg(3, nc.scalar)
+        quantize_pg(0)
+        drain_x(0, 0, nc.scalar)
+        row_max(6)
+        turn_pg(5, 1)
+        turn_x(1, 1, 2)
+        drain_pg(1, nc.scalar)
+        quantize_pg(3)
+        quantize_x(0, 0)
+        square_sum(6)
         quantize_pg(2)
+        archetypes(3, 4)
+        permute_we(0, nc.vector)
+        square_sum(5)
+        square_sum(4)
+        quantize_pg(1)
+        permute_we(1, nc.vector)
+        archetypes(1, 3)
+        square_sum(7)
+        weigh(4)
+        exponentiate(6)
+        lam_gain(1)
+        archetypes(2, 0)
+        dictionary(3)
+        encode(1, 0, 1, 5)
+        drain_x(1, 0, nc.scalar)
+        invert(6, nc.vector)
+        dictionary(2)
+        encode(0, 0, 0, 4)
+        exponentiate(7)
+        turn_pg(4, 6)
+        scale_lam(7, nc.gpsimd)
+        weigh(6)
+        archetypes(0, 0)
+        scale_lam(5, nc.gpsimd)
+        relu(0, 0, 0, nc.scalar)
+        invert(7, nc.vector)
+        dictionary(1)
+        drain_x(1, 1, nc.scalar)
+        scale_lam(4, nc.gpsimd)
+        turn_pg(6, 4)
+        weigh(7)
         drain_pg(4, nc.scalar)
         encode(0, 0, 1, 3)
-        quantize_x(1, 1)
-        archetypes(2, 6)
-        quantize_pg(5)
-        relu(0, 0, 0, nc.scalar)
-        quantize_pg(4)
-        archetypes(5, 2)
+        scale_lam(6, nc.gpsimd)
+        encode(1, 0, 2, 2)
         drain_pg(6, nc.scalar)
-        quantize_x(0, 1)
-        quantize_x(1, 0)
-        encode(0, 1, 3, 4)
-        drain_pg(7, nc.scalar)
-        quantize_pg(6)
-        archetypes(4, 0)
-        dictionary(2)
+        encode(1, 0, 0, 6)
+        dictionary(0)
+        drain_pg(5, nc.scalar)
+        turn_pg(7, 4)
+        quantize_x(1, 1)
+        encode(1, 0, 3, 0)
         relu(0, 0, 1, nc.scalar)
-        encode(1, 0, 3, 5)
-        quantize_pg(7)
-        archetypes(6, 6)
-        relu(1, 0, 0, nc.scalar)
+        quantize_pg(5)
+        encode(0, 0, 3, 1)
+        quantize_pg(6)
+        drain_pg(7, nc.scalar)
+        archetypes(5, 3)
         quantize_z(0, 0, 0)
+        relu(1, 0, 1, nc.scalar)
+        quantize_pg(4)
+        archetypes(6, 4)
+        quantize_x(1, 0)
+        relu(1, 0, 0, nc.scalar)
+        quantize_pg(7)
+        archetypes(4, 5)
         interleave_dic(0, 0, nc.gpsimd)
         dictionary(5)
-        encode(1, 0, 2, 3)
-        relu(0, 1, 3, nc.scalar)
-        encode(0, 0, 2, 1)
-        dictionary(6)
-        archetypes(7, 2)
-        relu(1, 0, 3, nc.scalar)
-        dictionary(4)
-        encode(1, 1, 0, 4)
         relu(1, 0, 2, nc.scalar)
-        encode(0, 1, 1, 6)
-        dictionary(7)
-        relu(0, 0, 2, nc.scalar)
-        encode(1, 1, 2, 5)
-        encode(0, 1, 0, 0)
-        quantize_dic(0, 0)
+        archetypes(7, 6)
+        dictionary(6)
         interleave_dic(0, 1, nc.scalar)
-        encode(0, 0, 3, 3)
+        encode(1, 1, 1, 3)
+        encode(0, 0, 2, 2)
+        dictionary(4)
+        encode(0, 1, 2, 4)
+        dictionary(7)
+        encode(0, 1, 0, 5)
+        relu(0, 0, 2, nc.scalar)
+        quantize_dic(0, 0)
+        encode(1, 1, 0, 6)
+        relu(1, 0, 3, nc.scalar)
         quantize_z(1, 0, 0)
-        encode(1, 1, 3, 2)
-        interleave_dic(1, 0, nc.vector)
-        encode(0, 1, 2, 1)
+        encode(1, 1, 2, 2)
         interleave_dic(1, 1, nc.vector)
-        relu(1, 1, 0, nc.scalar)
         relu(0, 0, 3, nc.scalar)
-        quantize_dic(0, 1)
-        encode(1, 1, 1, 4)
-        quantize_dic(1, 1)
-        relu(1, 1, 2, nc.scalar)
-        quantize_dic(1, 0)
-        quantize_z(1, 0, 1)
+        encode(0, 1, 3, 0)
+        interleave_dic(1, 0, nc.vector)
         relu(1, 1, 1, nc.scalar)
-        decode_rows(0, 1, 3)
-        quantize_z(0, 0, 1)
-        relu(0, 1, 1, nc.vector)
-        relu(0, 1, 2, nc.scalar)
-        decode_rows(0, 0, 5)
-        relu(0, 1, 0, nc.vector)
-        drain_rows(0, 1, nc.scalar)
-        decode_rows(0, 2, 4)
-        quantize_z(1, 1, 0)
-        drain_rows(0, 0, nc.scalar)
-        decode_rows(0, 3, 6)
-        store_rows(0, 1)
-        quantize_z(0, 1, 0)
+        encode(1, 1, 3, 1)
+        quantize_dic(1, 1)
+        relu(1, 1, 0, nc.scalar)
+        encode(0, 1, 1, 3)
+        quantize_dic(0, 1)
         relu(1, 1, 3, nc.scalar)
+        quantize_dic(1, 0)
+        quantize_z(0, 0, 1)
+        relu(0, 1, 2, nc.scalar)
+        decode_rows(0, 1, 6)
+        quantize_z(1, 0, 1)
+        relu(0, 1, 0, nc.vector)
+        relu(0, 1, 1, nc.scalar)
+        decode_rows(0, 2, 1)
+        quantize_z(1, 1, 0)
+        drain_rows(0, 1, nc.scalar)
+        decode_rows(0, 0, 4)
+        quantize_z(0, 1, 0)
         drain_rows(0, 2, nc.vector)
-        store_rows(0, 0)
-        decode_rows(1, 1, 1)
-        drain_rows(0, 3, nc.scalar)
-        quantize_z(0, 1, 1)
+        relu(1, 1, 2, nc.scalar)
+        decode_rows(0, 3, 5)
+        store_rows(0, 1)
+        drain_rows(0, 0, nc.vector)
+        relu(0, 1, 3, nc.scalar)
+        decode_rows(1, 1, 3)
         store_rows(0, 2)
-        decode_rows(1, 0, 0)
         quantize_z(1, 1, 1)
+        decode_rows(1, 0, 6)
+        drain_rows(0, 3, nc.scalar)
+        store_rows(0, 0)
+        quantize_z(0, 1, 1)
         drain_rows(1, 1, nc.scalar)
+        round_out(0, 1, nc.vector)
         store_rows(0, 3)
-        round_out(0, 2, nc.vector)
-        decode_rows(1, 2, 3)
-        round_out(0, 0, nc.vector)
+        decode_rows(1, 3, 1)
+        round_out(0, 3, nc.vector)
         drain_rows(1, 0, nc.scalar)
         store_rows(1, 1)
-        round_out(0, 3, nc.vector)
-        decode_rows(1, 3, 5)
-        drain_rows(1, 2, nc.scalar)
-        round_out(0, 1, nc.vector)
-        store_rows(1, 0)
-        quantize_out(0, 2, 2)
+        decode_rows(1, 2, 2)
+        round_out(0, 0, nc.vector)
         drain_rows(1, 3, nc.scalar)
+        round_out(0, 2, nc.vector)
+        store_rows(1, 0)
         quantize_out(0, 0, 2)
-        store_codes(0, 2, 2, nc.sync)
-        round_out(1, 2, nc.vector)
+        drain_rows(1, 2, nc.scalar)
+        quantize_out(0, 2, 2)
         store_codes(0, 0, 2, nc.sync)
-        round_out(1, 3, nc.scalar)
+        round_out(1, 2, nc.vector)
+        store_codes(0, 2, 2, nc.sync)
+        round_out(1, 1, nc.scalar)
         store_rows(1, 3)
         store_rows(1, 2)
+        round_out(1, 3, nc.vector)
         round_out(1, 0, nc.vector)
-        round_out(1, 1, nc.vector)
         quantize_out(1, 2, 2)
         quantize_out(1, 0, 2)
         store_codes(1, 2, 2, nc.scalar)

from contextlib import ExitStack

import concourse.mybir as mybir
from concourse.masks import make_identity

B, D, F, N = 1024, 512, 1024, 1024
FLOPS = 2 * B * D * F + 2 * F * N * D + 2 * B * F * D

F32 = mybir.dt.float32
BF16 = mybir.dt.bfloat16
I32 = mybir.dt.int32
U32 = mybir.dt.uint32
U8 = mybir.dt.uint8
FP8X4 = mybir.dt.float8_e4m3fn_x4
ALU = mybir.AluOpType
ACT = mybir.ActivationFunctionType

P = 128
HALF = D // 2


def tile_relaxedarchetypalreluautoencoder_x2_kernel(
    tc, x, we_words, we_scales, logits, g, c_words, c_scales, lam, s, out_0, out_1, out_2
):
    nc = tc.nc
    with ExitStack() as ctx:
        sb = ctx.enter_context(tc.tile_pool(name="sb", bufs=1))
        psum = ctx.enter_context(tc.psum_pool(name="psum", bufs=1))
        ctx.enter_context(tc.manual_schedule())

        def keep(name, shape, dtype, tag=None):
            return sb.tile(shape, dtype, name=name, tag=tag or name, align_bytes=64)

        def bank(name, k):
            return psum.tile([P, 512], F32, name=name, tag="bank%d" % k)

        logits_v = logits.rearrange("(G p t) n -> G p t n", G=2, t=4)
        x_v = x.rearrange("(G p t) k -> G p t k", G=2, t=4)
        lam_v = lam.rearrange("(G p t) d -> G p t d", G=2, t=4)
        out_v = out_0.rearrange("(G p t) d -> G p t d", G=2, t=4)

        zeros = keep("zeros", [P, P], BF16)
        ones = keep("ones", [P, P], BF16)
        g_row = keep("g_row", [P, N], BF16)
        ident = keep("ident", [P, P], F32)
        neg_half = keep("neg_half", [P, 4], F32)
        we_scale_raw = keep("we_scale_raw", [P, F], U8)
        c_scale = keep("c_scale", [P, 2, D], U8)
        we_raw = keep("we_raw", [P, F], U32)
        we_code = keep("we_code", [P, F], U32)
        we_scale = keep("we_scale", [P, F], U8)
        c_code = keep("c_code", [P, 2, D], U32)
        s_raw = keep("s_raw", [P, 2, 4], BF16)
        s_col = keep("s_col", [P, 8], F32)
        lg = [keep("lg%d" % i, [P, N], BF16) for i in range(4)]
        lg_pair = [keep("lgp%d" % j, [P, 2, N], BF16) for j in range(2)]
        lam_sb = [keep("lam%d" % G, [P, 4, D], BF16) for G in range(2)]
        x_sb = [keep("x%d" % G, [P, 4, D], BF16) for G in range(2)]
        neg_max = [keep("nmax%d" % i, [P, 1], F32) for i in range(8)]
        total = [keep("total%d" % i, [P, 1], F32) for i in range(8)]
        inv_total = [keep("inv%d" % i, [P, 1], F32) for i in range(8)]
        e = {}
        pg = {}
        pg_t = [keep("pgt%d" % i, [P, 2, P, 4], BF16) for i in range(8)]
        pg_code = [keep("pgc%d" % i, [P, 2 * P], U32) for i in range(8)]
        pg_scale = [keep("pgs%d" % i, [P, 2 * P], U8) for i in range(8)]
        sq = [keep("sq%d" % G, [P, 4], F32) for G in range(2)]
        clamp = [keep("clamp%d" % G, [P, 4], F32) for G in range(2)]
        shrink = [keep("shrink%d" % G, [P, 4], F32) for G in range(2)]
        gain = [keep("gain%d" % G, [P, 4], F32) for G in range(2)]
        lam_term = [keep("lamt%d" % i, [P, D], F32) for i in range(8)]
        dic = [keep("dic%d" % G, [P, 4, D], BF16) for G in range(2)]
        dic_il = [[keep("dici%d%d" % (G, h), [P, HALF, 4], BF16) for h in range(2)] for G in range(2)]
        dic_code = [keep("dicc%d" % G, [P, D], U32) for G in range(2)]
        dic_scale = [keep("dics%d" % G, [P, D], U8) for G in range(2)]
        x_t = [keep("xt%d" % R, [P, 4, P, 4], BF16) for R in range(2)]
        x_code = [keep("xc%d" % R, [P, 4 * P], U32) for R in range(2)]
        x_scale = [keep("xs%d" % R, [P, 4 * P], U8) for R in range(2)]
        z = [[keep("z%d%d" % (G, R), [P, 4, P, 4], BF16) for R in range(2)] for G in range(2)]
        z_code = [[keep("zc%d%d" % (G, R), [P, 4 * P], U32) for R in range(2)] for G in range(2)]
        z_scale = [[keep("zs%d%d" % (G, R), [P, 4 * P], U8) for R in range(2)] for G in range(2)]
        res = [keep("res%d" % R, [P, 4, D], F32) for R in range(2)]
        res_il = [keep("resi%d" % R, [P, D, 4], BF16) for R in range(2)]
        res_code = [keep("resc%d" % R, [P, D], U32) for R in range(2)]
        res_scale = keep("ress", [P, 2, D], U8)
        g_bank = psum.tile([P, N], BF16, name="g_bank", tag="bank7")
        held = {}

        def logit_rows(i):
            return lg[i][:] if i < 4 else lg_pair[i // 2 - 2][:, i % 2, :]

        def load_logits(i):
            if i < 4:
                nc.sync.dma_start(out=lg[i][:], in_=logits_v[0, :, i, :])
            else:
                t = i % 4
                nc.sync.dma_start(out=lg_pair[i // 2 - 2][:], in_=logits_v[i // 4, :, t : t + 2, :])

        def load_rows(tiles, view, G):
            nc.sync.dma_start(out=tiles[G][:], in_=view[G])

        def load_lam(G, j):
            nc.sync.dma_start(out=lam_sb[G][:, 2 * j : 2 * j + 2, :], in_=lam_v[G, :, 2 * j : 2 * j + 2, :])

        def load_g():
            nc.sync.dma_start(out=g_row[0:1, :], in_=g.rearrange("(o n) -> o n", o=1))

        def load_s():
            nc.sync.dma_start(out=s_raw[:], in_=s.rearrange("(G p t) -> p G t", G=2, t=4))

        def load_c_scales():
            for q in range(4):
                nc.sync.dma_start(
                    out=c_scale[32 * q : 32 * q + 4, :, :].bitcast(I32),
                    in_=c_scales[:, 4 * q : 4 * q + 4, :].rearrange("g r d -> r g d").bitcast(I32),
                )

        def load_we_scales():
            for q in range(4):
                nc.sync.dma_start(
                    out=we_scale_raw[32 * q : 32 * q + 4, :].bitcast(I32),
                    in_=we_scales[0, 4 * q : 4 * q + 4, :].bitcast(I32),
                )

        def load_c():
            nc.sync.dma_start(
                out=c_code[:].bitcast(I32),
                in_=c_words.rearrange("g p d t -> p g (d t)").bitcast(I32),
            )

        def load_we():
            nc.sync.dma_start(
                out=we_raw[:].bitcast(I32),
                in_=we_words[0].rearrange("p f t -> p (f t)").bitcast(I32),
            )

        def setup_zeros():
            nc.vector.memset(zeros[:], 0.0)

        def setup_vector():
            nc.vector.memset(g_row[:], 0.0)
            nc.vector.memset(c_scale[:].rearrange("p g d -> p (g d)").bitcast(I32), 0)
            nc.vector.memset(we_scale_raw[:].bitcast(I32), 0)

        def setup_scalar():
            nc.scalar.activation(out=ones[:], in_=zeros[:], func=ACT.Exp)

        def setup_gpsimd():
            make_identity(nc, ident[:])
            nc.gpsimd.memset(neg_half[:], -0.5)

        def copy(eng, out, in_):
            if eng is nc.scalar:
                nc.scalar.copy(out=out, in_=in_)
            elif eng is nc.vector:
                nc.vector.tensor_copy(out=out, in_=in_)
            else:
                nc.gpsimd.tensor_scalar(out=out, in0=in_, scalar1=1.0, scalar2=0.0, op0=ALU.mult, op1=ALU.add)

        def spread_g():
            g_pairs = g_row[:].rearrange("p (q u e) -> p u q e", u=2, e=2)
            for u in range(2):
                nc.tensor.matmul(
                    out=g_bank[:, 512 * u : 512 * (u + 1)], lhsT=ones[:], rhs=g_pairs[:, u, :, :], start=True, stop=True
                )

        def widen_s():
            nc.gpsimd.tensor_copy(out=s_col[:], in_=s_raw[:].rearrange("p G t -> p (G t)"))

        def permute_we(G, eng):
            cols = slice(512 * G, 512 * (G + 1))
            eng.tensor_copy(
                out=(we_code[:, cols] if eng is nc.gpsimd else we_code[:, cols].bitcast(I32)).rearrange("p (t m) -> p t m", t=4),
                in_=(we_raw[:, cols] if eng is nc.gpsimd else we_raw[:, cols].bitcast(I32)).rearrange("p (m t) -> p t m", t=4),
            )
            eng.tensor_copy(
                out=we_scale[:, cols].rearrange("p (t m) -> p t m", t=4),
                in_=we_scale_raw[:, cols].rearrange("p (m t) -> p t m", t=4),
            )

        def row_max(i):
            rows = logit_rows(i)
            nc.vector.tensor_scalar(
                out=rows, in0=rows, scalar1=-1.0, scalar2=None, op0=ALU.mult, op1=ALU.min, accum_out=neg_max[i][:]
            )

        def exponentiate(i):
            e[i] = keep("e%d" % i, [P, N], F32, "e%d" % i)
            nc.scalar.activation(
                out=e[i][:].rearrange("p (u q e) -> p u q e", u=2, e=2),
                in_=logit_rows(i).rearrange("p (q u e) -> p u q e", u=2, e=2),
                func=ACT.Exp,
                bias=neg_max[i][:],
                scale=-1.0,
                accum_out=total[i][:],
            )

        def invert(i, eng):
            nc.vector.reciprocal(out=inv_total[i][:], in_=total[i][:])

        def weigh(i):
            pg[i] = keep("pg%d" % i, [P, N], BF16, "pg%d" % i)
            nc.vector.scalar_tensor_tensor(
                out=pg[i][:], in0=e[i][:], scalar=inv_total[i][:], in1=g_bank[:], op0=ALU.mult, op1=ALU.mult
            )

        def turn_pg(i, k):
            words = pg[i][:].bitcast(F32)
            b = bank("tp%d" % i, k)
            held["tp", i] = b
            for u in range(2):
                for c in range(2):
                    j = 2 * c + u
                    nc.tensor.transpose(
                        b[:, P * j : P * (j + 1)], words[:, 256 * u + P * c : 256 * u + P * (c + 1)], ident[:]
                    )

        def drain_pg(i, eng):
            copy(
                eng, out=pg_t[i][:].bitcast(F32), in_=held["tp", i][:].rearrange("p (c u f) -> p c f u", c=2, u=2)
            )

        def quantize(codes, scales, values):
            nc.vector.quantize_mx(out=codes.bitcast(FP8X4), scales=scales, in_=values)

        def quantize_pg(i):
            quantize(pg_code[i][:], pg_scale[i][:], pg_t[i][:].rearrange("p c f t -> p (c f t)"))

        def archetypes(i, k):
            b = bank("a%d" % i, k)
            held["a", i] = b
            for c in range(2):
                cols = slice(P * c, P * (c + 1))
                nc.tensor.matmul_mx(
                    out=b[:],
                    lhsT=pg_code[i][:, cols].bitcast(FP8X4),
                    lhsT_scale=pg_scale[i][:, cols],
                    rhs=c_code[:, c, :].bitcast(FP8X4),
                    rhs_scale=c_scale[:, c, :],
                    start=(c == 0),
                    stop=(c == 1),
                )

        def square_sum(i):
            nc.scalar.activation(
                out=lam_term[i][:],
                in_=lam_sb[i // 4][:, i % 4, :],
                func=ACT.Square,
                accum_out=sq[i // 4][:, i % 4 : i % 4 + 1],
            )

        def lam_gain(G):
            nc.gpsimd.tensor_scalar(
                out=clamp[G][:], in0=sq[G][:], scalar1=1e-12, scalar2=1.0, op0=ALU.add, op1=ALU.max
            )
            nc.gpsimd.tensor_tensor(out=shrink[G][:], in0=clamp[G][:], in1=neg_half[:], op=ALU.pow)
            nc.gpsimd.tensor_tensor(out=gain[G][:], in0=shrink[G][:], in1=s_col[:, 4 * G : 4 * G + 4], op=ALU.mult)

        def scale_lam(i, eng):
            rows = lam_sb[i // 4][:, i % 4, :]
            factor = gain[i // 4][:, i % 4 : i % 4 + 1]
            if eng is nc.scalar:
                nc.scalar.activation(out=lam_term[i][:], in_=rows, func=ACT.Copy, scale=factor)
            else:
                eng.tensor_scalar(
                    out=lam_term[i][:], in0=rows, scalar1=factor, scalar2=0.0, op0=ALU.mult, op1=ALU.add
                )

        def dictionary(i):
            nc.vector.scalar_tensor_tensor(
                out=dic[i // 4][:, i % 4, :],
                in0=held["a", i][:],
                scalar=s_col[:, i : i + 1],
                in1=lam_term[i][:],
                op0=ALU.mult,
                op1=ALU.add,
            )

        def interleave(eng, dst, src):
            if eng is nc.gpsimd:
                copy(eng, out=dst, in_=src.rearrange("p t d -> p d t"))
            else:
                copy(
                    eng,
                    out=dst.rearrange("p (c i) t -> p c t i", i=4),
                    in_=src.rearrange("p t (c i) -> p c t i", i=4),
                )

        def interleave_dic(G, h, eng):
            interleave(eng, dic_il[G][h][:], dic[G][:, :, HALF * h : HALF * (h + 1)])

        def quantize_dic(G, h):
            cols = slice(HALF * h, HALF * (h + 1))
            quantize(dic_code[G][:, cols], dic_scale[G][:, cols], dic_il[G][h][:].rearrange("p d t -> p (d t)"))

        def turn_x(R, j, k):
            b = bank("tx%d%d" % (R, j), k)
            held["tx", R, j] = b
            for c in range(2):
                words = x_sb[R][:, 2 * j + c, :].bitcast(F32)
                for u in range(2):
                    nc.tensor.transpose(b[:, P * (2 * c + u) : P * (2 * c + u + 1)], words[:, u : 256 : 2], ident[:])

        def drain_x(R, j, eng):
            copy(
                eng, out=x_t[R][:, 2 * j : 2 * j + 2, :, :].bitcast(F32),
                in_=held["tx", R, j][:].rearrange("p (c u m) -> p c m u", c=2, u=2),
            )

        def quantize_x(R, j):
            cols = slice(2 * P * j, 2 * P * (j + 1))
            quantize(
                x_code[R][:, cols], x_scale[R][:, cols], x_t[R][:, 2 * j : 2 * j + 2].rearrange("p c m t -> p (c m t)")
            )

        def encode(G, R, c, k):
            b = bank("zb%d%d%d" % (G, R, c), k)
            held["z", G, R, c] = b
            rows = slice(P * c, P * (c + 1))
            for t in range(4):
                cols = slice(512 * G + P * t, 512 * G + P * (t + 1))
                nc.tensor.matmul_mx(
                    out=b[:, P * t : P * (t + 1)],
                    lhsT=we_code[:, cols].bitcast(FP8X4),
                    lhsT_scale=we_scale[:, cols],
                    rhs=x_code[R][:, rows].bitcast(FP8X4),
                    rhs_scale=x_scale[R][:, rows],
                    start=True,
                    stop=True,
                )

        def relu(G, R, c, eng):
            sums = held["z", G, R, c][:].rearrange("p (t m) -> p m t", t=4)
            if eng is nc.scalar:
                nc.scalar.activation(out=z[G][R][:, c, :, :], in_=sums, func=ACT.Relu)
            else:
                nc.vector.tensor_scalar(out=z[G][R][:, c, :, :], in0=sums, scalar1=0.0, scalar2=None, op0=ALU.max)

        def quantize_z(G, R, j):
            cols = slice(2 * P * j, 2 * P * (j + 1))
            quantize(
                z_code[G][R][:, cols],
                z_scale[G][R][:, cols],
                z[G][R][:, 2 * j : 2 * j + 2].rearrange("p c m t -> p (c m t)"),
            )

        def decode_rows(R, t, k):
            b = bank("o%d%d" % (R, t), k)
            held["o", R, t] = b
            rows = slice(P * t, P * (t + 1))
            for G in range(2):
                nc.tensor.matmul_mx(
                    out=b[:],
                    lhsT=z_code[G][R][:, rows].bitcast(FP8X4),
                    lhsT_scale=z_scale[G][R][:, rows],
                    rhs=dic_code[G][:].bitcast(FP8X4),
                    rhs_scale=dic_scale[G][:],
                    start=(G == 0),
                    stop=(G == 1),
                )

        def drain_rows(R, t, eng):
            copy(eng, out=res[R][:, t, :], in_=held["o", R, t][:])

        def store_rows(R, t):
            nc.sync.dma_start(out=out_v[R, :, t, :], in_=res[R][:, t, :])

        def round_out(R, q, eng):
            cols = slice(P * q, P * (q + 1))
            interleave(eng, res_il[R][:, cols, :], res[R][:, :, cols])

        def quantize_out(R, q, n):
            cols = slice(P * q, P * (q + n))
            quantize(res_code[R][:, cols], res_scale[:, R, cols], res_il[R][:, cols, :].rearrange("p d t -> p (d t)"))

        def store_codes(R, q, n, eng):
            cols = slice(P * q, P * (q + n))
            eng.dma_start(
                out=out_1[R].rearrange("p d t -> p (d t)").bitcast(I32)[:, cols], in_=res_code[R][:, cols].bitcast(I32)
            )

        def store_scales(eng):
            for q in range(4):
                (eng if q % 2 else nc.scalar).dma_start(
                    out=out_2[:, 4 * q : 4 * q + 4, :].rearrange("g r d -> r g d").bitcast(I32),
                    in_=res_scale[32 * q : 32 * q + 4, :, :].bitcast(I32),
                )

        load_lam(0, 0)
        setup_zeros()
        load_logits(0)
        setup_vector()
        setup_scalar()
        setup_gpsimd()
        load_g()
        load_logits(3)
        load_logits(1)
        load_logits(2)
        load_lam(0, 1)
        load_logits(4)
        load_s()
        square_sum(1)
        load_rows(x_sb, x_v, 0)
        square_sum(0)
        row_max(0)
        load_logits(6)
        spread_g()
        load_lam(1, 1)
        row_max(3)
        exponentiate(0)
        load_lam(1, 0)
        row_max(1)
        load_we_scales()
        exponentiate(3)
        invert(0, nc.vector)
        row_max(2)
        weigh(0)
        square_sum(2)
        square_sum(3)
        invert(3, nc.vector)
        widen_s()
        row_max(4)
        exponentiate(2)
        lam_gain(0)
        weigh(3)
        load_we()
        turn_x(0, 0, 0)
        exponentiate(1)
        invert(2, nc.vector)
        row_max(5)
        turn_pg(0, 1)
        scale_lam(0, nc.gpsimd)
        load_rows(x_sb, x_v, 1)
        weigh(2)
        turn_x(0, 1, 2)
        exponentiate(5)
        load_c_scales()
        scale_lam(3, nc.gpsimd)
        turn_pg(3, 3)
        invert(1, nc.vector)
        row_max(7)
        exponentiate(4)
        scale_lam(2, nc.gpsimd)
        turn_pg(2, 4)
        load_c()
        invert(5, nc.vector)
        weigh(1)
        scale_lam(1, nc.gpsimd)
        drain_pg(0, nc.scalar)
        invert(4, nc.vector)
        drain_x(0, 1, nc.scalar)
        weigh(5)
        turn_pg(1, 5)
        drain_pg(2, nc.scalar)
        turn_x(1, 0, 6)
        quantize_x(0, 1)
        drain_pg(3, nc.scalar)
        quantize_pg(0)
        drain_x(0, 0, nc.scalar)
        row_max(6)
        turn_pg(5, 1)
        turn_x(1, 1, 2)
        drain_pg(1, nc.scalar)
        quantize_pg(3)
        quantize_x(0, 0)
        square_sum(6)
        quantize_pg(2)
        archetypes(3, 4)
        permute_we(0, nc.vector)
        square_sum(5)
        square_sum(4)
        quantize_pg(1)
        permute_we(1, nc.vector)
        archetypes(1, 3)
        square_sum(7)
        weigh(4)
        exponentiate(6)
        lam_gain(1)
        archetypes(2, 0)
        dictionary(3)
        encode(1, 0, 1, 5)
        drain_x(1, 0, nc.scalar)
        invert(6, nc.vector)
        dictionary(2)
        encode(0, 0, 0, 4)
        exponentiate(7)
        turn_pg(4, 6)
        scale_lam(7, nc.gpsimd)
        weigh(6)
        archetypes(0, 0)
        scale_lam(5, nc.gpsimd)
        relu(0, 0, 0, nc.scalar)
        invert(7, nc.vector)
        dictionary(1)
        drain_x(1, 1, nc.scalar)
        scale_lam(4, nc.gpsimd)
        turn_pg(6, 4)
        weigh(7)
        drain_pg(4, nc.scalar)
        encode(0, 0, 1, 3)
        scale_lam(6, nc.gpsimd)
        encode(1, 0, 2, 2)
        drain_pg(6, nc.scalar)
        encode(1, 0, 0, 6)
        dictionary(0)
        drain_pg(5, nc.scalar)
        turn_pg(7, 4)
        quantize_x(1, 1)
        encode(1, 0, 3, 0)
        relu(0, 0, 1, nc.scalar)
        quantize_pg(5)
        encode(0, 0, 3, 1)
        quantize_pg(6)
        drain_pg(7, nc.scalar)
        archetypes(5, 3)
        quantize_z(0, 0, 0)
        relu(1, 0, 1, nc.scalar)
        quantize_pg(4)
        archetypes(6, 4)
        quantize_x(1, 0)
        relu(1, 0, 0, nc.scalar)
        quantize_pg(7)
        archetypes(4, 5)
        interleave_dic(0, 0, nc.gpsimd)
        dictionary(5)
        relu(1, 0, 2, nc.scalar)
        archetypes(7, 6)
        dictionary(6)
        interleave_dic(0, 1, nc.scalar)
        encode(1, 1, 1, 3)
        encode(0, 0, 2, 2)
        dictionary(4)
        encode(0, 1, 2, 4)
        dictionary(7)
        encode(0, 1, 0, 5)
        relu(0, 0, 2, nc.scalar)
        quantize_dic(0, 0)
        encode(1, 1, 0, 6)
        relu(1, 0, 3, nc.scalar)
        quantize_z(1, 0, 0)
        encode(1, 1, 2, 2)
        interleave_dic(1, 1, nc.vector)
        relu(0, 0, 3, nc.scalar)
        encode(0, 1, 3, 0)
        interleave_dic(1, 0, nc.vector)
        relu(1, 1, 1, nc.scalar)
        encode(1, 1, 3, 1)
        quantize_dic(1, 1)
        relu(1, 1, 0, nc.scalar)
        encode(0, 1, 1, 3)
        quantize_dic(0, 1)
        relu(1, 1, 3, nc.scalar)
        quantize_dic(1, 0)
        quantize_z(0, 0, 1)
        relu(0, 1, 2, nc.scalar)
        decode_rows(0, 1, 6)
        quantize_z(1, 0, 1)
        relu(0, 1, 0, nc.vector)
        relu(0, 1, 1, nc.scalar)
        decode_rows(0, 2, 1)
        quantize_z(1, 1, 0)
        drain_rows(0, 1, nc.scalar)
        decode_rows(0, 0, 4)
        quantize_z(0, 1, 0)
        drain_rows(0, 2, nc.vector)
        relu(1, 1, 2, nc.scalar)
        decode_rows(0, 3, 5)
        store_rows(0, 1)
        drain_rows(0, 0, nc.vector)
        relu(0, 1, 3, nc.scalar)
        decode_rows(1, 1, 3)
        store_rows(0, 2)
        quantize_z(1, 1, 1)
        decode_rows(1, 0, 6)
        drain_rows(0, 3, nc.scalar)
        store_rows(0, 0)
        quantize_z(0, 1, 1)
        drain_rows(1, 1, nc.scalar)
        round_out(0, 1, nc.vector)
        store_rows(0, 3)
        decode_rows(1, 3, 1)
        round_out(0, 3, nc.vector)
        drain_rows(1, 0, nc.scalar)
        store_rows(1, 1)
        decode_rows(1, 2, 2)
        round_out(0, 0, nc.vector)
        drain_rows(1, 3, nc.scalar)
        round_out(0, 2, nc.vector)
        store_rows(1, 0)
        quantize_out(0, 0, 2)
        drain_rows(1, 2, nc.scalar)
        quantize_out(0, 2, 2)
        store_codes(0, 0, 2, nc.sync)
        round_out(1, 2, nc.vector)
        store_codes(0, 2, 2, nc.sync)
        round_out(1, 1, nc.scalar)
        store_rows(1, 3)
        store_rows(1, 2)
        round_out(1, 3, nc.vector)
        round_out(1, 0, nc.vector)
        quantize_out(1, 2, 2)
        quantize_out(1, 0, 2)
        store_codes(1, 2, 2, nc.scalar)
        store_codes(1, 0, 2, nc.sync)
        store_scales(nc.sync)
